import numpy as np
import ml_dtypes


def mxq(x, axis, fmt="e4m3"):
    dtype, down = {"e4m3": (ml_dtypes.float8_e4m3fn, 7), "e5m2": (ml_dtypes.float8_e5m2, 14)}[fmt]
    v = np.moveaxis(np.asarray(x, np.float32).astype(ml_dtypes.bfloat16).astype(np.float64), axis, -1)
    blocks = v.reshape(v.shape[:-1] + (-1, 32))
    amax = np.abs(blocks).max(-1, keepdims=True)
    byte = np.maximum(np.where(amax > 0, np.frexp(amax)[1] - 1 + 127, 0) - down, 1)
    scale = np.exp2(byte - 127.0)
    codes = (blocks / scale).astype(np.float32).astype(dtype).astype(np.float64)
    return np.moveaxis((codes * scale).reshape(v.shape), -1, axis)


WIDE = False


def mx_kscale(k):
    if not WIDE:
        return np.ones(k)
    levels = np.array([10, -10, 5, -5, 0])
    if k % 512:
        return np.exp2(np.random.permutation(np.resize(levels, k // 32))).repeat(32)
    a = np.empty((k // 512, 16))
    for p in range(k // 512):
        a[p, :8] = np.random.permutation(np.resize(levels, 8))
        for g in range(8):
            far = levels[np.abs(levels - a[p, g]) >= 10]
            a[p, g + 8] = far[np.random.randint(len(far))]
    return np.exp2(a.ravel()).repeat(32)


def f64(x):
    return np.asarray(x).astype(np.float64)


def striped(idx):
    return np.tile(idx.reshape(-1, 16).T, (8, 1)).astype(np.uint16)


def unstriped(offs):
    return offs[:16].T.reshape(-1).astype(np.int64)


def striped8(idx):
    return np.concatenate([x.reshape(-1, 16).T for x in idx]).astype(np.uint16)


def runs(offs, k):
    lists = np.stack([offs[16 * r : 16 * r + 16].T.reshape(-1) for r in range(8)]).astype(np.int64)
    return lists[np.arange(k) % 512 // 64]


def pack_weight(w):
    k, n = w.shape
    w = f64(np.asarray(w, np.float32).astype(ml_dtypes.bfloat16)).reshape(k // 32, 32, n)
    amax = np.abs(w).max(1)
    byte = np.clip(np.where(amax > 0, np.frexp(amax)[1] - 1 + 127 - 7, 1), 1, 254)
    scaled = (w * np.exp2(127.0 - byte)[:, None, :]).reshape(k, n).astype(np.float32)
    words = np.ascontiguousarray(scaled.reshape(k // 512, 128, 4, n).transpose(0, 1, 3, 2)).astype(ml_dtypes.float8_e4m3fn).view(np.uint8)
    return words, np.ascontiguousarray(byte.astype(np.uint8).reshape(k // 512, 16, n))


def unpack_weight(words, scales):
    g, p, n, _ = words.shape
    vals = np.ascontiguousarray(words).view(ml_dtypes.float8_e4m3fn).astype(np.float64) * np.repeat(np.exp2(scales.astype(np.float64) - 127.0), 8, axis=1)[..., None]
    return vals.transpose(0, 1, 3, 2).reshape(g * 512, n)


K, T, S, N, H = 512, 2048, 512, 512, 512


def setup_inputs():
    n = np.random.standard_normal
    s = mx_kscale(K)[:, None]
    u = mx_kscale(H)
    packed_xT = pack_weight(n((K, T)) * s)
    return {
        "x_words": packed_xT[0],
        "x_scales": packed_xT[1],
        "w1": (n((K, H)) / np.sqrt(K) / s).astype(np.float32),
        "gn": (np.random.uniform(0.5, 1.5, (H, 1)) * u[:, None]).astype(np.float32),
        "w2": (n((H, N)) / np.sqrt(H) / u[:, None]).astype(np.float32),
        "offs": striped(np.random.permutation(T)[:S]),
        "p1": striped8(np.stack([np.random.permutation(S) for _ in range(8)])),
        "p2": striped8(np.stack([np.random.permutation(S) for _ in range(8)])),
        "q1": striped8(np.stack([np.random.permutation(S) for _ in range(8)])),
        "q2": striped8(np.stack([np.random.permutation(S) for _ in range(8)])),
    }


def reference(x_words, x_scales, w1, gn, w2, offs, p1, p2, q1, q2):
    xq = unpack_weight(x_words, x_scales)[:, unstriped(offs)]
    y = mxq(f64(w1), 0, "e4m3").T @ xq
    h = y + 0.5 * (np.tanh(y[np.arange(H)[:, None], runs(p1, H)] - y) + np.tanh(y[np.arange(H)[:, None], runs(p2, H)] - y))
    z = f64(gn) * (h + 0.5 * (np.tanh(h[np.arange(H)[:, None], runs(q1, H)] - h) + np.tanh(h[np.arange(H)[:, None], runs(q2, H)] - h)))
    return mxq(f64(w2), 0, "e4m3").T @ mxq(z, 0, "e4m3")

@@ -1,0 +1,200 @@
+from contextlib import ExitStack
+
+import concourse.mybir as mybir
+from concourse.masks import make_identity
+
+K, T, S, N, H = 512, 2048, 512, 512, 512
+FLOPS = 2 * K * H * S + 2 * H * N * S
+
+F32 = mybir.dt.float32
+BF16 = mybir.dt.bfloat16
+I32 = mybir.dt.int32
+U32 = mybir.dt.uint32
+U16 = mybir.dt.uint16
+U8 = mybir.dt.uint8
+FP8X4 = mybir.dt.float8_e4m3fn_x4
+MULT = mybir.AluOpType.mult
+ADD = mybir.AluOpType.add
+TANH = mybir.ActivationFunctionType.Tanh
+COPY = mybir.ActivationFunctionType.Copy
+
+P = 128
+PACK = 4
+BANK = 512
+PIECES = [(0, 256), (256, 128), (384, 128)]
+
+
+def tile_picked_coupled_none_p_kernel(tc, x_words, x_scales, w1, gn, w2, offs, p1, p2, q1, q2, out):
+    nc = tc.nc
+    with ExitStack() as ctx:
+        keep = ctx.enter_context(tc.tile_pool(name="keep", bufs=1))
+        ring = ctx.enter_context(tc.tile_pool(name="ring", bufs=4))
+        psum_d = ctx.enter_context(tc.psum_pool(name="psum_d", bufs=4))
+        psum_s = ctx.enter_context(tc.psum_pool(name="psum_s", bufs=4))
+
+        lists = {}
+        for name in ("offs", "p1", "p2", "q1", "q2"):
+            lists[name] = keep.tile([P, S // 16], U16, name="list_" + name)
+
+        xs = keep.tile([P, T], U8, name="xs", align_bytes=64)
+        xw = keep.tile([P, T], I32, name="xw", align_bytes=64)
+        w1_raw = keep.tile([P, PACK, H], F32, name="w1_raw", align_bytes=64)
+        w2_raw = keep.tile([P, PACK, N], F32, name="w2_raw", align_bytes=64)
+        gain = keep.tile([P, PACK], F32, name="gain")
+        half_gain = keep.tile([P, PACK], F32, name="half_gain")
+        ident = keep.tile([P, P], F32, name="ident", align_bytes=64)
+
+        nc.vector.memset(xs[:].bitcast(I32), 0)
+        nc.sync.dma_start(out=w1_raw[:], in_=w1.rearrange("(p j) c -> p j c", j=PACK))
+        for q in range(4):
+            nc.sync.dma_start(out=xs[32 * q : 32 * q + 4, :].bitcast(I32), in_=x_scales[0, 4 * q : 4 * q + 4, :].bitcast(I32))
+        nc.sync.dma_start(out=lists["offs"][:], in_=offs)
+        nc.sync.dma_start(out=xw[:], in_=x_words[0].rearrange("p n t -> p (n t)").bitcast(I32))
+        nc.sync.dma_start(out=lists["p1"][:], in_=p1)
+        nc.sync.dma_start(out=lists["p2"][:], in_=p2)
+        nc.sync.dma_start(out=w2_raw[:], in_=w2.rearrange("(p j) c -> p j c", j=PACK))
+        nc.sync.dma_start(out=gain[:], in_=gn.rearrange("(p t) o -> p (t o)", t=PACK))
+        nc.sync.dma_start(out=lists["q1"][:], in_=q1)
+        nc.sync.dma_start(out=lists["q2"][:], in_=q2)
+
+        make_identity(nc, ident[:])
+        warm = keep.tile([P, 1], F32, name="warm")
+        nc.scalar.activation(out=warm[:], in_=ident[:, 0:1], func=TANH)
+
+        y_win = []
+        for t in range(PACK):
+            y_t = keep.tile([P, 2 * S], F32, name="y_%d" % t, align_bytes=64)
+            nc.gpsimd.memset(y_t[:, S:], 0.0)
+            y_win.append(y_t)
+
+        xg_s = keep.tile([P, S], U8, name="xg_s", align_bytes=64)
+        xg_w = keep.tile([P, S], U32, name="xg_w", align_bytes=64)
+        nc.vector.tensor_copy(out=xg_s[:], in_=xs[:].indirect(lists["offs"][:]))
+
+        w1_codes, w1_scales = [], []
+        w1_view = w1_raw[:].rearrange("p j (m t) -> p t m j", t=PACK)
+        for t in range(PACK):
+            grouped = keep.tile([P, P, PACK], BF16, name="w1_grouped_%d" % t, align_bytes=64)
+            if t % 2 == 0:
+                nc.vector.tensor_copy(out=grouped[:], in_=w1_view[:, t])
+            else:
+                nc.scalar.copy(out=grouped[:], in_=w1_view[:, t])
+            codes = keep.tile([P, P], U32, name="w1_codes_%d" % t, align_bytes=64)
+            scales = keep.tile([P, P], U8, name="w1_scales_%d" % t, align_bytes=64)
+            nc.vector.quantize_mx(out=codes[:].bitcast(FP8X4), scales=scales[:], in_=grouped[:].rearrange("p m j -> p (m j)"))
+            w1_codes.append(codes)
+            w1_scales.append(scales)
+
+        for c0 in (0, S // 2):
+            nc.vector.tensor_copy(out=xg_w[:, c0 : c0 + S // 2], in_=xw[:].bitcast(U32).indirect(lists["offs"][:, c0 // 16 : (c0 + S // 2) // 16]))
+
+        for t, c0, width in [(0, 0, S // 2), (0, S // 2, S // 2), (1, 0, S), (2, 0, S), (3, 0, S)]:
+            acc = psum_s.tile([P, BANK], F32, name="s")
+            nc.tensor.matmul_mx(out=acc[:, :width], lhsT=w1_codes[t][:].bitcast(FP8X4), lhsT_scale=w1_scales[t][:],
+                                rhs=xg_w[:, c0 : c0 + width].bitcast(FP8X4), rhs_scale=xg_s[:, c0 : c0 + width], start=True, stop=True)
+            nc.scalar.copy(out=y_win[t][:, c0 : c0 + width], in_=acc[:, :width])
+
+        def turn(dst, src, start, stop):
+            nc.tensor.matmul(dst, lhsT=src, rhs=ident[:], start=start, stop=stop, is_transpose=True)
+
+        def gather_negated(window, offsets, width):
+            g = ring.tile([P, BANK], F32, name="g", align_bytes=64)
+            nc.vector.tensor_scalar(out=g[:, :width], in0=window[:].indirect(offsets), scalar1=-1.0, scalar2=0.0, op0=MULT, op1=ADD)
+            return g
+
+        def pulls(sources):
+            nb = len(sources)
+            d = psum_d.tile([P, BANK], F32, name="d")
+            for b, (state, g, c0, n0) in enumerate(sources):
+                turn(d[:, b * P : (b + 1) * P], state[:, n0 : n0 + P], b == 0, False)
+            for b, (state, g, c0, n0) in enumerate(sources):
+                turn(d[:, b * P : (b + 1) * P], g[:, c0 : c0 + P], False, b == nb - 1)
+            th = ring.tile([P, BANK], F32, name="th", align_bytes=64)
+            nc.scalar.activation(out=th[:, : nb * P], in_=d[:, : nb * P], func=TANH)
+            return th
+
+        def sum_back(parts):
+            s = psum_s.tile([P, BANK], F32, name="s")
+            for i, (th, c0, o0) in enumerate(parts):
+                turn(s[:, o0 : o0 + P], th[:, c0 : c0 + P], i == 0, i == len(parts) - 1)
+            return s
+
+        w2_grouped = keep.tile([P, N, PACK], BF16, name="w2_grouped", align_bytes=64)
+        w2_codes = keep.tile([P, N], U32, name="w2_codes", align_bytes=64)
+        w2_scales = keep.tile([P, N], U8, name="w2_scales", align_bytes=64)
+        w2_view = w2_raw[:].rearrange("p j c -> p c j")
+
+        nc.scalar.activation(out=half_gain[:], in_=gain[:], func=COPY, scale=-0.5)
+        h_win = [keep.tile([P, S], F32, name="h_%d" % t, align_bytes=64) for t in range(PACK)]
+        gh = [keep.tile([P, S], F32, name="gh_%d" % t, align_bytes=64) for t in range(PACK)]
+        planes = [keep.tile([P, PACK, width], BF16, name="planes_%d" % i, align_bytes=64) for i, (n0, width) in enumerate(PIECES)]
+        out_view = out.rearrange("(b p) n -> p b n", p=P)
+
+        def first_pull(t, name):
+            g = gather_negated(y_win[t], lists[name][:], S)
+            return pulls([(y_win[t], g, b * P, b * P) for b in range(4)])
+
+        def first_sum(t, ths):
+            s = sum_back([(th, b * P, b * P) for th in ths for b in range(4)])
+            nc.vector.scalar_tensor_tensor(out=h_win[t][:], in0=s[:], scalar=-0.5, in1=y_win[t][:, :S], op0=MULT, op1=ADD)
+            nc.scalar.activation(out=gh[t][:], in_=h_win[t][:], func=COPY, scale=gain[:, t : t + 1])
+            nc.scalar.copy(out=w2_grouped[:, t * P : (t + 1) * P, :], in_=w2_view[:, t * P : (t + 1) * P, :])
+            if t == PACK - 1:
+                nc.vector.quantize_mx(out=w2_codes[:].bitcast(FP8X4), scales=w2_scales[:], in_=w2_grouped[:].rearrange("p c j -> p (c j)"))
+
+        def second_pull(i, tiles):
+            n0, width = PIECES[i]
+            sources = []
+            for t in tiles:
+                for name in ("q1", "q2"):
+                    g = gather_negated(h_win[t], lists[name][:, n0 // 16 : (n0 + width) // 16], width)
+                    sources.extend((h_win[t], g, c, n0 + c) for c in range(0, width, P))
+            return pulls(sources)
+
+        def second_sum(i, tiles, th):
+            n0, width = PIECES[i]
+            s = sum_back([(th, (2 * k + a) * width + c, k * width + c) for k in range(len(tiles)) for a in range(2) for c in range(0, width, P)])
+            for k, t in enumerate(tiles):
+                nc.vector.scalar_tensor_tensor(out=planes[i][:, t, :], in0=s[:, k * width : (k + 1) * width], scalar=half_gain[:, t : t + 1],
+                                               in1=gh[t][:, n0 : n0 + width], op0=MULT, op1=ADD)
+            if tiles[-1] == PACK - 1:
+                finish(i)
+
+        def finish(i):
+            n0, width = PIECES[i]
+            z_grouped = keep.tile([P, width, PACK], BF16, name="z_grouped_%d" % i, align_bytes=64)
+            if i == len(PIECES) - 1:
+                nc.vector.tensor_copy(out=z_grouped[:], in_=planes[i][:].rearrange("p t n -> p n t"))
+            else:
+                nc.scalar.copy(out=z_grouped[:], in_=planes[i][:].rearrange("p t n -> p n t"))
+            z_codes = keep.tile([P, width], U32, name="z_codes_%d" % i, align_bytes=64)
+            z_scales = keep.tile([P, width], U8, name="z_scales_%d" % i, align_bytes=64)
+            nc.vector.quantize_mx(out=z_codes[:].bitcast(FP8X4), scales=z_scales[:], in_=z_grouped[:].rearrange("p n t -> p (n t)"))
+            per_bank = BANK // width
+            for b0 in range(0, 4, per_bank):
+                acc = psum_s.tile([P, BANK], F32, name="s")
+                for b in range(per_bank):
+                    cols = slice((b0 + b) * P, (b0 + b + 1) * P)
+                    nc.tensor.matmul_mx(out=acc[:, b * width : (b + 1) * width], lhsT=w2_codes[:, cols].bitcast(FP8X4), lhsT_scale=w2_scales[:, cols],
+                                        rhs=z_codes[:].bitcast(FP8X4), rhs_scale=z_scales[:], start=True, stop=True)
+                res = keep.tile([P, per_bank, width], F32, name="res_%d_%d" % (i, b0), align_bytes=64)
+                nc.scalar.copy(out=res[:].rearrange("p b n -> p (b n)"), in_=acc[:])
+                nc.sync.dma_start(out=out_view[:, b0 : b0 + per_bank, n0 : n0 + width], in_=res[:])
+
+        pending = None
+        for t in range(PACK):
+            th_1 = first_pull(t, "p1")
+            if pending is not None:
+                first_sum(*pending)
+            th_2 = first_pull(t, "p2")
+            pending = (t, [th_1, th_2])
+        units = [(0, [t]) for t in range(PACK)] + [(1, [0, 1]), (1, [2, 3]), (2, [0, 1]), (2, [2]), (2, [3])]
+        waiting = None
+        for i, tiles in units:
+            th = second_pull(i, tiles)
+            if waiting is None:
+                first_sum(*pending)
+            else:
+                second_sum(*waiting)
+            waiting = (i, tiles, th)
+        second_sum(*waiting)

@@ -21,38 +21,50 @@ COPY = mybir.ActivationFunctionType.Copy
 P = 128
 PACK = 4
 BANK = 512
-PIECES = [(0, 256), (256, 128), (384, 128)]
+HOLD = {-1: 2}
+HALF = S // 2
+BLOCKS = [(0, 256), (256, 128), (384, 128)]
+SUB = mybir.AluOpType.subtract
+RING = 6
+SKEW = 2
+D_BANKS = 3
+UNITS = [("first", 0, ["p1"], 0, 512, "tensor"), ("first", 0, ["p2"], 0, 512, "tensor"), ("first", 1, ["p1"], 0, 512, "tensor"), ("first", 1, ["p2"], 0, 512, "tensor"), ("first", 2, ["p1"], 0, 512, "tensor"), ("first", 2, ["p2"], 0, 512, "tensor"), ("first", 3, ["p1"], 0, 512, "tensor"), ("first", 3, ["p2"], 0, 512, "tensor"), ("second", 0, ["q1"], 0, 512, "vector"), ("second", 0, ["q2"], 0, 512, "vector"), ("second", 1, ["q1"], 0, 512, "tensor"), ("second", 1, ["q2"], 0, 512, "tensor"), ("second", 2, ["q1", "q2"], 0, 256, "tensor"), ("second", 3, ["q1", "q2"], 0, 256, "vector"), ("second", 2, ["q1", "q2"], 256, 256, "tensor"), ("second", 3, ["q1", "q2"], 256, 256, "vector")]
+
+
+def advance(ring):
+    ring.append(ring.pop(0))
+    return ring[-1]
 
 
 def tile_picked_coupled_none_p_kernel(tc, x_words, x_scales, w1, gn, w2, offs, p1, p2, q1, q2, out):
     nc = tc.nc
     with ExitStack() as ctx:
         keep = ctx.enter_context(tc.tile_pool(name="keep", bufs=1))
-        ring = ctx.enter_context(tc.tile_pool(name="ring", bufs=4))
-        psum_d = ctx.enter_context(tc.psum_pool(name="psum_d", bufs=4))
-        psum_s = ctx.enter_context(tc.psum_pool(name="psum_s", bufs=4))
+        psum = ctx.enter_context(tc.psum_pool(name="psum", bufs=1))
 
+        banks = [psum.tile([P, BANK], F32, name="bank_%d" % b) for b in range(8)]
+        d_banks = banks[:D_BANKS]
+        s_banks = banks[D_BANKS:]
         lists = {}
         for name in ("offs", "p1", "p2", "q1", "q2"):
             lists[name] = keep.tile([P, S // 16], U16, name="list_" + name)
 
         xs = keep.tile([P, T], U8, name="xs", align_bytes=64)
         xw = keep.tile([P, T], I32, name="xw", align_bytes=64)
-        w1_raw = keep.tile([P, PACK, H], F32, name="w1_raw", align_bytes=64)
-        w2_raw = keep.tile([P, PACK, N], F32, name="w2_raw", align_bytes=64)
+        w1_raw = keep.tile([P, PACK, H], F32, name="w_raw", align_bytes=64)
+        w2_raw = w1_raw
         gain = keep.tile([P, PACK], F32, name="gain")
         half_gain = keep.tile([P, PACK], F32, name="half_gain")
         ident = keep.tile([P, P], F32, name="ident", align_bytes=64)
 
         nc.vector.memset(xs[:].bitcast(I32), 0)
-        nc.sync.dma_start(out=w1_raw[:], in_=w1.rearrange("(p j) c -> p j c", j=PACK))
+        nc.sync.dma_start(out=lists["offs"][:], in_=offs)
         for q in range(4):
             nc.sync.dma_start(out=xs[32 * q : 32 * q + 4, :].bitcast(I32), in_=x_scales[0, 4 * q : 4 * q + 4, :].bitcast(I32))
-        nc.sync.dma_start(out=lists["offs"][:], in_=offs)
+        nc.sync.dma_start(out=w1_raw[:], in_=w1.rearrange("(p j) c -> p j c", j=PACK))
         nc.sync.dma_start(out=xw[:], in_=x_words[0].rearrange("p n t -> p (n t)").bitcast(I32))
         nc.sync.dma_start(out=lists["p1"][:], in_=p1)
         nc.sync.dma_start(out=lists["p2"][:], in_=p2)
-        nc.sync.dma_start(out=w2_raw[:], in_=w2.rearrange("(p j) c -> p j c", j=PACK))
         nc.sync.dma_start(out=gain[:], in_=gn.rearrange("(p t) o -> p (t o)", t=PACK))
         nc.sync.dma_start(out=lists["q1"][:], in_=q1)
         nc.sync.dma_start(out=lists["q2"][:], in_=q2)
@@ -75,7 +87,7 @@ def tile_picked_coupled_none_p_kernel(tc, x_words, x_scales, w1, gn, w2, offs, p
         w1_view = w1_raw[:].rearrange("p j (m t) -> p t m j", t=PACK)
         for t in range(PACK):
             grouped = keep.tile([P, P, PACK], BF16, name="w1_grouped_%d" % t, align_bytes=64)
-            if t % 2 == 0:
+            if t in [0,2]:
                 nc.vector.tensor_copy(out=grouped[:], in_=w1_view[:, t])
             else:
                 nc.scalar.copy(out=grouped[:], in_=w1_view[:, t])
@@ -88,113 +100,136 @@ def tile_picked_coupled_none_p_kernel(tc, x_words, x_scales, w1, gn, w2, offs, p
         for c0 in (0, S // 2):
             nc.vector.tensor_copy(out=xg_w[:, c0 : c0 + S // 2], in_=xw[:].bitcast(U32).indirect(lists["offs"][:, c0 // 16 : (c0 + S // 2) // 16]))
 
+        plain = [keep.tile([P, S], F32, name="plain_%d" % t, align_bytes=64) for t in range(PACK)]
+        first_on_vector = [u[1] for u in UNITS if u[0] == "first" and u[5] == "vector"]
         for t, c0, width in [(0, 0, S // 2), (0, S // 2, S // 2), (1, 0, S), (2, 0, S), (3, 0, S)]:
-            acc = psum_s.tile([P, BANK], F32, name="s")
+            acc = advance(s_banks)
             nc.tensor.matmul_mx(out=acc[:, :width], lhsT=w1_codes[t][:].bitcast(FP8X4), lhsT_scale=w1_scales[t][:],
                                 rhs=xg_w[:, c0 : c0 + width].bitcast(FP8X4), rhs_scale=xg_s[:, c0 : c0 + width], start=True, stop=True)
-            nc.scalar.copy(out=y_win[t][:, c0 : c0 + width], in_=acc[:, :width])
+            if (t, c0) in [(0,256)]:
+                nc.vector.tensor_copy(out=y_win[t][:, c0 : c0 + width], in_=acc[:, :width])
+            else:
+                nc.scalar.copy(out=y_win[t][:, c0 : c0 + width], in_=acc[:, :width])
+            if t in first_on_vector:
+                nc.scalar.copy(out=plain[t][:, c0 : c0 + width], in_=acc[:, :width])
 
         def turn(dst, src, start, stop):
             nc.tensor.matmul(dst, lhsT=src, rhs=ident[:], start=start, stop=stop, is_transpose=True)
 
-        def gather_negated(window, offsets, width):
-            g = ring.tile([P, BANK], F32, name="g", align_bytes=64)
-            nc.vector.tensor_scalar(out=g[:, :width], in0=window[:].indirect(offsets), scalar1=-1.0, scalar2=0.0, op0=MULT, op1=ADD)
-            return g
-
-        def pulls(sources):
-            nb = len(sources)
-            d = psum_d.tile([P, BANK], F32, name="d")
-            for b, (state, g, c0, n0) in enumerate(sources):
-                turn(d[:, b * P : (b + 1) * P], state[:, n0 : n0 + P], b == 0, False)
-            for b, (state, g, c0, n0) in enumerate(sources):
-                turn(d[:, b * P : (b + 1) * P], g[:, c0 : c0 + P], False, b == nb - 1)
-            th = ring.tile([P, BANK], F32, name="th", align_bytes=64)
-            nc.scalar.activation(out=th[:, : nb * P], in_=d[:, : nb * P], func=TANH)
-            return th
-
-        def sum_back(parts):
-            s = psum_s.tile([P, BANK], F32, name="s")
-            for i, (th, c0, o0) in enumerate(parts):
-                turn(s[:, o0 : o0 + P], th[:, c0 : c0 + P], i == 0, i == len(parts) - 1)
-            return s
-
+        nc.sync.dma_start(out=w2_raw[:], in_=w2.rearrange("(p j) c -> p j c", j=PACK))
         w2_grouped = keep.tile([P, N, PACK], BF16, name="w2_grouped", align_bytes=64)
         w2_codes = keep.tile([P, N], U32, name="w2_codes", align_bytes=64)
         w2_scales = keep.tile([P, N], U8, name="w2_scales", align_bytes=64)
         w2_view = w2_raw[:].rearrange("p j c -> p c j")
-
-        nc.scalar.activation(out=half_gain[:], in_=gain[:], func=COPY, scale=-0.5)
-        h_win = [keep.tile([P, S], F32, name="h_%d" % t, align_bytes=64) for t in range(PACK)]
+        minus_half_gain = keep.tile([P, PACK], F32, name="minus_half_gain")
+        nc.gpsimd.tensor_scalar(out=half_gain[:], in0=gain[:], scalar1=0.5, scalar2=0.0, op0=MULT, op1=ADD)
+        nc.gpsimd.tensor_scalar(out=minus_half_gain[:], in0=gain[:], scalar1=-0.5, scalar2=0.0, op0=MULT, op1=ADD)
+        h_win = [y_win[t] if t < PACK - 1 else keep.tile([P, S], F32, name="h_last", align_bytes=64) for t in range(PACK)]
         gh = [keep.tile([P, S], F32, name="gh_%d" % t, align_bytes=64) for t in range(PACK)]
-        planes = [keep.tile([P, PACK, width], BF16, name="planes_%d" % i, align_bytes=64) for i, (n0, width) in enumerate(PIECES)]
+        planes = keep.tile([P, S // P, PACK, P], BF16, name="planes", align_bytes=64)
+        work = [keep.tile([P, BANK], F32, name="work_%d" % r, align_bytes=64) for r in range(RING)]
+        for u in range(RING, len(UNITS)):
+            work.append(work[u - HOLD.get(u - len(UNITS), RING)])
         out_view = out.rearrange("(b p) n -> p b n", p=P)
 
-        def first_pull(t, name):
-            g = gather_negated(y_win[t], lists[name][:], S)
-            return pulls([(y_win[t], g, b * P, b * P) for b in range(4)])
+        def pull(unit, buf):
+            step, t, names, n0, width, route = unit
+            window = y_win[t] if step == "first" else h_win[t]
+            for a, name in enumerate(names):
+                picked = window[:].indirect(lists[name][:, n0 // 16 : (n0 + width) // 16])
+                dst = buf[:, a * width : (a + 1) * width]
+                if route == "vector":
+                    nc.vector.tensor_tensor(out=dst, in0=picked, in1=plain[t][:, n0 : n0 + width], op=SUB)
+                    if unit in UNITS[-1:]:
+                        nc.scalar.activation(out=dst, in_=dst, func=TANH)
+                else:
+                    nc.vector.tensor_scalar(out=dst, in0=picked, scalar1=-1.0, scalar2=0.0, op0=MULT, op1=ADD)
+            if route == "vector":
+                if unit not in UNITS[-1:]:
+                    nc.scalar.activation(out=buf[:, : len(names) * width], in_=buf[:, : len(names) * width], func=TANH)
+                return
+            d = advance(d_banks)
+            for c in range(0, BANK, P):
+                n = n0 + c % width
+                turn(d[:, c : c + P], window[:, n : n + P], c == 0, False)
+            for c in range(0, BANK, P):
+                turn(d[:, c : c + P], buf[:, c : c + P], False, c == BANK - P)
+            nc.scalar.activation(out=buf[:], in_=d[:], func=TANH)
 
-        def first_sum(t, ths):
-            s = sum_back([(th, b * P, b * P) for th in ths for b in range(4)])
-            nc.vector.scalar_tensor_tensor(out=h_win[t][:], in0=s[:], scalar=-0.5, in1=y_win[t][:, :S], op0=MULT, op1=ADD)
-            nc.scalar.activation(out=gh[t][:], in_=h_win[t][:], func=COPY, scale=gain[:, t : t + 1])
-            nc.scalar.copy(out=w2_grouped[:, t * P : (t + 1) * P, :], in_=w2_view[:, t * P : (t + 1) * P, :])
-            if t == PACK - 1:
-                nc.vector.quantize_mx(out=w2_codes[:].bitcast(FP8X4), scales=w2_scales[:], in_=w2_grouped[:].rearrange("p c j -> p (c j)"))
-
-        def second_pull(i, tiles):
-            n0, width = PIECES[i]
-            sources = []
-            for t in tiles:
-                for name in ("q1", "q2"):
-                    g = gather_negated(h_win[t], lists[name][:, n0 // 16 : (n0 + width) // 16], width)
-                    sources.extend((h_win[t], g, c, n0 + c) for c in range(0, width, P))
-            return pulls(sources)
-
-        def second_sum(i, tiles, th):
-            n0, width = PIECES[i]
-            s = sum_back([(th, (2 * k + a) * width + c, k * width + c) for k in range(len(tiles)) for a in range(2) for c in range(0, width, P)])
-            for k, t in enumerate(tiles):
-                nc.vector.scalar_tensor_tensor(out=planes[i][:, t, :], in0=s[:, k * width : (k + 1) * width], scalar=half_gain[:, t : t + 1],
-                                               in1=gh[t][:, n0 : n0 + width], op0=MULT, op1=ADD)
-            if tiles[-1] == PACK - 1:
-                finish(i)
+        def close(u):
+            step, t, names, n0, width, route = UNITS[u]
+            if names[-1] not in ("p2", "q2"):
+                return
+            if len(names) == 1:
+                pulls = [work[u - 1][:], work[u][:]]
+            else:
+                pulls = [work[u][:, :width], work[u][:, width : 2 * width]]
+            if step == "first":
+                dst = h_win[t][:, :S]
+                base = plain[t][:] if route == "vector" else y_win[t][:, :S]
+                plus, minus = 0.5, -0.5
+            else:
+                base = gh[t][:, n0 : n0 + width]
+                dst = planes[:, n0 // P : (n0 + width) // P, t, :]
+                plus, minus = half_gain[:, t : t + 1], minus_half_gain[:, t : t + 1]
+            shaped = "p (a n) -> p a n"
+            cut = P if step == "second" else S
+            if step == "first":
+                dst = dst.rearrange(shaped, n=cut)
+            if route == "vector":
+                nc.vector.scalar_tensor_tensor(out=base, in0=pulls[0], scalar=plus, in1=base, op0=MULT, op1=ADD)
+                nc.vector.scalar_tensor_tensor(out=dst, in0=pulls[1].rearrange(shaped, n=cut), scalar=plus, in1=base.rearrange(shaped, n=cut), op0=MULT, op1=ADD)
+            else:
+                s = advance(s_banks)
+                for a, th in enumerate(pulls):
+                    for c in range(0, width, P):
+                        turn(s[:, c : c + P], th[:, c : c + P], a == 0 and c == 0, a == 1 and c == width - P)
+                nc.vector.scalar_tensor_tensor(out=dst, in0=s[:, :width].rearrange(shaped, n=cut), scalar=minus, in1=base.rearrange(shaped, n=cut), op0=MULT, op1=ADD)
+            if step == "first":
+                if any(v[0] == "second" and v[1] == t and v[5] == "vector" for v in UNITS):
+                    nc.scalar.copy(out=plain[t][:], in_=h_win[t][:, :S])
+                nc.scalar.activation(out=gh[t][:], in_=h_win[t][:, :S], func=COPY, scale=gain[:, t : t + 1])
+                nc.scalar.copy(out=w2_grouped[:, t * P : (t + 1) * P, :], in_=w2_view[:, t * P : (t + 1) * P, :])
+                if t == PACK - 1:
+                    nc.vector.quantize_mx(out=w2_codes[:].bitcast(FP8X4), scales=w2_scales[:], in_=w2_grouped[:].rearrange("p c j -> p (c j)"))
+            elif all(v[3] >= n0 + width for v in UNITS[u + 1 :]):
+                for i, (b0, size) in enumerate(BLOCKS):
+                    if n0 <= b0 < n0 + width:
+                        finish(i)
 
         def finish(i):
-            n0, width = PIECES[i]
+            n0, width = BLOCKS[i]
+            last = i == len(BLOCKS) - 1
             z_grouped = keep.tile([P, width, PACK], BF16, name="z_grouped_%d" % i, align_bytes=64)
-            if i == len(PIECES) - 1:
-                nc.vector.tensor_copy(out=z_grouped[:], in_=planes[i][:].rearrange("p t n -> p n t"))
+            source = planes[:, n0 // P : (n0 + width) // P].rearrange("p a t n -> p a n t")
+            target = z_grouped[:].rearrange("p (a n) t -> p a n t", n=P)
+            if i in [1]:
+                nc.vector.tensor_copy(out=target, in_=source)
             else:
-                nc.scalar.copy(out=z_grouped[:], in_=planes[i][:].rearrange("p t n -> p n t"))
+                nc.scalar.copy(out=target, in_=source)
             z_codes = keep.tile([P, width], U32, name="z_codes_%d" % i, align_bytes=64)
             z_scales = keep.tile([P, width], U8, name="z_scales_%d" % i, align_bytes=64)
             nc.vector.quantize_mx(out=z_codes[:].bitcast(FP8X4), scales=z_scales[:], in_=z_grouped[:].rearrange("p n t -> p (n t)"))
-            per_bank = BANK // width
+            per_bank = 2 if last else BANK // width
             for b0 in range(0, 4, per_bank):
-                acc = psum_s.tile([P, BANK], F32, name="s")
+                acc = advance(s_banks)
                 for b in range(per_bank):
                     cols = slice((b0 + b) * P, (b0 + b + 1) * P)
                     nc.tensor.matmul_mx(out=acc[:, b * width : (b + 1) * width], lhsT=w2_codes[:, cols].bitcast(FP8X4), lhsT_scale=w2_scales[:, cols],
                                         rhs=z_codes[:].bitcast(FP8X4), rhs_scale=z_scales[:], start=True, stop=True)
                 res = keep.tile([P, per_bank, width], F32, name="res_%d_%d" % (i, b0), align_bytes=64)
-                nc.scalar.copy(out=res[:].rearrange("p b n -> p (b n)"), in_=acc[:])
-                nc.sync.dma_start(out=out_view[:, b0 : b0 + per_bank, n0 : n0 + width], in_=res[:])
+                if (i, b0) in [(1, 0), (2, 2)]:
+                    nc.vector.tensor_copy(out=res[:].rearrange("p b n -> p (b n)"), in_=acc[:, : per_bank * width])
+                else:
+                    nc.scalar.copy(out=res[:].rearrange("p b n -> p (b n)"), in_=acc[:, : per_bank * width])
+                (nc.scalar if (i, b0) in [(2, 0)] else nc.sync).dma_start(out=out_view[:, b0 : b0 + per_bank, n0 : n0 + width], in_=res[:])
 
-        pending = None
-        for t in range(PACK):
-            th_1 = first_pull(t, "p1")
-            if pending is not None:
-                first_sum(*pending)
-            th_2 = first_pull(t, "p2")
-            pending = (t, [th_1, th_2])
-        units = [(0, [t]) for t in range(PACK)] + [(1, [0, 1]), (1, [2, 3]), (2, [0, 1]), (2, [2]), (2, [3])]
-        waiting = None
-        for i, tiles in units:
-            th = second_pull(i, tiles)
-            if waiting is None:
-                first_sum(*pending)
-            else:
-                second_sum(*waiting)
-            waiting = (i, tiles, th)
-        second_sum(*waiting)
+        closed = 0
+        for u, unit in enumerate(UNITS):
+            lag = HOLD.get(u - len(UNITS), SKEW + 1)
+            while closed <= u - lag:
+                close(closed)
+                closed = closed + 1
+            pull(unit, work[u])
+        for u in range(closed, len(UNITS)):
+            close(u)

@@ -15,20 +15,29 @@ U8 = mybir.dt.uint8
 FP8X4 = mybir.dt.float8_e4m3fn_x4
 MULT = mybir.AluOpType.mult
 ADD = mybir.AluOpType.add
+SUBTRACT = mybir.AluOpType.subtract
 TANH = mybir.ActivationFunctionType.Tanh
 COPY = mybir.ActivationFunctionType.Copy
 
 P = 128
 PACK = 4
 BANK = 512
-HOLD = {-1: 2}
 HALF = S // 2
-BLOCKS = [(0, 256), (256, 128), (384, 128)]
-SUB = mybir.AluOpType.subtract
-RING = 6
-SKEW = 2
-D_BANKS = 3
-UNITS = [("first", 0, ["p1"], 0, 512, "tensor"), ("first", 0, ["p2"], 0, 512, "tensor"), ("first", 1, ["p1"], 0, 512, "tensor"), ("first", 1, ["p2"], 0, 512, "tensor"), ("first", 2, ["p1"], 0, 512, "tensor"), ("first", 2, ["p2"], 0, 512, "tensor"), ("first", 3, ["p1"], 0, 512, "tensor"), ("first", 3, ["p2"], 0, 512, "tensor"), ("second", 0, ["q1"], 0, 512, "vector"), ("second", 0, ["q2"], 0, 512, "vector"), ("second", 1, ["q1"], 0, 512, "tensor"), ("second", 1, ["q2"], 0, 512, "tensor"), ("second", 2, ["q1", "q2"], 0, 256, "tensor"), ("second", 3, ["q1", "q2"], 0, 256, "vector"), ("second", 2, ["q1", "q2"], 256, 256, "tensor"), ("second", 3, ["q1", "q2"], 256, 256, "vector")]
+
+VECTOR_PLANE = PACK - 2
+LAST_PLANE = PACK - 1
+
+UNITS = (
+    [("first", t, [name], 0, S, "tensor") for t in range(PACK) for name in ("p1", "p2")]
+    + [("second", t, [name], 0, S, "tensor") for t in range(VECTOR_PLANE) for name in ("q1", "q2")]
+    + [("second", t, ["q1", "q2"], n0, HALF, way) for n0 in (0, HALF) for t, way in ((LAST_PLANE, "tensor"), (VECTOR_PLANE, "vector"))]
+)
+WORK_TILES = 6
+LAG = 3
+LAST_LAG = 2
+DIFFERENCE_BANKS = 3
+
+BLOCKS = [(0, HALF), (HALF, P), (HALF + P, P)]
 
 
 def advance(ring):
@@ -43,26 +52,23 @@ def tile_picked_coupled_none_p_kernel(tc, x_words, x_scales, w1, gn, w2, offs, p
         psum = ctx.enter_context(tc.psum_pool(name="psum", bufs=1))
 
         banks = [psum.tile([P, BANK], F32, name="bank_%d" % b) for b in range(8)]
-        d_banks = banks[:D_BANKS]
-        s_banks = banks[D_BANKS:]
-        lists = {}
-        for name in ("offs", "p1", "p2", "q1", "q2"):
-            lists[name] = keep.tile([P, S // 16], U16, name="list_" + name)
+        difference_banks = banks[:DIFFERENCE_BANKS]
+        sum_banks = banks[DIFFERENCE_BANKS:]
+        lists = {name: keep.tile([P, S // 16], U16, name="list_" + name) for name in ("offs", "p1", "p2", "q1", "q2")}
 
-        xs = keep.tile([P, T], U8, name="xs", align_bytes=64)
-        xw = keep.tile([P, T], I32, name="xw", align_bytes=64)
-        w1_raw = keep.tile([P, PACK, H], F32, name="w_raw", align_bytes=64)
-        w2_raw = w1_raw
+        x_bytes = keep.tile([P, T], U8, name="x_bytes", align_bytes=64)
+        x_packed = keep.tile([P, T], I32, name="x_packed", align_bytes=64)
+        w_raw = keep.tile([P, PACK, H], F32, name="w_raw", align_bytes=64)
         gain = keep.tile([P, PACK], F32, name="gain")
         half_gain = keep.tile([P, PACK], F32, name="half_gain")
         ident = keep.tile([P, P], F32, name="ident", align_bytes=64)
 
-        nc.vector.memset(xs[:].bitcast(I32), 0)
+        nc.vector.memset(x_bytes[:].bitcast(I32), 0)
         nc.sync.dma_start(out=lists["offs"][:], in_=offs)
         for q in range(4):
-            nc.sync.dma_start(out=xs[32 * q : 32 * q + 4, :].bitcast(I32), in_=x_scales[0, 4 * q : 4 * q + 4, :].bitcast(I32))
-        nc.sync.dma_start(out=w1_raw[:], in_=w1.rearrange("(p j) c -> p j c", j=PACK))
-        nc.sync.dma_start(out=xw[:], in_=x_words[0].rearrange("p n t -> p (n t)").bitcast(I32))
+            nc.sync.dma_start(out=x_bytes[32 * q : 32 * q + 4, :].bitcast(I32), in_=x_scales[0, 4 * q : 4 * q + 4, :].bitcast(I32))
+        nc.sync.dma_start(out=w_raw[:], in_=w1.rearrange("(p j) c -> p j c", j=PACK))
+        nc.sync.dma_start(out=x_packed[:], in_=x_words[0].rearrange("p n t -> p (n t)").bitcast(I32))
         nc.sync.dma_start(out=lists["p1"][:], in_=p1)
         nc.sync.dma_start(out=lists["p2"][:], in_=p2)
         nc.sync.dma_start(out=gain[:], in_=gn.rearrange("(p t) o -> p (t o)", t=PACK))
@@ -70,24 +76,22 @@ def tile_picked_coupled_none_p_kernel(tc, x_words, x_scales, w1, gn, w2, offs, p
         nc.sync.dma_start(out=lists["q2"][:], in_=q2)
 
         make_identity(nc, ident[:])
-        warm = keep.tile([P, 1], F32, name="warm")
-        nc.scalar.activation(out=warm[:], in_=ident[:, 0:1], func=TANH)
 
-        y_win = []
+        state = []
         for t in range(PACK):
-            y_t = keep.tile([P, 2 * S], F32, name="y_%d" % t, align_bytes=64)
-            nc.gpsimd.memset(y_t[:, S:], 0.0)
-            y_win.append(y_t)
+            window = keep.tile([P, 2 * S], F32, name="state_%d" % t, align_bytes=64)
+            nc.gpsimd.memset(window[:, S:], 0.0)
+            state.append(window)
 
-        xg_s = keep.tile([P, S], U8, name="xg_s", align_bytes=64)
-        xg_w = keep.tile([P, S], U32, name="xg_w", align_bytes=64)
-        nc.vector.tensor_copy(out=xg_s[:], in_=xs[:].indirect(lists["offs"][:]))
+        picked_bytes = keep.tile([P, S], U8, name="picked_bytes", align_bytes=64)
+        picked_words = keep.tile([P, S], U32, name="picked_words", align_bytes=64)
+        nc.vector.tensor_copy(out=picked_bytes[:], in_=x_bytes[:].indirect(lists["offs"][:]))
 
         w1_codes, w1_scales = [], []
-        w1_view = w1_raw[:].rearrange("p j (m t) -> p t m j", t=PACK)
+        w1_view = w_raw[:].rearrange("p j (m t) -> p t m j", t=PACK)
         for t in range(PACK):
             grouped = keep.tile([P, P, PACK], BF16, name="w1_grouped_%d" % t, align_bytes=64)
-            if t in [0,2]:
+            if t % 2 == 0:
                 nc.vector.tensor_copy(out=grouped[:], in_=w1_view[:, t])
             else:
                 nc.scalar.copy(out=grouped[:], in_=w1_view[:, t])
@@ -97,139 +101,128 @@ def tile_picked_coupled_none_p_kernel(tc, x_words, x_scales, w1, gn, w2, offs, p
             w1_codes.append(codes)
             w1_scales.append(scales)
 
-        for c0 in (0, S // 2):
-            nc.vector.tensor_copy(out=xg_w[:, c0 : c0 + S // 2], in_=xw[:].bitcast(U32).indirect(lists["offs"][:, c0 // 16 : (c0 + S // 2) // 16]))
-
-        plain = [keep.tile([P, S], F32, name="plain_%d" % t, align_bytes=64) for t in range(PACK)]
-        first_on_vector = [u[1] for u in UNITS if u[0] == "first" and u[5] == "vector"]
-        for t, c0, width in [(0, 0, S // 2), (0, S // 2, S // 2), (1, 0, S), (2, 0, S), (3, 0, S)]:
-            acc = advance(s_banks)
+        for n0 in (0, HALF):
+            nc.vector.tensor_copy(out=picked_words[:, n0 : n0 + HALF],
+                                  in_=x_packed[:].bitcast(U32).indirect(lists["offs"][:, n0 // 16 : (n0 + HALF) // 16]))
+        for t, n0, width in [(0, 0, HALF), (0, HALF, HALF)] + [(t, 0, S) for t in range(1, PACK)]:
+            acc = advance(sum_banks)
             nc.tensor.matmul_mx(out=acc[:, :width], lhsT=w1_codes[t][:].bitcast(FP8X4), lhsT_scale=w1_scales[t][:],
-                                rhs=xg_w[:, c0 : c0 + width].bitcast(FP8X4), rhs_scale=xg_s[:, c0 : c0 + width], start=True, stop=True)
-            if (t, c0) in [(0,256)]:
-                nc.vector.tensor_copy(out=y_win[t][:, c0 : c0 + width], in_=acc[:, :width])
+                                rhs=picked_words[:, n0 : n0 + width].bitcast(FP8X4), rhs_scale=picked_bytes[:, n0 : n0 + width],
+                                start=True, stop=True)
+            if n0 > 0:
+                nc.vector.tensor_copy(out=state[t][:, n0 : n0 + width], in_=acc[:, :width])
             else:
-                nc.scalar.copy(out=y_win[t][:, c0 : c0 + width], in_=acc[:, :width])
-            if t in first_on_vector:
-                nc.scalar.copy(out=plain[t][:, c0 : c0 + width], in_=acc[:, :width])
+                nc.scalar.copy(out=state[t][:, n0 : n0 + width], in_=acc[:, :width])
 
         def turn(dst, src, start, stop):
             nc.tensor.matmul(dst, lhsT=src, rhs=ident[:], start=start, stop=stop, is_transpose=True)
 
-        nc.sync.dma_start(out=w2_raw[:], in_=w2.rearrange("(p j) c -> p j c", j=PACK))
+        nc.sync.dma_start(out=w_raw[:], in_=w2.rearrange("(p j) c -> p j c", j=PACK))
         w2_grouped = keep.tile([P, N, PACK], BF16, name="w2_grouped", align_bytes=64)
         w2_codes = keep.tile([P, N], U32, name="w2_codes", align_bytes=64)
         w2_scales = keep.tile([P, N], U8, name="w2_scales", align_bytes=64)
-        w2_view = w2_raw[:].rearrange("p j c -> p c j")
+        w2_view = w_raw[:].rearrange("p j c -> p c j")
         minus_half_gain = keep.tile([P, PACK], F32, name="minus_half_gain")
         nc.gpsimd.tensor_scalar(out=half_gain[:], in0=gain[:], scalar1=0.5, scalar2=0.0, op0=MULT, op1=ADD)
         nc.gpsimd.tensor_scalar(out=minus_half_gain[:], in0=gain[:], scalar1=-0.5, scalar2=0.0, op0=MULT, op1=ADD)
-        h_win = [y_win[t] if t < PACK - 1 else keep.tile([P, S], F32, name="h_last", align_bytes=64) for t in range(PACK)]
-        gh = [keep.tile([P, S], F32, name="gh_%d" % t, align_bytes=64) for t in range(PACK)]
-        planes = keep.tile([P, S // P, PACK, P], BF16, name="planes", align_bytes=64)
-        work = [keep.tile([P, BANK], F32, name="work_%d" % r, align_bytes=64) for r in range(RING)]
-        for u in range(RING, len(UNITS)):
-            work.append(work[u - HOLD.get(u - len(UNITS), RING)])
+        plain_h = keep.tile([P, S], F32, name="plain_h", align_bytes=64)
+        gained_h = [keep.tile([P, S], F32, name="gained_h_%d" % t, align_bytes=64) for t in range(PACK)]
+        z_planes = keep.tile([P, S // P, PACK, P], BF16, name="z_planes", align_bytes=64)
+        work = [keep.tile([P, BANK], F32, name="work_%d" % r, align_bytes=64) for r in range(WORK_TILES)]
+        for u in range(WORK_TILES, len(UNITS) - 1):
+            work.append(work[u - WORK_TILES])
+        work.append(work[len(UNITS) - 1 - LAST_LAG])
         out_view = out.rearrange("(b p) n -> p b n", p=P)
 
-        def pull(unit, buf):
-            step, t, names, n0, width, route = unit
-            window = y_win[t] if step == "first" else h_win[t]
+        def pull(u):
+            step, t, names, n0, width, way = UNITS[u]
             for a, name in enumerate(names):
-                picked = window[:].indirect(lists[name][:, n0 // 16 : (n0 + width) // 16])
-                dst = buf[:, a * width : (a + 1) * width]
-                if route == "vector":
-                    nc.vector.tensor_tensor(out=dst, in0=picked, in1=plain[t][:, n0 : n0 + width], op=SUB)
-                    if unit in UNITS[-1:]:
-                        nc.scalar.activation(out=dst, in_=dst, func=TANH)
-                else:
+                picked = state[t][:].indirect(lists[name][:, n0 // 16 : (n0 + width) // 16])
+                dst = work[u][:, a * width : (a + 1) * width]
+                if way == "tensor":
                     nc.vector.tensor_scalar(out=dst, in0=picked, scalar1=-1.0, scalar2=0.0, op0=MULT, op1=ADD)
-            if route == "vector":
-                if unit not in UNITS[-1:]:
-                    nc.scalar.activation(out=buf[:, : len(names) * width], in_=buf[:, : len(names) * width], func=TANH)
-                return
-            d = advance(d_banks)
-            for c in range(0, BANK, P):
-                n = n0 + c % width
-                turn(d[:, c : c + P], window[:, n : n + P], c == 0, False)
-            for c in range(0, BANK, P):
-                turn(d[:, c : c + P], buf[:, c : c + P], False, c == BANK - P)
-            nc.scalar.activation(out=buf[:], in_=d[:], func=TANH)
+                else:
+                    nc.vector.tensor_tensor(out=dst, in0=picked, in1=plain_h[:, n0 : n0 + width], op=SUBTRACT)
+                    if u == len(UNITS) - 1:
+                        nc.scalar.activation(out=dst, in_=dst, func=TANH)
+            if way == "tensor":
+                difference = advance(difference_banks)
+                for c in range(0, BANK, P):
+                    n = n0 + c % width
+                    turn(difference[:, c : c + P], state[t][:, n : n + P], c == 0, False)
+                for c in range(0, BANK, P):
+                    turn(difference[:, c : c + P], work[u][:, c : c + P], False, c == BANK - P)
+                nc.scalar.activation(out=work[u][:], in_=difference[:], func=TANH)
+            elif u < len(UNITS) - 1:
+                nc.scalar.activation(out=work[u][:], in_=work[u][:], func=TANH)
 
         def close(u):
-            step, t, names, n0, width, route = UNITS[u]
+            step, t, names, n0, width, way = UNITS[u]
             if names[-1] not in ("p2", "q2"):
                 return
-            if len(names) == 1:
-                pulls = [work[u - 1][:], work[u][:]]
-            else:
-                pulls = [work[u][:, :width], work[u][:, width : 2 * width]]
-            if step == "first":
-                dst = h_win[t][:, :S]
-                base = plain[t][:] if route == "vector" else y_win[t][:, :S]
-                plus, minus = 0.5, -0.5
-            else:
-                base = gh[t][:, n0 : n0 + width]
-                dst = planes[:, n0 // P : (n0 + width) // P, t, :]
-                plus, minus = half_gain[:, t : t + 1], minus_half_gain[:, t : t + 1]
-            shaped = "p (a n) -> p a n"
-            cut = P if step == "second" else S
-            if step == "first":
-                dst = dst.rearrange(shaped, n=cut)
-            if route == "vector":
-                nc.vector.scalar_tensor_tensor(out=base, in0=pulls[0], scalar=plus, in1=base, op0=MULT, op1=ADD)
-                nc.vector.scalar_tensor_tensor(out=dst, in0=pulls[1].rearrange(shaped, n=cut), scalar=plus, in1=base.rearrange(shaped, n=cut), op0=MULT, op1=ADD)
-            else:
-                s = advance(s_banks)
-                for a, th in enumerate(pulls):
+            terms = [work[u - 1][:], work[u][:]] if len(names) == 1 else [work[u][:, :width], work[u][:, width:]]
+            if way == "tensor":
+                total = advance(sum_banks)
+                for a, term in enumerate(terms):
                     for c in range(0, width, P):
-                        turn(s[:, c : c + P], th[:, c : c + P], a == 0 and c == 0, a == 1 and c == width - P)
-                nc.vector.scalar_tensor_tensor(out=dst, in0=s[:, :width].rearrange(shaped, n=cut), scalar=minus, in1=base.rearrange(shaped, n=cut), op0=MULT, op1=ADD)
+                        turn(total[:, c : c + P], term[:, c : c + P], a == 0 and c == 0, a == 1 and c == width - P)
             if step == "first":
-                if any(v[0] == "second" and v[1] == t and v[5] == "vector" for v in UNITS):
-                    nc.scalar.copy(out=plain[t][:], in_=h_win[t][:, :S])
-                nc.scalar.activation(out=gh[t][:], in_=h_win[t][:, :S], func=COPY, scale=gain[:, t : t + 1])
+                h = state[t][:, :S]
+                nc.vector.scalar_tensor_tensor(out=h, in0=total[:], scalar=-0.5, in1=h, op0=MULT, op1=ADD)
+                if t == VECTOR_PLANE:
+                    nc.scalar.copy(out=plain_h[:], in_=h)
+                nc.scalar.activation(out=gained_h[t][:], in_=h, func=COPY, scale=gain[:, t : t + 1])
                 nc.scalar.copy(out=w2_grouped[:, t * P : (t + 1) * P, :], in_=w2_view[:, t * P : (t + 1) * P, :])
-                if t == PACK - 1:
+                if t == LAST_PLANE:
                     nc.vector.quantize_mx(out=w2_codes[:].bitcast(FP8X4), scales=w2_scales[:], in_=w2_grouped[:].rearrange("p c j -> p (c j)"))
-            elif all(v[3] >= n0 + width for v in UNITS[u + 1 :]):
-                for i, (b0, size) in enumerate(BLOCKS):
-                    if n0 <= b0 < n0 + width:
+                return
+            base = gained_h[t][:, n0 : n0 + width]
+            if way == "tensor":
+                last_term, factor = total[:, :width], minus_half_gain[:, t : t + 1]
+            else:
+                last_term, factor = terms[1], half_gain[:, t : t + 1]
+                nc.vector.scalar_tensor_tensor(out=base, in0=terms[0], scalar=factor, in1=base, op0=MULT, op1=ADD)
+            nc.vector.scalar_tensor_tensor(out=z_planes[:, n0 // P : (n0 + width) // P, t, :], in0=last_term.rearrange("p (a n) -> p a n", n=P),
+                                           scalar=factor, in1=base.rearrange("p (a n) -> p a n", n=P), op0=MULT, op1=ADD)
+            if t == VECTOR_PLANE:
+                for i, (first, nodes) in enumerate(BLOCKS):
+                    if n0 <= first < n0 + width:
                         finish(i)
 
         def finish(i):
             n0, width = BLOCKS[i]
-            last = i == len(BLOCKS) - 1
             z_grouped = keep.tile([P, width, PACK], BF16, name="z_grouped_%d" % i, align_bytes=64)
-            source = planes[:, n0 // P : (n0 + width) // P].rearrange("p a t n -> p a n t")
+            source = z_planes[:, n0 // P : (n0 + width) // P].rearrange("p a t n -> p a n t")
             target = z_grouped[:].rearrange("p (a n) t -> p a n t", n=P)
-            if i in [1]:
+            if i == 1:
                 nc.vector.tensor_copy(out=target, in_=source)
             else:
                 nc.scalar.copy(out=target, in_=source)
             z_codes = keep.tile([P, width], U32, name="z_codes_%d" % i, align_bytes=64)
             z_scales = keep.tile([P, width], U8, name="z_scales_%d" % i, align_bytes=64)
             nc.vector.quantize_mx(out=z_codes[:].bitcast(FP8X4), scales=z_scales[:], in_=z_grouped[:].rearrange("p n t -> p (n t)"))
+            last = i == len(BLOCKS) - 1
             per_bank = 2 if last else BANK // width
-            for b0 in range(0, 4, per_bank):
-                acc = advance(s_banks)
+            for b0 in range(0, N // P, per_bank):
+                acc = advance(difference_banks if i > 0 else sum_banks)
                 for b in range(per_bank):
-                    cols = slice((b0 + b) * P, (b0 + b + 1) * P)
-                    nc.tensor.matmul_mx(out=acc[:, b * width : (b + 1) * width], lhsT=w2_codes[:, cols].bitcast(FP8X4), lhsT_scale=w2_scales[:, cols],
+                    rows = slice((b0 + b) * P, (b0 + b + 1) * P)
+                    nc.tensor.matmul_mx(out=acc[:, b * width : (b + 1) * width], lhsT=w2_codes[:, rows].bitcast(FP8X4), lhsT_scale=w2_scales[:, rows],
                                         rhs=z_codes[:].bitcast(FP8X4), rhs_scale=z_scales[:], start=True, stop=True)
-                res = keep.tile([P, per_bank, width], F32, name="res_%d_%d" % (i, b0), align_bytes=64)
-                if (i, b0) in [(1, 0), (2, 2)]:
-                    nc.vector.tensor_copy(out=res[:].rearrange("p b n -> p (b n)"), in_=acc[:, : per_bank * width])
+                result = keep.tile([P, per_bank, width], F32, name="result_%d_%d" % (i, b0), align_bytes=64)
+                if i == 1 or (last and b0 > 0):
+                    nc.vector.tensor_copy(out=result[:].rearrange("p b n -> p (b n)"), in_=acc[:, : per_bank * width])
                 else:
-                    nc.scalar.copy(out=res[:].rearrange("p b n -> p (b n)"), in_=acc[:, : per_bank * width])
-                (nc.scalar if (i, b0) in [(2, 0)] else nc.sync).dma_start(out=out_view[:, b0 : b0 + per_bank, n0 : n0 + width], in_=res[:])
+                    nc.scalar.copy(out=result[:].rearrange("p b n -> p (b n)"), in_=acc[:, : per_bank * width])
+                queue = nc.scalar if last and b0 == 0 else nc.sync
+                queue.dma_start(out=out_view[:, b0 : b0 + per_bank, n0 : n0 + width], in_=result[:])
 
         closed = 0
-        for u, unit in enumerate(UNITS):
-            lag = HOLD.get(u - len(UNITS), SKEW + 1)
+        for u in range(len(UNITS)):
+            lag = LAST_LAG if u == len(UNITS) - 1 else LAG
             while closed <= u - lag:
                 close(closed)
                 closed = closed + 1
-            pull(unit, work[u])
+            pull(u)
         for u in range(closed, len(UNITS)):
             close(u)

@@ -192,8 +192,8 @@ def tile_picked_coupled_none_p_kernel(tc, x_words, x_scales, w1, gn, w2, offs, p
         def finish(i):
             n0, width = BLOCKS[i]
             z_grouped = keep.tile([P, width, PACK], BF16, name="z_grouped_%d" % i, align_bytes=64)
-            source = z_planes[:, n0 // P : (n0 + width) // P].rearrange("p a t n -> p a n t")
-            target = z_grouped[:].rearrange("p (a n) t -> p a n t", n=P)
+            source = z_planes[:, n0 // P : (n0 + width) // P].rearrange("p a t (c i) -> p a c t i", i=PACK)
+            target = z_grouped[:].rearrange("p (a c i) t -> p a c t i", c=P // PACK, i=PACK)
             if i == 1:
                 nc.vector.tensor_copy(out=target, in_=source)
             else:

@@ -64,10 +64,10 @@ def tile_picked_coupled_none_p_kernel(tc, x_words, x_scales, w1, gn, w2, offs, p
         ident = keep.tile([P, P], F32, name="ident", align_bytes=64)
 
         nc.vector.memset(x_bytes[:].bitcast(I32), 0)
+        nc.sync.dma_start(out=w_raw[:], in_=w1.rearrange("(p j) c -> p j c", j=PACK))
         nc.sync.dma_start(out=lists["offs"][:], in_=offs)
         for q in range(4):
             nc.sync.dma_start(out=x_bytes[32 * q : 32 * q + 4, :].bitcast(I32), in_=x_scales[0, 4 * q : 4 * q + 4, :].bitcast(I32))
-        nc.sync.dma_start(out=w_raw[:], in_=w1.rearrange("(p j) c -> p j c", j=PACK))
         nc.sync.dma_start(out=x_packed[:], in_=x_words[0].rearrange("p n t -> p (n t)").bitcast(I32))
         nc.sync.dma_start(out=lists["p1"][:], in_=p1)
         nc.sync.dma_start(out=lists["p2"][:], in_=p2)
@@ -87,24 +87,26 @@ def tile_picked_coupled_none_p_kernel(tc, x_words, x_scales, w1, gn, w2, offs, p
         picked_words = keep.tile([P, S], U32, name="picked_words", align_bytes=64)
         nc.vector.tensor_copy(out=picked_bytes[:], in_=x_bytes[:].indirect(lists["offs"][:]))
 
-        w1_codes, w1_scales = [], []
         w1_view = w_raw[:].rearrange("p j (m t) -> p t m j", t=PACK)
-        for t in range(PACK):
-            grouped = keep.tile([P, P, PACK], BF16, name="w1_grouped_%d" % t, align_bytes=64)
-            if t % 2 == 0:
-                nc.vector.tensor_copy(out=grouped[:], in_=w1_view[:, t])
-            else:
-                nc.scalar.copy(out=grouped[:], in_=w1_view[:, t])
-            codes = keep.tile([P, P], U32, name="w1_codes_%d" % t, align_bytes=64)
-            scales = keep.tile([P, P], U8, name="w1_scales_%d" % t, align_bytes=64)
-            nc.vector.quantize_mx(out=codes[:].bitcast(FP8X4), scales=scales[:], in_=grouped[:].rearrange("p m j -> p (m j)"))
-            w1_codes.append(codes)
-            w1_scales.append(scales)
+        w1_grouped = [keep.tile([P, P, PACK], BF16, name="w1_grouped_%d" % t, align_bytes=64) for t in range(PACK)]
+        nc.vector.tensor_copy(out=w1_grouped[0][:], in_=w1_view[:, 0])
+        for t in range(1, PACK):
+            nc.scalar.copy(out=w1_grouped[t][:], in_=w1_view[:, t])
+        w1_codes = [keep.tile([P, P], U32, name="w1_codes_%d" % t, align_bytes=64) for t in range(2)] * 2
+        w1_scales = [keep.tile([P, P], U8, name="w1_scales_%d" % t, align_bytes=64) for t in range(2)] * 2
+
+        def quantize_w1(t):
+            nc.vector.quantize_mx(out=w1_codes[t][:].bitcast(FP8X4), scales=w1_scales[t][:], in_=w1_grouped[t][:].rearrange("p m j -> p (m j)"))
+
+        for t in range(2):
+            quantize_w1(t)
 
         for n0 in (0, HALF):
             nc.vector.tensor_copy(out=picked_words[:, n0 : n0 + HALF],
                                   in_=x_packed[:].bitcast(U32).indirect(lists["offs"][:, n0 // 16 : (n0 + HALF) // 16]))
         for t, n0, width in [(0, 0, HALF), (0, HALF, HALF)] + [(t, 0, S) for t in range(1, PACK)]:
+            if t >= 2:
+                quantize_w1(t)
             acc = advance(sum_banks)
             nc.tensor.matmul_mx(out=acc[:, :width], lhsT=w1_codes[t][:].bitcast(FP8X4), lhsT_scale=w1_scales[t][:],
                                 rhs=picked_words[:, n0 : n0 + width].bitcast(FP8X4), rhs_scale=picked_bytes[:, n0 : n0 + width],

@@ -24,18 +24,25 @@ PACK = 4
 BANK = 512
 HALF = S // 2
 
-VECTOR_PLANE = PACK - 2
-LAST_PLANE = PACK - 1
-
-UNITS = (
-    [("first", t, [name], 0, S, "tensor") for t in range(PACK) for name in ("p1", "p2")]
-    + [("second", t, [name], 0, S, "tensor") for t in range(VECTOR_PLANE) for name in ("q1", "q2")]
-    + [("second", t, ["q1", "q2"], n0, HALF, way) for n0 in (0, HALF) for t, way in ((LAST_PLANE, "tensor"), (VECTOR_PLANE, "vector"))]
-)
-WORK_TILES = 6
-LAG = 3
-LAST_LAG = 2
+FIRST_WAYS = ["gg", "gg", "gg", "tt"]
+FIRST_FINAL = "ppvv"
+SECOND = [[(0,0,HALF,"gg")],[(0,HALF,HALF,"gg")],[(1,0,HALF,"gg")],[(2,0,HALF,"gg")],[(3,0,HALF,"tt")],[(1,HALF,HALF,"gg")],[(2,HALF,P,"tt"),(3,HALF,P,"tt")],[(2,HALF+P,P,"tt"),(3,HALF+P,P,"vv")]]
+UNITS = [[(0, t, a, 0, S, FIRST_WAYS[t][a])] for t in range(PACK) for a in range(2)] + [
+    [(1, t, a, n0, width, ways[a]) for t, n0, width, ways in unit for a in range(2)] for unit in SECOND
+]
+LISTS = [("p1", "p2"), ("q1", "q2")]
+GATHER_TILES = 2
+LAGS = [4]*8+[3]*8
 DIFFERENCE_BANKS = 3
+LATE_PRODUCT = 0
+W2_AT = 0
+WEAVE = "vsv"
+EMPTY = ["ss", "v", "sv"]
+GAIN_ON = "ssss"
+SPLIT_LAST = 0
+VWAIT = 1
+PRODUCT_AT = [-1, -1, -1, -1]
+OUT_RING = "sddd"
 
 BLOCKS = [(0, HALF), (HALF, P), (HALF + P, P)]
 
@@ -104,7 +111,8 @@ def tile_picked_coupled_none_p_kernel(tc, x_words, x_scales, w1, gn, w2, offs, p
         for n0 in (0, HALF):
             nc.vector.tensor_copy(out=picked_words[:, n0 : n0 + HALF],
                                   in_=x_packed[:].bitcast(U32).indirect(lists["offs"][:, n0 // 16 : (n0 + HALF) // 16]))
-        for t, n0, width in [(0, 0, HALF), (0, HALF, HALF)] + [(t, 0, S) for t in range(1, PACK)]:
+
+        def first_product(t, n0, width):
             if t >= 2:
                 quantize_w1(t)
             acc = advance(sum_banks)
@@ -112,9 +120,12 @@ def tile_picked_coupled_none_p_kernel(tc, x_words, x_scales, w1, gn, w2, offs, p
                                 rhs=picked_words[:, n0 : n0 + width].bitcast(FP8X4), rhs_scale=picked_bytes[:, n0 : n0 + width],
                                 start=True, stop=True)
             if n0 > 0:
-                nc.vector.tensor_copy(out=state[t][:, n0 : n0 + width], in_=acc[:, :width])
+                nc.vector.tensor_scalar(out=state[t][:, n0 : n0 + width], in0=acc[:, :width], scalar1=2.0, scalar2=0.0, op0=MULT, op1=ADD)
             else:
-                nc.scalar.copy(out=state[t][:, n0 : n0 + width], in_=acc[:, :width])
+                nc.scalar.activation(out=state[t][:, n0 : n0 + width], in_=acc[:, :width], func=COPY, scale=2.0)
+
+        for t, n0, width in [(0, 0, HALF), (0, HALF, HALF), (1, 0, S)]:
+            first_product(t, n0, width)
 
         def turn(dst, src, start, stop):
             nc.tensor.matmul(dst, lhsT=src, rhs=ident[:], start=start, stop=stop, is_transpose=True)
@@ -124,71 +135,113 @@ def tile_picked_coupled_none_p_kernel(tc, x_words, x_scales, w1, gn, w2, offs, p
         w2_codes = keep.tile([P, N], U32, name="w2_codes", align_bytes=64)
         w2_scales = keep.tile([P, N], U8, name="w2_scales", align_bytes=64)
         w2_view = w_raw[:].rearrange("p j c -> p c j")
-        minus_half_gain = keep.tile([P, PACK], F32, name="minus_half_gain")
         nc.gpsimd.tensor_scalar(out=half_gain[:], in0=gain[:], scalar1=0.5, scalar2=0.0, op0=MULT, op1=ADD)
-        nc.gpsimd.tensor_scalar(out=minus_half_gain[:], in0=gain[:], scalar1=-0.5, scalar2=0.0, op0=MULT, op1=ADD)
-        plain_h = keep.tile([P, S], F32, name="plain_h", align_bytes=64)
-        gained_h = [keep.tile([P, S], F32, name="gained_h_%d" % t, align_bytes=64) for t in range(PACK)]
+        h = [keep.tile([P, S], F32, name="h_%d" % t, align_bytes=64) for t in range(PACK)]
+        states = [state, h]
+        plain = [keep.tile([P, S], F32, name="plain_%d" % t, align_bytes=64) for t in range(PACK)]
+        base_tiles = [keep.tile([P, S], F32, name="base_%d" % t, align_bytes=64) for t in range(PACK)]
         z_planes = keep.tile([P, S // P, PACK, P], BF16, name="z_planes", align_bytes=64)
-        work = [keep.tile([P, BANK], F32, name="work_%d" % r, align_bytes=64) for r in range(WORK_TILES)]
-        for u in range(WORK_TILES, len(UNITS) - 1):
-            work.append(work[u - WORK_TILES])
-        work.append(work[len(UNITS) - 1 - LAST_LAG])
+        gathered = [keep.tile([P, BANK], F32, name="gathered_%d" % r, align_bytes=64) for r in range(GATHER_TILES)]
+        pulls = [keep.tile([P, BANK], F32, name="pull_%d" % r, align_bytes=64) for r in range(len(UNITS))]
+        done = [set() for b in range(S // P)]
+        terms = {}
+        quantized = {}
         out_view = out.rearrange("(b p) n -> p b n", p=P)
 
         def pull(u):
-            step, t, names, n0, width, way = UNITS[u]
-            for a, name in enumerate(names):
-                picked = state[t][:].indirect(lists[name][:, n0 // 16 : (n0 + width) // 16])
-                dst = work[u][:, a * width : (a + 1) * width]
-                if way == "tensor":
-                    nc.vector.tensor_scalar(out=dst, in0=picked, scalar1=-1.0, scalar2=0.0, op0=MULT, op1=ADD)
+            work = advance(gathered)
+            turned = []
+            c0 = 0
+            for step, t, a, n0, width, way in UNITS[u]:
+                window = states[step][t]
+                picked = window[:].indirect(lists[LISTS[step][a]][:, n0 // 16 : (n0 + width) // 16])
+                cols = slice(c0, c0 + width)
+                result = pulls[u][:, cols]
+                if way == "v":
+                    result = work[:, cols] if VWAIT else result
+                    nc.vector.tensor_tensor(out=result, in0=picked, in1=plain[t][:, n0 : n0 + width], op=SUBTRACT)
+                    nc.scalar.activation(out=result, in_=result, func=TANH, scale=0.5)
                 else:
-                    nc.vector.tensor_tensor(out=dst, in0=picked, in1=plain_h[:, n0 : n0 + width], op=SUBTRACT)
-                    if u == len(UNITS) - 1:
-                        nc.scalar.activation(out=dst, in_=dst, func=TANH)
-            if way == "tensor":
-                difference = advance(difference_banks)
-                for c in range(0, BANK, P):
-                    n = n0 + c % width
-                    turn(difference[:, c : c + P], state[t][:, n : n + P], c == 0, False)
-                for c in range(0, BANK, P):
-                    turn(difference[:, c : c + P], work[u][:, c : c + P], False, c == BANK - P)
-                nc.scalar.activation(out=work[u][:], in_=difference[:], func=TANH)
-            elif u < len(UNITS) - 1:
-                nc.scalar.activation(out=work[u][:], in_=work[u][:], func=TANH)
+                    nc.vector.tensor_scalar(out=work[:, cols], in0=picked, scalar1=-1.0, scalar2=0.0, op0=MULT, op1=ADD)
+                if way == "p":
+                    nc.gpsimd.tensor_tensor(out=result, in0=work[:, cols], in1=window[:, n0 : n0 + width], op=ADD)
+                    nc.scalar.activation(out=result, in_=result, func=TANH, scale=-0.5)
+                if way in "tg":
+                    turned.extend([(c0 + c, window[:, n0 + c : n0 + c + P]) for c in range(0, width, P)])
+                terms[step, t, a, n0] = (way, result)
+                c0 = c0 + width
+            parts = [turned[:2], turned[2:]] if SPLIT_LAST and u == len(UNITS) - 1 else [turned]
+            for part in parts:
+                if part:
+                    difference = advance(difference_banks)
+                    for c, own in part:
+                        turn(difference[:, c : c + P], own, c == part[0][0], False)
+                    for c, own in part:
+                        turn(difference[:, c : c + P], work[:, c : c + P], False, c == part[-1][0])
+                    cols = slice(part[0][0], part[-1][0] + P)
+                    nc.scalar.activation(out=pulls[u][:, cols], in_=difference[:, cols], func=TANH, scale=-0.5)
 
         def close(u):
-            step, t, names, n0, width, way = UNITS[u]
-            if names[-1] not in ("p2", "q2"):
-                return
-            terms = [work[u - 1][:], work[u][:]] if len(names) == 1 else [work[u][:, :width], work[u][:, width:]]
-            if way == "tensor":
+            closing = [(step, t, n0, width) for step, t, a, n0, width, way in UNITS[u] if a == 1]
+            passes = []
+            plans = []
+            c0 = 0
+            for step, t, n0, width in closing:
+                pair = [terms[step, t, a, n0] for a in range(2)]
+                base = states[step][t][:, n0 : n0 + width]
+                for way, term in pair:
+                    if way == "p":
+                        nc.gpsimd.tensor_tensor(out=base_tiles[t][:, n0 : n0 + width], in0=term, in1=base, op=ADD)
+                        base = base_tiles[t][:, n0 : n0 + width]
+                turned = [term for way, term in pair if way == "t"]
+                if pair[0][0] == "g":
+                    nc.gpsimd.tensor_tensor(out=pair[0][1], in0=pair[0][1], in1=pair[1][1], op=ADD)
+                    turned = [pair[0][1]]
+                passes.extend([(c0 + c, term[:, c : c + P]) for term in turned for c in range(0, width, P)])
+                plans.append((step, t, n0, width, pair, base, turned, c0))
+                c0 = c0 + width
+            if passes:
                 total = advance(sum_banks)
-                for a, term in enumerate(terms):
-                    for c in range(0, width, P):
-                        turn(total[:, c : c + P], term[:, c : c + P], a == 0 and c == 0, a == 1 and c == width - P)
-            if step == "first":
-                h = state[t][:, :S]
-                nc.vector.scalar_tensor_tensor(out=h, in0=total[:], scalar=-0.5, in1=h, op0=MULT, op1=ADD)
-                if t == VECTOR_PLANE:
-                    nc.scalar.copy(out=plain_h[:], in_=h)
-                nc.scalar.activation(out=gained_h[t][:], in_=h, func=COPY, scale=gain[:, t : t + 1])
-                nc.scalar.copy(out=w2_grouped[:, t * P : (t + 1) * P, :], in_=w2_view[:, t * P : (t + 1) * P, :])
-                if t == LAST_PLANE:
-                    nc.vector.quantize_mx(out=w2_codes[:].bitcast(FP8X4), scales=w2_scales[:], in_=w2_grouped[:].rearrange("p c j -> p (c j)"))
-                return
-            base = gained_h[t][:, n0 : n0 + width]
-            if way == "tensor":
-                last_term, factor = total[:, :width], minus_half_gain[:, t : t + 1]
-            else:
-                last_term, factor = terms[1], half_gain[:, t : t + 1]
-                nc.vector.scalar_tensor_tensor(out=base, in0=terms[0], scalar=factor, in1=base, op0=MULT, op1=ADD)
-            nc.vector.scalar_tensor_tensor(out=z_planes[:, n0 // P : (n0 + width) // P, t, :], in0=last_term.rearrange("p (a n) -> p a n", n=P),
-                                           scalar=factor, in1=base.rearrange("p (a n) -> p a n", n=P), op0=MULT, op1=ADD)
-            if t == VECTOR_PLANE:
-                for i, (first, nodes) in enumerate(BLOCKS):
-                    if n0 <= first < n0 + width:
+                for k, (c, block) in enumerate(passes):
+                    turn(total[:, c : c + P], block, k == 0, k == len(passes) - 1)
+            for step, t, n0, width, pair, base, turned, c0 in plans:
+                rest = [term for way, term in pair if way == "v"]
+                if turned:
+                    rest = rest + [total[:, c0 : c0 + width]]
+                factor = half_gain[:, t : t + 1]
+                if step == 0:
+                    for k, term in enumerate(rest):
+                        target = h[t][:] if k == len(rest) - 1 else base_tiles[t][:]
+                        if FIRST_FINAL[t] == "p" and k == len(rest) - 1:
+                            nc.scalar.copy(out=turned[0], in_=term)
+                            nc.gpsimd.tensor_tensor(out=target, in0=turned[0], in1=base, op=ADD)
+                        else:
+                            nc.vector.tensor_tensor(out=target, in0=term, in1=base, op=ADD)
+                        base = target
+                    later = [(n1, count, ways) for unit in SECOND for t1, n1, count, ways in unit if t1 == t]
+                    for n1, count, ways in later:
+                        if "v" in ways:
+                            nc.scalar.copy(out=plain[t][:, n1 : n1 + count], in_=h[t][:, n1 : n1 + count])
+                    plainly = [(n1, count) for n1, count, ways in later if "p" not in ways]
+                    if plainly:
+                        lo = min(n1 for n1, count in plainly)
+                        hi = max(n1 + count for n1, count in plainly)
+                        if GAIN_ON[t] == "s":
+                            nc.scalar.activation(out=base_tiles[t][:, lo:hi], in_=h[t][:, lo:hi], func=COPY, scale=factor)
+                        else:
+                            nc.gpsimd.tensor_scalar(out=base_tiles[t][:, lo:hi], in0=h[t][:, lo:hi], scalar1=factor, scalar2=0.0, op0=MULT, op1=ADD)
+                    continue
+                if "p" in [way for way, term in pair]:
+                    nc.scalar.activation(out=base, in_=base, func=COPY, scale=factor)
+                base = base_tiles[t][:, n0 : n0 + width]
+                for term in rest[:-1]:
+                    nc.vector.scalar_tensor_tensor(out=base, in0=term, scalar=factor, in1=base, op0=MULT, op1=ADD)
+                nc.vector.scalar_tensor_tensor(out=z_planes[:, n0 // P : (n0 + width) // P, t, :], in0=rest[-1].rearrange("p (a n) -> p a n", n=P),
+                                               scalar=factor, in1=base.rearrange("p (a n) -> p a n", n=P), op0=MULT, op1=ADD)
+                for b in range(n0 // P, (n0 + width) // P):
+                    done[b].add(t)
+                for i, (first, count) in enumerate(BLOCKS):
+                    if n0 <= first < n0 + width and len(done[first // P]) == PACK:
                         finish(i)
 
         def finish(i):
@@ -196,23 +249,32 @@ def tile_picked_coupled_none_p_kernel(tc, x_words, x_scales, w1, gn, w2, offs, p
             z_grouped = keep.tile([P, width, PACK], BF16, name="z_grouped_%d" % i, align_bytes=64)
             source = z_planes[:, n0 // P : (n0 + width) // P].rearrange("p a t (c i) -> p a c t i", i=PACK)
             target = z_grouped[:].rearrange("p (a c i) t -> p a c t i", c=P // PACK, i=PACK)
-            if i == 1:
+            if WEAVE[i] == "v":
                 nc.vector.tensor_copy(out=target, in_=source)
+            elif WEAVE[i] == "g":
+                nc.gpsimd.tensor_copy(out=target, in_=source)
             else:
                 nc.scalar.copy(out=target, in_=source)
             z_codes = keep.tile([P, width], U32, name="z_codes_%d" % i, align_bytes=64)
             z_scales = keep.tile([P, width], U8, name="z_scales_%d" % i, align_bytes=64)
             nc.vector.quantize_mx(out=z_codes[:].bitcast(FP8X4), scales=z_scales[:], in_=z_grouped[:].rearrange("p n t -> p (n t)"))
+            quantized[i] = (z_codes, z_scales)
+            if PRODUCT_AT[i] < 0:
+                multiply(i)
+
+        def multiply(i):
+            n0, width = BLOCKS[i]
+            z_codes, z_scales = quantized[i]
             last = i == len(BLOCKS) - 1
-            per_bank = 2 if last else BANK // width
+            per_bank = PACK // len(EMPTY[i])
             for b0 in range(0, N // P, per_bank):
-                acc = advance(difference_banks if i > 0 else sum_banks)
+                acc = advance(difference_banks if OUT_RING[i] == "d" else sum_banks)
                 for b in range(per_bank):
                     rows = slice((b0 + b) * P, (b0 + b + 1) * P)
                     nc.tensor.matmul_mx(out=acc[:, b * width : (b + 1) * width], lhsT=w2_codes[:, rows].bitcast(FP8X4), lhsT_scale=w2_scales[:, rows],
                                         rhs=z_codes[:].bitcast(FP8X4), rhs_scale=z_scales[:], start=True, stop=True)
                 result = keep.tile([P, per_bank, width], F32, name="result_%d_%d" % (i, b0), align_bytes=64)
-                if i == 1 or (last and b0 > 0):
+                if EMPTY[i][b0 // per_bank] == "v":
                     nc.vector.tensor_copy(out=result[:].rearrange("p b n -> p (b n)"), in_=acc[:, : per_bank * width])
                 else:
                     nc.scalar.copy(out=result[:].rearrange("p b n -> p (b n)"), in_=acc[:, : per_bank * width])
@@ -221,10 +283,23 @@ def tile_picked_coupled_none_p_kernel(tc, x_words, x_scales, w1, gn, w2, offs, p
 
         closed = 0
         for u in range(len(UNITS)):
-            lag = LAST_LAG if u == len(UNITS) - 1 else LAG
-            while closed <= u - lag:
+            while closed + LAGS[closed] <= u:
                 close(closed)
                 closed = closed + 1
+            if u == LATE_PRODUCT:
+                for t in (2, 3):
+                    first_product(t, 0, S)
             pull(u)
+            for i in range(len(BLOCKS)):
+                if PRODUCT_AT[i] == u:
+                    multiply(i)
+            if W2_AT <= u < W2_AT + 2 * PACK and (u - W2_AT) % 2 == 1:
+                c = (u - W2_AT) // 2
+                nc.scalar.copy(out=w2_grouped[:, c * P : (c + 1) * P, :], in_=w2_view[:, c * P : (c + 1) * P, :])
+                if c == PACK - 1:
+                    nc.vector.quantize_mx(out=w2_codes[:].bitcast(FP8X4), scales=w2_scales[:], in_=w2_grouped[:].rearrange("p c j -> p (c j)"))
         for u in range(closed, len(UNITS)):
             close(u)
+            for i in range(len(BLOCKS)):
+                if PRODUCT_AT[i] == 100 + u:
+                    multiply(i)

@@ -24,27 +24,37 @@ PACK = 4
 BANK = 512
 HALF = S // 2
 
-FIRST_WAYS = ["gg", "gg", "gg", "tt"]
+FIRST_WAYS = ["pt","tt","pt","tt"]
 FIRST_FINAL = "ppvv"
-SECOND = [[(0,0,HALF,"gg")],[(0,HALF,HALF,"gg")],[(1,0,HALF,"gg")],[(2,0,HALF,"gg")],[(3,0,HALF,"tt")],[(1,HALF,HALF,"gg")],[(2,HALF,P,"tt"),(3,HALF,P,"tt")],[(2,HALF+P,P,"tt"),(3,HALF+P,P,"vv")]]
-UNITS = [[(0, t, a, 0, S, FIRST_WAYS[t][a])] for t in range(PACK) for a in range(2)] + [
-    [(1, t, a, n0, width, ways[a]) for t, n0, width, ways in unit for a in range(2)] for unit in SECOND
-]
+SECOND = [[(0,0,0,S,"p")],[(0,1,0,S,"t")],[(1,0,0,S,"p")],[(1,1,0,S,"t")],[(2,0,0*P,P,"t"),(2,1,0*P,P,"t"),(3,0,0*P,P,"t"),(3,1,0*P,P,"t")],[(2,0,1*P,P,"t"),(2,1,1*P,P,"t"),(3,0,1*P,P,"t"),(3,1,1*P,P,"t")],[(2,0,2*P,P,"t"),(2,1,2*P,P,"t"),(3,0,2*P,P,"t"),(3,1,2*P,P,"t")],[(2,0,3*P,P,"t"),(2,1,3*P,P,"t"),(3,0,3*P,P,"t"),(3,1,3*P,P,"t")]]
+UNITS = [[(0, t, a, 0, S, FIRST_WAYS[t][a])] for t in range(PACK) for a in range(2)] + [[(1,) + piece for piece in unit] for unit in SECOND]
+AHEAD = 2
 LISTS = [("p1", "p2"), ("q1", "q2")]
-GATHER_TILES = 2
-LAGS = [4]*8+[3]*8
+GATHER_TILES = 3
+LAGS = [3,3,2,2,3,3,3,3,3,3,3,3,2,2,2,2]
 DIFFERENCE_BANKS = 3
 LATE_PRODUCT = 0
 W2_AT = 0
-WEAVE = "vsv"
-EMPTY = ["ss", "v", "sv"]
+WEAVE = "ggvv"
+EMPTY = ["s","s","sv","sv"]
 GAIN_ON = "ssss"
 SPLIT_LAST = 0
 VWAIT = 1
-PRODUCT_AT = [-1, -1, -1, -1]
-OUT_RING = "sddd"
+EARLY_STATE = {}
+Y_BANKS = [3, 4, 5, 6, 7]
+EARLY_Q = 1
+Z_POOL = [0]
+QUANT_AT = [-1,114,115,-1]
+CODE_TAG = ["","pull_14","pull_15",""]
+REUSE = {15:0}
+TAKE = 1
+GAIN_TILE = [-1,-1,6,9]
+W2_TAG = "state_2"
+W2Q_AT = 9
+PRODUCT_AT = [114,115,115,115]
+OUT_RING = "ssss"
 
-BLOCKS = [(0, HALF), (HALF, P), (HALF + P, P)]
+BLOCKS = [(0,P),(P,P),(HALF,P),(HALF+P,P)]
 
 
 def advance(ring):
@@ -64,7 +74,7 @@ def tile_picked_coupled_none_p_kernel(tc, x_words, x_scales, w1, gn, w2, offs, p
         lists = {name: keep.tile([P, S // 16], U16, name="list_" + name) for name in ("offs", "p1", "p2", "q1", "q2")}
 
         x_bytes = keep.tile([P, T], U8, name="x_bytes", align_bytes=64)
-        x_packed = keep.tile([P, T], I32, name="x_packed", align_bytes=64)
+        x_packed = keep.tile([P, T], I32, name="x_packed", tag="x_packed", align_bytes=64)
         w_raw = keep.tile([P, PACK, H], F32, name="w_raw", align_bytes=64)
         gain = keep.tile([P, PACK], F32, name="gain")
         half_gain = keep.tile([P, PACK], F32, name="half_gain")
@@ -86,7 +96,7 @@ def tile_picked_coupled_none_p_kernel(tc, x_words, x_scales, w1, gn, w2, offs, p
 
         state = []
         for t in range(PACK):
-            window = keep.tile([P, 2 * S], F32, name="state_%d" % t, align_bytes=64)
+            window = keep.tile([P, 2 * S], F32, name="state_%d" % t, tag="state_%d" % t, align_bytes=64)
             nc.gpsimd.memset(window[:, S:], 0.0)
             state.append(window)
 
@@ -96,6 +106,9 @@ def tile_picked_coupled_none_p_kernel(tc, x_words, x_scales, w1, gn, w2, offs, p
 
         w1_view = w_raw[:].rearrange("p j (m t) -> p t m j", t=PACK)
         w1_grouped = [keep.tile([P, P, PACK], BF16, name="w1_grouped_%d" % t, align_bytes=64) for t in range(PACK)]
+        if EARLY_Q:
+            late_grouped = keep.tile([P, 2, P, PACK], BF16, name="late_grouped", align_bytes=64)
+            w1_grouped[2:] = [late_grouped[:, 0], late_grouped[:, 1]]
         nc.vector.tensor_copy(out=w1_grouped[0][:], in_=w1_view[:, 0])
         for t in range(1, PACK):
             nc.scalar.copy(out=w1_grouped[t][:], in_=w1_view[:, t])
@@ -112,10 +125,17 @@ def tile_picked_coupled_none_p_kernel(tc, x_words, x_scales, w1, gn, w2, offs, p
             nc.vector.tensor_copy(out=picked_words[:, n0 : n0 + HALF],
                                   in_=x_packed[:].bitcast(U32).indirect(lists["offs"][:, n0 // 16 : (n0 + HALF) // 16]))
 
+        if EARLY_Q:
+            late_codes = keep.tile([P, 2 * P], U32, name="late_codes", tag="x_packed", align_bytes=64)
+            late_scales = keep.tile([P, 2 * P], U8, name="late_scales", align_bytes=64)
+            nc.vector.quantize_mx(out=late_codes[:].bitcast(FP8X4), scales=late_scales[:], in_=late_grouped[:].rearrange("p t m j -> p (t m j)"))
+            w1_codes[2:] = [late_codes[:, :P], late_codes[:, P:]]
+            w1_scales[2:] = [late_scales[:, :P], late_scales[:, P:]]
+
         def first_product(t, n0, width):
-            if t >= 2:
+            if t >= 2 and not EARLY_Q:
                 quantize_w1(t)
-            acc = advance(sum_banks)
+            acc = banks[Y_BANKS[t + 1 if t or n0 else 0]]
             nc.tensor.matmul_mx(out=acc[:, :width], lhsT=w1_codes[t][:].bitcast(FP8X4), lhsT_scale=w1_scales[t][:],
                                 rhs=picked_words[:, n0 : n0 + width].bitcast(FP8X4), rhs_scale=picked_bytes[:, n0 : n0 + width],
                                 start=True, stop=True)
@@ -132,24 +152,39 @@ def tile_picked_coupled_none_p_kernel(tc, x_words, x_scales, w1, gn, w2, offs, p
 
         nc.sync.dma_start(out=w_raw[:], in_=w2.rearrange("(p j) c -> p j c", j=PACK))
         w2_grouped = keep.tile([P, N, PACK], BF16, name="w2_grouped", align_bytes=64)
-        w2_codes = keep.tile([P, N], U32, name="w2_codes", align_bytes=64)
+        w2_codes = keep.tile([P, N], U32, name="w2_codes", tag=W2_TAG, align_bytes=64)
         w2_scales = keep.tile([P, N], U8, name="w2_scales", align_bytes=64)
         w2_view = w_raw[:].rearrange("p j c -> p c j")
         nc.gpsimd.tensor_scalar(out=half_gain[:], in0=gain[:], scalar1=0.5, scalar2=0.0, op0=MULT, op1=ADD)
-        h = [keep.tile([P, S], F32, name="h_%d" % t, align_bytes=64) for t in range(PACK)]
+        h = state[:2] + [keep.tile([P, S], F32, name="h_%d" % t, align_bytes=64) for t in range(2, PACK)]
         states = [state, h]
         plain = [keep.tile([P, S], F32, name="plain_%d" % t, align_bytes=64) for t in range(PACK)]
         base_tiles = [keep.tile([P, S], F32, name="base_%d" % t, align_bytes=64) for t in range(PACK)]
         z_planes = keep.tile([P, S // P, PACK, P], BF16, name="z_planes", align_bytes=64)
-        gathered = [keep.tile([P, BANK], F32, name="gathered_%d" % r, align_bytes=64) for r in range(GATHER_TILES)]
-        pulls = [keep.tile([P, BANK], F32, name="pull_%d" % r, align_bytes=64) for r in range(len(UNITS))]
+        turning = [u for u in range(len(UNITS)) if UNITS[u][0][5] != "p"]
+        release = [max([v for v in turning if v <= u - AHEAD] + [-1]) for u in range(len(UNITS))]
+        places = []
+        for u in range(len(UNITS)):
+            v = release[u]
+            if v < 0:
+                places.append((keep.tile([P, 4 * BANK], F32, name="strip_%d" % u, align_bytes=64), BANK))
+            elif u + 1 < len(UNITS) and release[u + 1] == v:
+                places.append((places[v][0], places[v][1] - P))
+            elif release[u - 1] == v:
+                places.append((places[v][0], places[v][1] + BANK - P))
+            else:
+                places.append(places[v])
+        pulls = [keep.tile([P, BANK], F32, name="pull_%d" % r, tag="pull_%d" % r, align_bytes=64) for r in range(len(UNITS))]
+        gain_tiles = [pulls[GAIN_TILE[t]] if GAIN_TILE[t] >= 0 else base_tiles[t] for t in range(PACK)]
         done = [set() for b in range(S // P)]
         terms = {}
         quantized = {}
+        woven = {}
+        opened = {}
         out_view = out.rearrange("(b p) n -> p b n", p=P)
 
         def pull(u):
-            work = advance(gathered)
+            work = places[u][0][:, places[u][1] : places[u][1] + BANK]
             turned = []
             c0 = 0
             for step, t, a, n0, width, way in UNITS[u]:
@@ -157,31 +192,71 @@ def tile_picked_coupled_none_p_kernel(tc, x_words, x_scales, w1, gn, w2, offs, p
                 picked = window[:].indirect(lists[LISTS[step][a]][:, n0 // 16 : (n0 + width) // 16])
                 cols = slice(c0, c0 + width)
                 result = pulls[u][:, cols]
+                spot = work[:, cols]
+                if u in REUSE:
+                    owner = c0 // P
+                    spot = (base_tiles if owner < 2 else gain_tiles)[owner][:, REUSE[u] * P : (REUSE[u] + 1) * P]
                 if way == "v":
                     result = work[:, cols] if VWAIT else result
                     nc.vector.tensor_tensor(out=result, in0=picked, in1=plain[t][:, n0 : n0 + width], op=SUBTRACT)
                     nc.scalar.activation(out=result, in_=result, func=TANH, scale=0.5)
                 else:
-                    nc.vector.tensor_scalar(out=work[:, cols], in0=picked, scalar1=-1.0, scalar2=0.0, op0=MULT, op1=ADD)
+                    nc.vector.tensor_scalar(out=spot, in0=picked, scalar1=-1.0, scalar2=0.0, op0=MULT, op1=ADD)
                 if way == "p":
+                    result = pulls[u - 3][:, cols] if u >= 3 else work[:, cols]
                     nc.gpsimd.tensor_tensor(out=result, in0=work[:, cols], in1=window[:, n0 : n0 + width], op=ADD)
                     nc.scalar.activation(out=result, in_=result, func=TANH, scale=-0.5)
                 if way in "tg":
-                    turned.extend([(c0 + c, window[:, n0 + c : n0 + c + P]) for c in range(0, width, P)])
+                    turned.extend([(c0 + c, window[:, n0 + c : n0 + c + P], spot[:, c : c + P]) for c in range(0, width, P)])
                 terms[step, t, a, n0] = (way, result)
+                c0 = c0 + width
+            parts = [turned[:2], turned[2:]] if SPLIT_LAST and u == len(UNITS) - 1 else [turned]
+            for v in [u] + EARLY_STATE.get(u, []):
+                open_difference(v)
+            for part in parts:
+                if part:
+                    difference = opened[u, part[0][0]]
+                    for c, own, other in part:
+                        turn(difference[:, c : c + P], other, False, c == part[-1][0])
+                    cols = slice(part[0][0], part[-1][0] + P)
+                    nc.scalar.activation(out=pulls[u][:, cols], in_=difference[:, cols], func=TANH, scale=-0.5)
+
+        def open_difference(u):
+            if u in opened:
+                return
+            opened[u] = True
+            turned = []
+            c0 = 0
+            for step, t, a, n0, width, way in UNITS[u]:
+                if way in "tg":
+                    turned.extend([(c0 + c, states[step][t][:, n0 + c : n0 + c + P]) for c in range(0, width, P)])
                 c0 = c0 + width
             parts = [turned[:2], turned[2:]] if SPLIT_LAST and u == len(UNITS) - 1 else [turned]
             for part in parts:
                 if part:
                     difference = advance(difference_banks)
+                    opened[u, part[0][0]] = difference
                     for c, own in part:
                         turn(difference[:, c : c + P], own, c == part[0][0], False)
-                    for c, own in part:
-                        turn(difference[:, c : c + P], work[:, c : c + P], False, c == part[-1][0])
-                    cols = slice(part[0][0], part[-1][0] + P)
-                    nc.scalar.activation(out=pulls[u][:, cols], in_=difference[:, cols], func=TANH, scale=-0.5)
+
+        def gained(t):
+            plainly = [(n1, count) for unit in SECOND for t1, a1, n1, count, ways in unit if t1 == t and a1 == 0 and "p" not in ways]
+            if plainly:
+                lo = min(n1 for n1, count in plainly)
+                hi = max(n1 + count for n1, count in plainly)
+                target = gain_tiles[t]
+                if GAIN_ON[t] == "s":
+                    nc.scalar.activation(out=target[:, lo:hi], in_=h[t][:, lo:hi], func=COPY, scale=half_gain[:, t : t + 1])
+                else:
+                    nc.gpsimd.tensor_scalar(out=target[:, lo:hi], in0=h[t][:, lo:hi], scalar1=half_gain[:, t : t + 1], scalar2=0.0, op0=MULT, op1=ADD)
 
         def close(u):
+            closing_work(u)
+            for t in range(PACK):
+                if GAIN_TILE[t] | 1 == u and GAIN_TILE[t] >= 0:
+                    gained(t)
+
+        def closing_work(u):
             closing = [(step, t, n0, width) for step, t, a, n0, width, way in UNITS[u] if a == 1]
             passes = []
             plans = []
@@ -211,32 +286,32 @@ def tile_picked_coupled_none_p_kernel(tc, x_words, x_scales, w1, gn, w2, offs, p
                 factor = half_gain[:, t : t + 1]
                 if step == 0:
                     for k, term in enumerate(rest):
-                        target = h[t][:] if k == len(rest) - 1 else base_tiles[t][:]
+                        target = h[t][:, :S] if k == len(rest) - 1 else base_tiles[t][:]
                         if FIRST_FINAL[t] == "p" and k == len(rest) - 1:
-                            nc.scalar.copy(out=turned[0], in_=term)
-                            nc.gpsimd.tensor_tensor(out=target, in0=turned[0], in1=base, op=ADD)
+                            nc.scalar.copy(out=pulls[2 * t][:], in_=term)
+                            nc.gpsimd.tensor_tensor(out=target, in0=pulls[2 * t][:], in1=base, op=ADD)
                         else:
                             nc.vector.tensor_tensor(out=target, in0=term, in1=base, op=ADD)
                         base = target
-                    later = [(n1, count, ways) for unit in SECOND for t1, n1, count, ways in unit if t1 == t]
+                    later = [(n1, count, ways) for unit in SECOND for t1, a1, n1, count, ways in unit if t1 == t and a1 == 1]
                     for n1, count, ways in later:
                         if "v" in ways:
                             nc.scalar.copy(out=plain[t][:, n1 : n1 + count], in_=h[t][:, n1 : n1 + count])
-                    plainly = [(n1, count) for n1, count, ways in later if "p" not in ways]
-                    if plainly:
-                        lo = min(n1 for n1, count in plainly)
-                        hi = max(n1 + count for n1, count in plainly)
-                        if GAIN_ON[t] == "s":
-                            nc.scalar.activation(out=base_tiles[t][:, lo:hi], in_=h[t][:, lo:hi], func=COPY, scale=factor)
-                        else:
-                            nc.gpsimd.tensor_scalar(out=base_tiles[t][:, lo:hi], in0=h[t][:, lo:hi], scalar1=factor, scalar2=0.0, op0=MULT, op1=ADD)
+                    if GAIN_TILE[t] < 0:
+                        gained(t)
                     continue
                 if "p" in [way for way, term in pair]:
                     nc.scalar.activation(out=base, in_=base, func=COPY, scale=factor)
-                base = base_tiles[t][:, n0 : n0 + width]
+                else:
+                    base = gain_tiles[t][:, n0 : n0 + width]
                 for term in rest[:-1]:
                     nc.vector.scalar_tensor_tensor(out=base, in0=term, scalar=factor, in1=base, op0=MULT, op1=ADD)
-                nc.vector.scalar_tensor_tensor(out=z_planes[:, n0 // P : (n0 + width) // P, t, :], in0=rest[-1].rearrange("p (a n) -> p a n", n=P),
+                if t in Z_POOL:
+                    nc.scalar.activation(out=pulls[u - 1][:], in_=rest[-1], func=COPY, scale=factor)
+                    nc.gpsimd.tensor_tensor(out=z_planes[:, n0 // P : (n0 + width) // P, t, :], in0=pulls[u - 1][:].rearrange("p (a n) -> p a n", n=P),
+                                            in1=base.rearrange("p (a n) -> p a n", n=P), op=ADD)
+                else:
+                    nc.vector.scalar_tensor_tensor(out=z_planes[:, n0 // P : (n0 + width) // P, t, :], in0=rest[-1].rearrange("p (a n) -> p a n", n=P),
                                                scalar=factor, in1=base.rearrange("p (a n) -> p a n", n=P), op0=MULT, op1=ADD)
                 for b in range(n0 // P, (n0 + width) // P):
                     done[b].add(t)
@@ -252,10 +327,19 @@ def tile_picked_coupled_none_p_kernel(tc, x_words, x_scales, w1, gn, w2, offs, p
             if WEAVE[i] == "v":
                 nc.vector.tensor_copy(out=target, in_=source)
             elif WEAVE[i] == "g":
-                nc.gpsimd.tensor_copy(out=target, in_=source)
+                nc.gpsimd.tensor_scalar(out=z_grouped[:].rearrange("p (a n) t -> p a n t", n=P),
+                                        in0=z_planes[:, n0 // P : (n0 + width) // P].rearrange("p a t n -> p a n t"),
+                                        scalar1=1.0, scalar2=0.0, op0=MULT, op1=ADD)
             else:
                 nc.scalar.copy(out=target, in_=source)
-            z_codes = keep.tile([P, width], U32, name="z_codes_%d" % i, align_bytes=64)
+            woven[i] = z_grouped
+            if QUANT_AT[i] < 0:
+                quantize_z(i)
+
+        def quantize_z(i):
+            n0, width = BLOCKS[i]
+            z_grouped = woven[i]
+            z_codes = keep.tile([P, width], U32, name="z_codes_%d" % i, tag=CODE_TAG[i] or "z_codes_%d" % i, align_bytes=64)
             z_scales = keep.tile([P, width], U8, name="z_scales_%d" % i, align_bytes=64)
             nc.vector.quantize_mx(out=z_codes[:].bitcast(FP8X4), scales=z_scales[:], in_=z_grouped[:].rearrange("p n t -> p (n t)"))
             quantized[i] = (z_codes, z_scales)
@@ -296,10 +380,13 @@ def tile_picked_coupled_none_p_kernel(tc, x_words, x_scales, w1, gn, w2, offs, p
             if W2_AT <= u < W2_AT + 2 * PACK and (u - W2_AT) % 2 == 1:
                 c = (u - W2_AT) // 2
                 nc.scalar.copy(out=w2_grouped[:, c * P : (c + 1) * P, :], in_=w2_view[:, c * P : (c + 1) * P, :])
-                if c == PACK - 1:
+            if u == max(W2Q_AT, W2_AT + 2 * PACK - 1):
                     nc.vector.quantize_mx(out=w2_codes[:].bitcast(FP8X4), scales=w2_scales[:], in_=w2_grouped[:].rearrange("p c j -> p (c j)"))
         for u in range(closed, len(UNITS)):
             close(u)
+            for i in range(len(BLOCKS)):
+                if QUANT_AT[i] == 100 + u:
+                    quantize_z(i)
             for i in range(len(BLOCKS)):
                 if PRODUCT_AT[i] == 100 + u:
                     multiply(i)

@@ -24,14 +24,14 @@ PACK = 4
 BANK = 512
 HALF = S // 2
 
-FIRST_WAYS = ["pt","tt","pt","tt"]
+FIRST_WAYS = ["tt","tt","pt","tt"]
 FIRST_FINAL = "ppvv"
-SECOND = [[(0,0,0,S,"p")],[(0,1,0,S,"t")],[(1,0,0,S,"p")],[(1,1,0,S,"t")],[(2,0,0*P,P,"t"),(2,1,0*P,P,"t"),(3,0,0*P,P,"t"),(3,1,0*P,P,"t")],[(2,0,1*P,P,"t"),(2,1,1*P,P,"t"),(3,0,1*P,P,"t"),(3,1,1*P,P,"t")],[(2,0,2*P,P,"t"),(2,1,2*P,P,"t"),(3,0,2*P,P,"t"),(3,1,2*P,P,"t")],[(2,0,3*P,P,"t"),(2,1,3*P,P,"t"),(3,0,3*P,P,"t"),(3,1,3*P,P,"t")]]
+SECOND = [[(0,0,0,S,"t")],[(0,1,0,S,"t")],[(1,0,0,S,"p")],[(1,1,0,S,"t")],[(2,0,0*P,P,"t"),(2,1,0*P,P,"t"),(3,0,0*P,P,"t"),(3,1,0*P,P,"t")],[(2,0,1*P,P,"t"),(2,1,1*P,P,"t"),(3,0,1*P,P,"t"),(3,1,1*P,P,"t")],[(2,0,2*P,P,"t"),(2,1,2*P,P,"t"),(3,0,2*P,P,"t"),(3,1,2*P,P,"t")],[(2,0,3*P,P,"t"),(2,1,3*P,P,"t"),(3,0,3*P,P,"t"),(3,1,3*P,P,"t")]]
 UNITS = [[(0, t, a, 0, S, FIRST_WAYS[t][a])] for t in range(PACK) for a in range(2)] + [[(1,) + piece for piece in unit] for unit in SECOND]
-AHEAD = 2
+AHEAD = 3
 LISTS = [("p1", "p2"), ("q1", "q2")]
 GATHER_TILES = 3
-LAGS = [3,3,2,2,3,3,3,3,3,3,3,3,2,2,2,2]
+LAGS = [3,3,2,2,3,3,3,3,2,2,3,3,2,2,2,2]
 DIFFERENCE_BANKS = 3
 LATE_PRODUCT = 0
 W2_AT = 0
@@ -40,15 +40,18 @@ EMPTY = ["s","s","sv","sv"]
 GAIN_ON = "ssss"
 SPLIT_LAST = 0
 VWAIT = 1
+SWAP = 0
+SPLIT_BACK = 0
+WIDE = 2
 EARLY_STATE = {}
 Y_BANKS = [3, 4, 5, 6, 7]
 EARLY_Q = 1
 Z_POOL = [0]
 QUANT_AT = [-1,114,115,-1]
 CODE_TAG = ["","pull_14","pull_15",""]
-REUSE = {15:0}
+REUSE = {15:[(0,0),(1,0),(2,0),(3,0)]}
 TAKE = 1
-GAIN_TILE = [-1,-1,6,9]
+GAIN_TILE = [5,-1,6,9]
 W2_TAG = "state_2"
 W2Q_AT = 9
 PRODUCT_AT = [114,115,115,115]
@@ -156,35 +159,27 @@ def tile_picked_coupled_none_p_kernel(tc, x_words, x_scales, w1, gn, w2, offs, p
         w2_scales = keep.tile([P, N], U8, name="w2_scales", align_bytes=64)
         w2_view = w_raw[:].rearrange("p j c -> p c j")
         nc.gpsimd.tensor_scalar(out=half_gain[:], in0=gain[:], scalar1=0.5, scalar2=0.0, op0=MULT, op1=ADD)
-        h = state[:2] + [keep.tile([P, S], F32, name="h_%d" % t, align_bytes=64) for t in range(2, PACK)]
+        h = state[:WIDE] + [keep.tile([P, S], F32, name="h_%d" % t, align_bytes=64) for t in range(WIDE, PACK)]
         states = [state, h]
         plain = [keep.tile([P, S], F32, name="plain_%d" % t, align_bytes=64) for t in range(PACK)]
         base_tiles = [keep.tile([P, S], F32, name="base_%d" % t, align_bytes=64) for t in range(PACK)]
         z_planes = keep.tile([P, S // P, PACK, P], BF16, name="z_planes", align_bytes=64)
-        turning = [u for u in range(len(UNITS)) if UNITS[u][0][5] != "p"]
-        release = [max([v for v in turning if v <= u - AHEAD] + [-1]) for u in range(len(UNITS))]
-        places = []
-        for u in range(len(UNITS)):
-            v = release[u]
-            if v < 0:
-                places.append((keep.tile([P, 4 * BANK], F32, name="strip_%d" % u, align_bytes=64), BANK))
-            elif u + 1 < len(UNITS) and release[u + 1] == v:
-                places.append((places[v][0], places[v][1] - P))
-            elif release[u - 1] == v:
-                places.append((places[v][0], places[v][1] + BANK - P))
-            else:
-                places.append(places[v])
+        ring = [keep.tile([P, BANK], F32, name="gathered_%d" % r, align_bytes=64) for r in range(AHEAD)]
         pulls = [keep.tile([P, BANK], F32, name="pull_%d" % r, tag="pull_%d" % r, align_bytes=64) for r in range(len(UNITS))]
         gain_tiles = [pulls[GAIN_TILE[t]] if GAIN_TILE[t] >= 0 else base_tiles[t] for t in range(PACK)]
         done = [set() for b in range(S // P)]
         terms = {}
         quantized = {}
         woven = {}
+        begun = {}
         opened = {}
         out_view = out.rearrange("(b p) n -> p b n", p=P)
 
         def pull(u):
-            work = places[u][0][:, places[u][1] : places[u][1] + BANK]
+            v = u - AHEAD
+            if v >= 0 and UNITS[v][0][5] == "p" and SWAP:
+                ring[u % AHEAD] = pulls[v - 1] if v > 0 else keep.tile([P, BANK], F32, name="gathered_spare", align_bytes=64)
+            work = ring[u % AHEAD]
             turned = []
             c0 = 0
             for step, t, a, n0, width, way in UNITS[u]:
@@ -193,18 +188,21 @@ def tile_picked_coupled_none_p_kernel(tc, x_words, x_scales, w1, gn, w2, offs, p
                 cols = slice(c0, c0 + width)
                 result = pulls[u][:, cols]
                 spot = work[:, cols]
-                if u in REUSE:
-                    owner = c0 // P
-                    spot = (base_tiles if owner < 2 else gain_tiles)[owner][:, REUSE[u] * P : (REUSE[u] + 1) * P]
+                if u in REUSE and REUSE[u][c0 // width]:
+                    owner, first = REUSE[u][c0 // width]
+                    if isinstance(owner, str):
+                        spot = keep.tile([P, S], F32, name="after_" + owner, tag=owner, align_bytes=64)[:, first : first + width]
+                    else:
+                        spot = (gain_tiles + base_tiles)[owner][:, first : first + width]
                 if way == "v":
-                    result = work[:, cols] if VWAIT else result
+                    result = spot
                     nc.vector.tensor_tensor(out=result, in0=picked, in1=plain[t][:, n0 : n0 + width], op=SUBTRACT)
                     nc.scalar.activation(out=result, in_=result, func=TANH, scale=0.5)
                 else:
                     nc.vector.tensor_scalar(out=spot, in0=picked, scalar1=-1.0, scalar2=0.0, op0=MULT, op1=ADD)
                 if way == "p":
-                    result = pulls[u - 3][:, cols] if u >= 3 else work[:, cols]
-                    nc.gpsimd.tensor_tensor(out=result, in0=work[:, cols], in1=window[:, n0 : n0 + width], op=ADD)
+                    result = pulls[u - 3][:, cols]
+                    nc.gpsimd.tensor_tensor(out=result, in0=spot, in1=window[:, n0 : n0 + width], op=ADD)
                     nc.scalar.activation(out=result, in_=result, func=TANH, scale=-0.5)
                 if way in "tg":
                     turned.extend([(c0 + c, window[:, n0 + c : n0 + c + P], spot[:, c : c + P]) for c in range(0, width, P)])
@@ -272,13 +270,17 @@ def tile_picked_coupled_none_p_kernel(tc, x_words, x_scales, w1, gn, w2, offs, p
                 if pair[0][0] == "g":
                     nc.gpsimd.tensor_tensor(out=pair[0][1], in0=pair[0][1], in1=pair[1][1], op=ADD)
                     turned = [pair[0][1]]
-                passes.extend([(c0 + c, term[:, c : c + P]) for term in turned for c in range(0, width, P)])
+                passes.extend([(c0 + c, term[:, c : c + P]) for term in (turned[1:] if u - 1 in begun else turned) for c in range(0, width, P)])
                 plans.append((step, t, n0, width, pair, base, turned, c0))
                 c0 = c0 + width
+            if not closing and UNITS[u][0][5] == "t" and UNITS[u + 1][0][5] == "t" and SPLIT_BACK:
+                begun[u] = advance(sum_banks)
+                for c in range(0, S, P):
+                    turn(begun[u][:, c : c + P], pulls[u][:, c : c + P], c == 0, False)
             if passes:
-                total = advance(sum_banks)
+                total = begun[u - 1] if u - 1 in begun else advance(sum_banks)
                 for k, (c, block) in enumerate(passes):
-                    turn(total[:, c : c + P], block, k == 0, k == len(passes) - 1)
+                    turn(total[:, c : c + P], block, k == 0 and u - 1 not in begun, k == len(passes) - 1)
             for step, t, n0, width, pair, base, turned, c0 in plans:
                 rest = [term for way, term in pair if way == "v"]
                 if turned:
@@ -307,8 +309,8 @@ def tile_picked_coupled_none_p_kernel(tc, x_words, x_scales, w1, gn, w2, offs, p
                 for term in rest[:-1]:
                     nc.vector.scalar_tensor_tensor(out=base, in0=term, scalar=factor, in1=base, op0=MULT, op1=ADD)
                 if t in Z_POOL:
-                    nc.scalar.activation(out=pulls[u - 1][:], in_=rest[-1], func=COPY, scale=factor)
-                    nc.gpsimd.tensor_tensor(out=z_planes[:, n0 // P : (n0 + width) // P, t, :], in0=pulls[u - 1][:].rearrange("p (a n) -> p a n", n=P),
+                    nc.scalar.activation(out=pulls[u - 1][:, :width], in_=rest[-1], func=COPY, scale=factor)
+                    nc.gpsimd.tensor_tensor(out=z_planes[:, n0 // P : (n0 + width) // P, t, :], in0=pulls[u - 1][:, :width].rearrange("p (a n) -> p a n", n=P),
                                             in1=base.rearrange("p (a n) -> p a n", n=P), op=ADD)
                 else:
                     nc.vector.scalar_tensor_tensor(out=z_planes[:, n0 // P : (n0 + width) // P, t, :], in0=rest[-1].rearrange("p (a n) -> p a n", n=P),

@@ -24,14 +24,14 @@ PACK = 4
 BANK = 512
 HALF = S // 2
 
-FIRST_WAYS = ["tt","tt","pt","tt"]
+FIRST_WAYS = ["pt","tt","pt","tt"]
 FIRST_FINAL = "ppvv"
-SECOND = [[(0,0,0,S,"t")],[(0,1,0,S,"t")],[(1,0,0,S,"p")],[(1,1,0,S,"t")],[(2,0,0*P,P,"t"),(2,1,0*P,P,"t"),(3,0,0*P,P,"t"),(3,1,0*P,P,"t")],[(2,0,1*P,P,"t"),(2,1,1*P,P,"t"),(3,0,1*P,P,"t"),(3,1,1*P,P,"t")],[(2,0,2*P,P,"t"),(2,1,2*P,P,"t"),(3,0,2*P,P,"t"),(3,1,2*P,P,"t")],[(2,0,3*P,P,"t"),(2,1,3*P,P,"t"),(3,0,3*P,P,"t"),(3,1,3*P,P,"t")]]
+SECOND = [[(0,0,0,S,"p")],[(0,1,0,S,"t")],[(1,0,0,S,"p")],[(1,1,0,S,"t")],[(2,0,0*P,P,"t"),(2,1,0*P,P,"t"),(3,0,0*P,P,"t"),(3,1,0*P,P,"t")],[(2,0,1*P,P,"t"),(2,1,1*P,P,"t"),(3,0,1*P,P,"t"),(3,1,1*P,P,"t")],[(2,0,2*P,P,"t"),(2,1,2*P,P,"t"),(3,0,2*P,P,"t"),(3,1,2*P,P,"t")],[(2,0,3*P,P,"t"),(2,1,3*P,P,"t"),(3,0,3*P,P,"t"),(3,1,3*P,P,"t")]]
 UNITS = [[(0, t, a, 0, S, FIRST_WAYS[t][a])] for t in range(PACK) for a in range(2)] + [[(1,) + piece for piece in unit] for unit in SECOND]
 AHEAD = 3
 LISTS = [("p1", "p2"), ("q1", "q2")]
 GATHER_TILES = 3
-LAGS = [3,3,2,2,3,3,3,3,2,2,3,3,2,2,2,2]
+LAGS = [3,3,2,2,3,3,3,3,3,3,3,3,2,2,2,2]
 DIFFERENCE_BANKS = 3
 LATE_PRODUCT = 0
 W2_AT = 0
@@ -40,6 +40,7 @@ EMPTY = ["s","s","sv","sv"]
 GAIN_ON = "ssss"
 SPLIT_LAST = 0
 VWAIT = 1
+PLAIN = 1
 SWAP = 0
 SPLIT_BACK = 0
 WIDE = 2
@@ -51,7 +52,7 @@ QUANT_AT = [-1,114,115,-1]
 CODE_TAG = ["","pull_14","pull_15",""]
 REUSE = {15:[(0,0),(1,0),(2,0),(3,0)]}
 TAKE = 1
-GAIN_TILE = [5,-1,6,9]
+GAIN_TILE = [-1,-1,6,9]
 W2_TAG = "state_2"
 W2Q_AT = 9
 PRODUCT_AT = [114,115,115,115]
@@ -135,6 +136,8 @@ def tile_picked_coupled_none_p_kernel(tc, x_words, x_scales, w1, gn, w2, offs, p
             w1_codes[2:] = [late_codes[:, :P], late_codes[:, P:]]
             w1_scales[2:] = [late_scales[:, :P], late_scales[:, P:]]
 
+        minus = [keep.tile([P, S], F32, name="minus_%d" % t, align_bytes=64) for t in range(PACK)]
+
         def first_product(t, n0, width):
             if t >= 2 and not EARLY_Q:
                 quantize_w1(t)
@@ -146,6 +149,8 @@ def tile_picked_coupled_none_p_kernel(tc, x_words, x_scales, w1, gn, w2, offs, p
                 nc.vector.tensor_scalar(out=state[t][:, n0 : n0 + width], in0=acc[:, :width], scalar1=2.0, scalar2=0.0, op0=MULT, op1=ADD)
             else:
                 nc.scalar.activation(out=state[t][:, n0 : n0 + width], in_=acc[:, :width], func=COPY, scale=2.0)
+            if PLAIN and FIRST_WAYS[t] != "pp":
+                nc.scalar.activation(out=minus[t][:, n0 : n0 + width], in_=acc[:, :width], func=COPY, scale=-2.0)
 
         for t, n0, width in [(0, 0, HALF), (0, HALF, HALF), (1, 0, S)]:
             first_product(t, n0, width)
@@ -198,12 +203,14 @@ def tile_picked_coupled_none_p_kernel(tc, x_words, x_scales, w1, gn, w2, offs, p
                     result = spot
                     nc.vector.tensor_tensor(out=result, in0=picked, in1=plain[t][:, n0 : n0 + width], op=SUBTRACT)
                     nc.scalar.activation(out=result, in_=result, func=TANH, scale=0.5)
+                elif PLAIN and (step == 0 or way == "p"):
+                    nc.vector.tensor_copy(out=spot, in_=picked)
                 else:
                     nc.vector.tensor_scalar(out=spot, in0=picked, scalar1=-1.0, scalar2=0.0, op0=MULT, op1=ADD)
                 if way == "p":
                     result = pulls[u - 3][:, cols]
-                    nc.gpsimd.tensor_tensor(out=result, in0=spot, in1=window[:, n0 : n0 + width], op=ADD)
-                    nc.scalar.activation(out=result, in_=result, func=TANH, scale=-0.5)
+                    nc.gpsimd.tensor_tensor(out=result, in0=spot, in1=window[:, n0 : n0 + width], op=SUBTRACT if PLAIN else ADD)
+                    nc.scalar.activation(out=result, in_=result, func=TANH, scale=0.5 if PLAIN else -0.5)
                 if way in "tg":
                     turned.extend([(c0 + c, window[:, n0 + c : n0 + c + P], spot[:, c : c + P]) for c in range(0, width, P)])
                 terms[step, t, a, n0] = (way, result)
@@ -217,7 +224,7 @@ def tile_picked_coupled_none_p_kernel(tc, x_words, x_scales, w1, gn, w2, offs, p
                     for c, own, other in part:
                         turn(difference[:, c : c + P], other, False, c == part[-1][0])
                     cols = slice(part[0][0], part[-1][0] + P)
-                    nc.scalar.activation(out=pulls[u][:, cols], in_=difference[:, cols], func=TANH, scale=-0.5)
+                    nc.scalar.activation(out=pulls[u][:, cols], in_=difference[:, cols], func=TANH, scale=0.5 if PLAIN and u < 2 * PACK else -0.5)
 
         def open_difference(u):
             if u in opened:
@@ -227,7 +234,7 @@ def tile_picked_coupled_none_p_kernel(tc, x_words, x_scales, w1, gn, w2, offs, p
             c0 = 0
             for step, t, a, n0, width, way in UNITS[u]:
                 if way in "tg":
-                    turned.extend([(c0 + c, states[step][t][:, n0 + c : n0 + c + P]) for c in range(0, width, P)])
+                    turned.extend([(c0 + c, (minus if PLAIN and step == 0 else states[step])[t][:, n0 + c : n0 + c + P]) for c in range(0, width, P)])
                 c0 = c0 + width
             parts = [turned[:2], turned[2:]] if SPLIT_LAST and u == len(UNITS) - 1 else [turned]
             for part in parts:
@@ -290,8 +297,8 @@ def tile_picked_coupled_none_p_kernel(tc, x_words, x_scales, w1, gn, w2, offs, p
                     for k, term in enumerate(rest):
                         target = h[t][:, :S] if k == len(rest) - 1 else base_tiles[t][:]
                         if FIRST_FINAL[t] == "p" and k == len(rest) - 1:
-                            nc.scalar.copy(out=pulls[2 * t][:], in_=term)
-                            nc.gpsimd.tensor_tensor(out=target, in0=pulls[2 * t][:], in1=base, op=ADD)
+                            nc.scalar.copy(out=plain[t][:], in_=term)
+                            nc.gpsimd.tensor_tensor(out=target, in0=plain[t][:], in1=base, op=ADD)
                         else:
                             nc.vector.tensor_tensor(out=target, in0=term, in1=base, op=ADD)
                         base = target
@@ -309,8 +316,8 @@ def tile_picked_coupled_none_p_kernel(tc, x_words, x_scales, w1, gn, w2, offs, p
                 for term in rest[:-1]:
                     nc.vector.scalar_tensor_tensor(out=base, in0=term, scalar=factor, in1=base, op0=MULT, op1=ADD)
                 if t in Z_POOL:
-                    nc.scalar.activation(out=pulls[u - 1][:, :width], in_=rest[-1], func=COPY, scale=factor)
-                    nc.gpsimd.tensor_tensor(out=z_planes[:, n0 // P : (n0 + width) // P, t, :], in0=pulls[u - 1][:, :width].rearrange("p (a n) -> p a n", n=P),
+                    nc.scalar.activation(out=plain[t][:, :width], in_=rest[-1], func=COPY, scale=factor)
+                    nc.gpsimd.tensor_tensor(out=z_planes[:, n0 // P : (n0 + width) // P, t, :], in0=plain[t][:, :width].rearrange("p (a n) -> p a n", n=P),
                                             in1=base.rearrange("p (a n) -> p a n", n=P), op=ADD)
                 else:
                     nc.vector.scalar_tensor_tensor(out=z_planes[:, n0 // P : (n0 + width) // P, t, :], in0=rest[-1].rearrange("p (a n) -> p a n", n=P),

@@ -23,47 +23,9 @@ P = 128
 PACK = 4
 BANK = 512
 HALF = S // 2
-
-FIRST_WAYS = ["pt","tt","pt","tt"]
-FIRST_FINAL = "ppvv"
-SECOND = [[(0,0,0,S,"p")],[(0,1,0,S,"t")],[(1,0,0,S,"p")],[(1,1,0,S,"t")],[(2,0,0*P,P,"t"),(2,1,0*P,P,"t"),(3,0,0*P,P,"t"),(3,1,0*P,P,"t")],[(2,0,1*P,P,"t"),(2,1,1*P,P,"t"),(3,0,1*P,P,"t"),(3,1,1*P,P,"t")],[(2,0,2*P,P,"t"),(2,1,2*P,P,"t"),(3,0,2*P,P,"t"),(3,1,2*P,P,"t")],[(2,0,3*P,P,"t"),(2,1,3*P,P,"t"),(3,0,3*P,P,"t"),(3,1,3*P,P,"t")]]
-UNITS = [[(0, t, a, 0, S, FIRST_WAYS[t][a])] for t in range(PACK) for a in range(2)] + [[(1,) + piece for piece in unit] for unit in SECOND]
-AHEAD = 3
-LISTS = [("p1", "p2"), ("q1", "q2")]
-GATHER_TILES = 3
-LAGS = [3,3,2,2,3,3,3,3,3,3,3,3,2,2,2,2]
-DIFFERENCE_BANKS = 3
-LATE_PRODUCT = 0
-W2_AT = 0
-WEAVE = "ggvv"
-EMPTY = ["s","s","sv","sv"]
-GAIN_ON = "ssss"
-SPLIT_LAST = 0
-VWAIT = 1
-PLAIN = 1
-SWAP = 0
-SPLIT_BACK = 0
-WIDE = 2
-EARLY_STATE = {}
-Y_BANKS = [3, 4, 5, 6, 7]
-EARLY_Q = 1
-Z_POOL = [0]
-QUANT_AT = [-1,114,115,-1]
-CODE_TAG = ["","pull_14","pull_15",""]
-REUSE = {15:[(0,0),(1,0),(2,0),(3,0)]}
-TAKE = 1
-GAIN_TILE = [-1,-1,6,9]
-W2_TAG = "state_2"
-W2Q_AT = 9
-PRODUCT_AT = [114,115,115,115]
-OUT_RING = "ssss"
-
-BLOCKS = [(0,P),(P,P),(HALF,P),(HALF+P,P)]
-
-
-def advance(ring):
-    ring.append(ring.pop(0))
-    return ring[-1]
+BLOCKS = S // P
+RING = 3
+CAST_SPLIT = 8
 
 
 def tile_picked_coupled_none_p_kernel(tc, x_words, x_scales, w1, gn, w2, offs, p1, p2, q1, q2, out):
@@ -73,329 +35,216 @@ def tile_picked_coupled_none_p_kernel(tc, x_words, x_scales, w1, gn, w2, offs, p
         psum = ctx.enter_context(tc.psum_pool(name="psum", bufs=1))
 
         banks = [psum.tile([P, BANK], F32, name="bank_%d" % b) for b in range(8)]
-        difference_banks = banks[:DIFFERENCE_BANKS]
-        sum_banks = banks[DIFFERENCE_BANKS:]
         lists = {name: keep.tile([P, S // 16], U16, name="list_" + name) for name in ("offs", "p1", "p2", "q1", "q2")}
+        step_lists = [(lists["p1"], lists["p2"]), (lists["q1"], lists["q2"])]
 
         x_bytes = keep.tile([P, T], U8, name="x_bytes", align_bytes=64)
         x_packed = keep.tile([P, T], I32, name="x_packed", tag="x_packed", align_bytes=64)
-        w_raw = keep.tile([P, PACK, H], F32, name="w_raw", align_bytes=64)
+        w1_raw = keep.tile([P, PACK, H], F32, name="w1_raw", align_bytes=64)
+        w2_raw = keep.tile([P, PACK, N], F32, name="w2_raw", align_bytes=64)
         gain = keep.tile([P, PACK], F32, name="gain")
-        half_gain = keep.tile([P, PACK], F32, name="half_gain")
         ident = keep.tile([P, P], F32, name="ident", align_bytes=64)
 
         nc.vector.memset(x_bytes[:].bitcast(I32), 0)
-        nc.sync.dma_start(out=w_raw[:], in_=w1.rearrange("(p j) c -> p j c", j=PACK))
+        nc.sync.dma_start(out=w1_raw[:], in_=w1.rearrange("(p j) c -> p j c", j=PACK))
         nc.sync.dma_start(out=lists["offs"][:], in_=offs)
         for q in range(4):
             nc.sync.dma_start(out=x_bytes[32 * q : 32 * q + 4, :].bitcast(I32), in_=x_scales[0, 4 * q : 4 * q + 4, :].bitcast(I32))
+        nc.sync.dma_start(out=gain[:], in_=gn.rearrange("(p j) o -> p (j o)", j=PACK))
         nc.sync.dma_start(out=x_packed[:], in_=x_words[0].rearrange("p n t -> p (n t)").bitcast(I32))
         nc.sync.dma_start(out=lists["p1"][:], in_=p1)
         nc.sync.dma_start(out=lists["p2"][:], in_=p2)
-        nc.sync.dma_start(out=gain[:], in_=gn.rearrange("(p t) o -> p (t o)", t=PACK))
         nc.sync.dma_start(out=lists["q1"][:], in_=q1)
         nc.sync.dma_start(out=lists["q2"][:], in_=q2)
+        nc.sync.dma_start(out=w2_raw[:], in_=w2.rearrange("(p j) c -> p j c", j=PACK))
 
         make_identity(nc, ident[:])
-
-        state = []
+        window = []
         for t in range(PACK):
-            window = keep.tile([P, 2 * S], F32, name="state_%d" % t, tag="state_%d" % t, align_bytes=64)
-            nc.gpsimd.memset(window[:, S:], 0.0)
-            state.append(window)
-
-        picked_bytes = keep.tile([P, S], U8, name="picked_bytes", align_bytes=64)
-        picked_words = keep.tile([P, S], U32, name="picked_words", align_bytes=64)
-        nc.vector.tensor_copy(out=picked_bytes[:], in_=x_bytes[:].indirect(lists["offs"][:]))
-
-        w1_view = w_raw[:].rearrange("p j (m t) -> p t m j", t=PACK)
-        w1_grouped = [keep.tile([P, P, PACK], BF16, name="w1_grouped_%d" % t, align_bytes=64) for t in range(PACK)]
-        if EARLY_Q:
-            late_grouped = keep.tile([P, 2, P, PACK], BF16, name="late_grouped", align_bytes=64)
-            w1_grouped[2:] = [late_grouped[:, 0], late_grouped[:, 1]]
-        nc.vector.tensor_copy(out=w1_grouped[0][:], in_=w1_view[:, 0])
-        for t in range(1, PACK):
-            nc.scalar.copy(out=w1_grouped[t][:], in_=w1_view[:, t])
-        w1_codes = [keep.tile([P, P], U32, name="w1_codes_%d" % t, align_bytes=64) for t in range(2)] * 2
-        w1_scales = [keep.tile([P, P], U8, name="w1_scales_%d" % t, align_bytes=64) for t in range(2)] * 2
-
-        def quantize_w1(t):
-            nc.vector.quantize_mx(out=w1_codes[t][:].bitcast(FP8X4), scales=w1_scales[t][:], in_=w1_grouped[t][:].rearrange("p m j -> p (m j)"))
-
-        for t in range(2):
-            quantize_w1(t)
-
-        for n0 in (0, HALF):
-            nc.vector.tensor_copy(out=picked_words[:, n0 : n0 + HALF],
-                                  in_=x_packed[:].bitcast(U32).indirect(lists["offs"][:, n0 // 16 : (n0 + HALF) // 16]))
-
-        if EARLY_Q:
-            late_codes = keep.tile([P, 2 * P], U32, name="late_codes", tag="x_packed", align_bytes=64)
-            late_scales = keep.tile([P, 2 * P], U8, name="late_scales", align_bytes=64)
-            nc.vector.quantize_mx(out=late_codes[:].bitcast(FP8X4), scales=late_scales[:], in_=late_grouped[:].rearrange("p t m j -> p (t m j)"))
-            w1_codes[2:] = [late_codes[:, :P], late_codes[:, P:]]
-            w1_scales[2:] = [late_scales[:, :P], late_scales[:, P:]]
-
-        minus = [keep.tile([P, S], F32, name="minus_%d" % t, align_bytes=64) for t in range(PACK)]
-
-        def first_product(t, n0, width):
-            if t >= 2 and not EARLY_Q:
-                quantize_w1(t)
-            acc = banks[Y_BANKS[t + 1 if t or n0 else 0]]
-            nc.tensor.matmul_mx(out=acc[:, :width], lhsT=w1_codes[t][:].bitcast(FP8X4), lhsT_scale=w1_scales[t][:],
-                                rhs=picked_words[:, n0 : n0 + width].bitcast(FP8X4), rhs_scale=picked_bytes[:, n0 : n0 + width],
-                                start=True, stop=True)
-            if n0 > 0:
-                nc.vector.tensor_scalar(out=state[t][:, n0 : n0 + width], in0=acc[:, :width], scalar1=2.0, scalar2=0.0, op0=MULT, op1=ADD)
-            else:
-                nc.scalar.activation(out=state[t][:, n0 : n0 + width], in_=acc[:, :width], func=COPY, scale=2.0)
-            if PLAIN and FIRST_WAYS[t] != "pp":
-                nc.scalar.activation(out=minus[t][:, n0 : n0 + width], in_=acc[:, :width], func=COPY, scale=-2.0)
-
-        for t, n0, width in [(0, 0, HALF), (0, HALF, HALF), (1, 0, S)]:
-            first_product(t, n0, width)
+            tile = keep.tile([P, 2 * S], F32, name="window_%d" % t, tag="window_%d" % t, align_bytes=64)
+            nc.gpsimd.memset(tile[:, S:], 0.0)
+            window.append(tile)
+        plain = [keep.tile([P, S], F32, name="plain_%d" % t, align_bytes=64) for t in range(PACK)]
 
         def turn(dst, src, start, stop):
             nc.tensor.matmul(dst, lhsT=src, rhs=ident[:], start=start, stop=stop, is_transpose=True)
 
-        nc.sync.dma_start(out=w_raw[:], in_=w2.rearrange("(p j) c -> p j c", j=PACK))
-        w2_grouped = keep.tile([P, N, PACK], BF16, name="w2_grouped", align_bytes=64)
-        w2_codes = keep.tile([P, N], U32, name="w2_codes", tag=W2_TAG, align_bytes=64)
-        w2_scales = keep.tile([P, N], U8, name="w2_scales", align_bytes=64)
-        w2_view = w_raw[:].rearrange("p j c -> p c j")
+        def turn_blocks(bank, src, start, stop):
+            for b in range(BLOCKS):
+                cols = slice(b * P, (b + 1) * P)
+                turn(bank[:, cols], src[:, cols], start and b == 0, stop and b == BLOCKS - 1)
+
+        half_gain = keep.tile([P, PACK], F32, name="half_gain")
+        gain_rows = keep.tile([P, PACK, P], F32, name="gain_rows", align_bytes=64)
         nc.gpsimd.tensor_scalar(out=half_gain[:], in0=gain[:], scalar1=0.5, scalar2=0.0, op0=MULT, op1=ADD)
-        h = state[:WIDE] + [keep.tile([P, S], F32, name="h_%d" % t, align_bytes=64) for t in range(WIDE, PACK)]
-        states = [state, h]
-        plain = [keep.tile([P, S], F32, name="plain_%d" % t, align_bytes=64) for t in range(PACK)]
-        base_tiles = [keep.tile([P, S], F32, name="base_%d" % t, align_bytes=64) for t in range(PACK)]
-        z_planes = keep.tile([P, S // P, PACK, P], BF16, name="z_planes", align_bytes=64)
-        ring = [keep.tile([P, BANK], F32, name="gathered_%d" % r, align_bytes=64) for r in range(AHEAD)]
-        pulls = [keep.tile([P, BANK], F32, name="pull_%d" % r, tag="pull_%d" % r, align_bytes=64) for r in range(len(UNITS))]
-        gain_tiles = [pulls[GAIN_TILE[t]] if GAIN_TILE[t] >= 0 else base_tiles[t] for t in range(PACK)]
-        done = [set() for b in range(S // P)]
-        terms = {}
-        quantized = {}
-        woven = {}
-        begun = {}
-        opened = {}
+        for j in range(PACK):
+            turn(banks[7][:, j * P : (j + 1) * P], half_gain[:, j : j + 1].to_broadcast([P, P]), j == 0, j == PACK - 1)
+        spread = banks[7][:].rearrange("n (l e b h c) -> n h l b c e", l=2, e=2, h=2, c=4)
+        for h in range(2):
+            nc.scalar.copy(out=gain_rows[:, 2 * h : 2 * h + 2].rearrange("n l (b c e) -> n l b c e", c=4, e=2), in_=spread[:, h])
+
+        picked_bytes = keep.tile([P, S], U8, name="picked_bytes", align_bytes=64)
+        nc.vector.tensor_copy(out=picked_bytes[:], in_=x_bytes[:].indirect(lists["offs"][:]))
+
+        w1_grouped = keep.tile([P, H * PACK], BF16, name="w1_grouped", tag="picked_words", align_bytes=64)
+        source = w1_raw[:].rearrange("p j (b g l e) -> p l b g e j", g=8, l=2, e=2)
+        target = w1_grouped[:].rearrange("p (h l b r) -> p l b h r", h=2, l=2, b=16)
+        nc.vector.tensor_copy(out=target[:, 0, :CAST_SPLIT], in_=source[:, 0, :CAST_SPLIT])
+        nc.gpsimd.tensor_scalar(out=target[:, 0, CAST_SPLIT:], in0=source[:, 0, CAST_SPLIT:].rearrange("p b g e j -> p (b g) e j"),
+                                scalar1=1.0, scalar2=0.0, op0=MULT, op1=ADD)
+        nc.scalar.copy(out=target[:, 1], in_=source[:, 1])
+        w1_codes = keep.tile([P, H], U32, name="w1_codes", align_bytes=64)
+        w1_scales = keep.tile([P, H], U8, name="w1_scales", align_bytes=64)
+        nc.vector.quantize_mx(out=w1_codes[:].bitcast(FP8X4), scales=w1_scales[:], in_=w1_grouped[:])
+        picked_words = keep.tile([P, S], U32, name="picked_words", tag="picked_words", align_bytes=64)
+        for n0 in (0, HALF):
+            nc.vector.tensor_copy(out=picked_words[:, n0 : n0 + HALF],
+                                  in_=x_packed[:].bitcast(U32).indirect(lists["offs"][:, n0 // 16 : (n0 + HALF) // 16]))
+
+        def first_product(acc, t, n0, width):
+            nc.tensor.matmul_mx(out=acc[:, :width], lhsT=w1_codes[:, t * P : (t + 1) * P].bitcast(FP8X4), lhsT_scale=w1_scales[:, t * P : (t + 1) * P],
+                                rhs=picked_words[:, n0 : n0 + width].bitcast(FP8X4), rhs_scale=picked_bytes[:, n0 : n0 + width],
+                                start=True, stop=True)
+
+        sum_banks = [banks[5], banks[6]] * 2
+        back_banks = [banks[0], banks[1]] * 2
+        z_banks = [banks[5], banks[6], banks[1]]
+        block_banks = [banks[0], banks[2], banks[3], banks[4]]
+        word_banks = [banks[7], banks[5], banks[6], banks[1]]
+        ring = [keep.tile([P, S], F32, name="ring_%d" % r, align_bytes=64) for r in range(RING)]
+        pair = keep.tile([P, 2 * S], F32, name="pair", align_bytes=64)
+        turned_h = [pair[:, :S], pair[:, S:]] * 2
+        tile_b = keep.tile([P, S], F32, name="tile_b", align_bytes=64)
+        tile_c = keep.tile([P, S], F32, name="tile_c", align_bytes=64)
+        pulls = [tile_b[:] if u % 2 else (turned_h[u // 2 % 2] if u < 12 else tile_c[:]) for u in range(16)]
+        z_turned = keep.tile([P, BLOCKS * H], BF16, name="z_turned", align_bytes=64)
+
+        def fused(u, n0=0, width=S):
+            step, t, a = u // 8, u // 2 % PACK, u % 2
+            nc.vector.tensor_tensor(out=ring[u % RING][:, n0 : n0 + width],
+                                    in0=window[t][:].indirect(step_lists[step][a][:, n0 // 16 : (n0 + width) // 16]),
+                                    in1=plain[t][:, n0 : n0 + width], op=SUBTRACT)
+
+        def tanh(u):
+            nc.scalar.activation(out=pulls[u], in_=ring[u % RING][:], func=TANH, scale=0.5)
+
+        def double(target, acc):
+            nc.scalar.activation(out=target, in_=acc, func=COPY, scale=2.0)
+
+        def open_sum(t):
+            turn_blocks(sum_banks[t], plain[t] if t < 2 else window[t], True, False)
+
+        def unit(u):
+            fused(u)
+            tanh(u)
+            if u >= 8 and u % 2 == 0:
+                turn_blocks(z_banks[u // 2 - 4], window[u // 2 - 4], True, False)
+            turn_blocks(sum_banks[u // 2] if u < 8 else z_banks[u // 2 - 4], pulls[u], False, u % 2 == 1)
+
+        def leave(t):
+            nc.scalar.copy(out=turned_h[t], in_=sum_banks[t][:])
+            turn_blocks(back_banks[t], turned_h[t], True, True)
+
+        def close(t):
+            nc.scalar.copy(out=window[t][:, :S], in_=back_banks[t][:])
+            if t:
+                nc.sync.dma_start(out=plain[t][:], in_=window[t][:, :S])
+
+        def round_z(t, b0, count, source):
+            h, l = divmod(t, 2)
+            target = z_turned[:].rearrange("n (a l b h r) -> n l h a b r", l=2, b=16, h=2, r=8)[:, l, h, b0 : b0 + count]
+            nc.vector.tensor_tensor(out=target, in0=source.rearrange("n (a b r) -> n a b r", b=16, r=8),
+                                    in1=gain_rows[:, t].rearrange("n (b r) -> n b r", r=8).unsqueeze(1).to_broadcast([P, count, 16, 8]), op=MULT)
+
+        first_product(banks[0], 0, 0, HALF)
+        double(window[0][:, :HALF], banks[0][:, :HALF])
+        double(plain[0][:, :HALF], banks[0][:, :HALF])
+        first_product(banks[1], 0, HALF, HALF)
+        nc.vector.tensor_scalar(out=window[0][:, HALF:S], in0=banks[1][:, :HALF], scalar1=2.0, scalar2=0.0, op0=MULT, op1=ADD)
+        double(plain[0][:, HALF:], banks[1][:, :HALF])
+        for t in range(1, PACK):
+            first_product(banks[t + 1], t, 0, S)
+        double(window[1][:, :S], banks[2][:])
+        double(window[2][:, :S], banks[3][:])
+        nc.sync.dma_start(out=plain[2][:], in_=window[2][:, :S])
+        double(plain[1][:], banks[2][:])
+        open_sum(0)
+        fused(0, 0, HALF)
+        fused(0, HALF, HALF)
+        tanh(0)
+        turn_blocks(sum_banks[0], pulls[0], False, False)
+        double(window[3][:, :S], banks[4][:])
+        nc.sync.dma_start(out=plain[3][:], in_=window[3][:, :S])
+        unit(1)
+
+        w2_grouped = pair[:].bitcast(BF16)
+        w2_view = w2_raw[:].rearrange("p j c -> p c j")
+        for u in range(2, 14):
+            if u < 8 and u % 2 == 0:
+                open_sum(u // 2)
+            if u == 8:
+                nc.vector.tensor_copy(out=plain[0][:], in_=window[0][:, :S])
+            unit(u)
+            if u < 10:
+                (close if u % 2 else leave)(u // 2 - 1)
+            if u in (9, 10):
+                for c in (2 * u - 18, 2 * u - 17):
+                    nc.scalar.copy(out=w2_grouped[:, c * S : (c + 1) * S].rearrange("p (c j) -> p c j", j=PACK), in_=w2_view[:, c * P : (c + 1) * P, :])
+            if u in (10, 12):
+                round_z(u // 2 - 5, 0, BLOCKS, z_banks[u // 2 - 5][:])
+
+        for b in range(BLOCKS):
+            turn(block_banks[b][:, :P], window[3][:, b * P : (b + 1) * P], True, False)
+        for half in range(2):
+            work = ring[(14 + half) % RING]
+            n0 = half * HALF
+            for a in range(2):
+                nc.vector.tensor_tensor(out=work[:, a * HALF : (a + 1) * HALF],
+                                        in0=window[3][:].indirect(step_lists[1][a][:, n0 // 16 : (n0 + HALF) // 16]),
+                                        in1=plain[3][:, n0 : n0 + HALF], op=SUBTRACT)
+            tanh(14 + half)
+        round_z(2, 0, BLOCKS, z_banks[2][:])
+        w2_codes = keep.tile([P, N], U32, name="w2_codes", tag="window_3", align_bytes=64)
+        w2_scales = keep.tile([P, N], U8, name="w2_scales", align_bytes=64)
+        nc.vector.quantize_mx(out=w2_codes[:].bitcast(FP8X4), scales=w2_scales[:], in_=w2_grouped)
+
         out_view = out.rearrange("(b p) n -> p b n", p=P)
+        z_grouped = [keep.tile([P, P * PACK], BF16, name="z_grouped_%d" % b, align_bytes=64) for b in range(BLOCKS)]
 
-        def pull(u):
-            v = u - AHEAD
-            if v >= 0 and UNITS[v][0][5] == "p" and SWAP:
-                ring[u % AHEAD] = pulls[v - 1] if v > 0 else keep.tile([P, BANK], F32, name="gathered_spare", align_bytes=64)
-            work = ring[u % AHEAD]
-            turned = []
-            c0 = 0
-            for step, t, a, n0, width, way in UNITS[u]:
-                window = states[step][t]
-                picked = window[:].indirect(lists[LISTS[step][a]][:, n0 // 16 : (n0 + width) // 16])
-                cols = slice(c0, c0 + width)
-                result = pulls[u][:, cols]
-                spot = work[:, cols]
-                if u in REUSE and REUSE[u][c0 // width]:
-                    owner, first = REUSE[u][c0 // width]
-                    if isinstance(owner, str):
-                        spot = keep.tile([P, S], F32, name="after_" + owner, tag=owner, align_bytes=64)[:, first : first + width]
-                    else:
-                        spot = (gain_tiles + base_tiles)[owner][:, first : first + width]
-                if way == "v":
-                    result = spot
-                    nc.vector.tensor_tensor(out=result, in0=picked, in1=plain[t][:, n0 : n0 + width], op=SUBTRACT)
-                    nc.scalar.activation(out=result, in_=result, func=TANH, scale=0.5)
-                elif PLAIN and (step == 0 or way == "p"):
-                    nc.vector.tensor_copy(out=spot, in_=picked)
-                else:
-                    nc.vector.tensor_scalar(out=spot, in0=picked, scalar1=-1.0, scalar2=0.0, op0=MULT, op1=ADD)
-                if way == "p":
-                    result = pulls[u - 3][:, cols]
-                    nc.gpsimd.tensor_tensor(out=result, in0=spot, in1=window[:, n0 : n0 + width], op=SUBTRACT if PLAIN else ADD)
-                    nc.scalar.activation(out=result, in_=result, func=TANH, scale=0.5 if PLAIN else -0.5)
-                if way in "tg":
-                    turned.extend([(c0 + c, window[:, n0 + c : n0 + c + P], spot[:, c : c + P]) for c in range(0, width, P)])
-                terms[step, t, a, n0] = (way, result)
-                c0 = c0 + width
-            parts = [turned[:2], turned[2:]] if SPLIT_LAST and u == len(UNITS) - 1 else [turned]
-            for v in [u] + EARLY_STATE.get(u, []):
-                open_difference(v)
-            for part in parts:
-                if part:
-                    difference = opened[u, part[0][0]]
-                    for c, own, other in part:
-                        turn(difference[:, c : c + P], other, False, c == part[-1][0])
-                    cols = slice(part[0][0], part[-1][0] + P)
-                    nc.scalar.activation(out=pulls[u][:, cols], in_=difference[:, cols], func=TANH, scale=0.5 if PLAIN and u < 2 * PACK else -0.5)
+        def last_plane(b):
+            for a in range(2):
+                c0 = a * HALF + b % 2 * P
+                turn(block_banks[b][:, :P], pulls[14 + b // 2][:, c0 : c0 + P], False, a == 1)
+            round_z(3, b, 1, block_banks[b][:, :P])
 
-        def open_difference(u):
-            if u in opened:
-                return
-            opened[u] = True
-            turned = []
-            c0 = 0
-            for step, t, a, n0, width, way in UNITS[u]:
-                if way in "tg":
-                    turned.extend([(c0 + c, (minus if PLAIN and step == 0 else states[step])[t][:, n0 + c : n0 + c + P]) for c in range(0, width, P)])
-                c0 = c0 + width
-            parts = [turned[:2], turned[2:]] if SPLIT_LAST and u == len(UNITS) - 1 else [turned]
-            for part in parts:
-                if part:
-                    difference = advance(difference_banks)
-                    opened[u, part[0][0]] = difference
-                    for c, own in part:
-                        turn(difference[:, c : c + P], own, c == part[0][0], False)
+        def turn_back(b):
+            words = z_turned[:, b * H : (b + 1) * H].bitcast(F32)
+            for u in range(2):
+                turn(word_banks[b][:, u * P : (u + 1) * P], words[:, u * P : (u + 1) * P], True, True)
+            nc.scalar.copy(out=z_grouped[b][:].bitcast(F32).rearrange("p (n u) -> p n u", u=2),
+                           in_=word_banks[b][:, : 2 * P].rearrange("p (u n) -> p n u", u=2))
 
-        def gained(t):
-            plainly = [(n1, count) for unit in SECOND for t1, a1, n1, count, ways in unit if t1 == t and a1 == 0 and "p" not in ways]
-            if plainly:
-                lo = min(n1 for n1, count in plainly)
-                hi = max(n1 + count for n1, count in plainly)
-                target = gain_tiles[t]
-                if GAIN_ON[t] == "s":
-                    nc.scalar.activation(out=target[:, lo:hi], in_=h[t][:, lo:hi], func=COPY, scale=half_gain[:, t : t + 1])
-                else:
-                    nc.gpsimd.tensor_scalar(out=target[:, lo:hi], in0=h[t][:, lo:hi], scalar1=half_gain[:, t : t + 1], scalar2=0.0, op0=MULT, op1=ADD)
-
-        def close(u):
-            closing_work(u)
-            for t in range(PACK):
-                if GAIN_TILE[t] | 1 == u and GAIN_TILE[t] >= 0:
-                    gained(t)
-
-        def closing_work(u):
-            closing = [(step, t, n0, width) for step, t, a, n0, width, way in UNITS[u] if a == 1]
-            passes = []
-            plans = []
-            c0 = 0
-            for step, t, n0, width in closing:
-                pair = [terms[step, t, a, n0] for a in range(2)]
-                base = states[step][t][:, n0 : n0 + width]
-                for way, term in pair:
-                    if way == "p":
-                        nc.gpsimd.tensor_tensor(out=base_tiles[t][:, n0 : n0 + width], in0=term, in1=base, op=ADD)
-                        base = base_tiles[t][:, n0 : n0 + width]
-                turned = [term for way, term in pair if way == "t"]
-                if pair[0][0] == "g":
-                    nc.gpsimd.tensor_tensor(out=pair[0][1], in0=pair[0][1], in1=pair[1][1], op=ADD)
-                    turned = [pair[0][1]]
-                passes.extend([(c0 + c, term[:, c : c + P]) for term in (turned[1:] if u - 1 in begun else turned) for c in range(0, width, P)])
-                plans.append((step, t, n0, width, pair, base, turned, c0))
-                c0 = c0 + width
-            if not closing and UNITS[u][0][5] == "t" and UNITS[u + 1][0][5] == "t" and SPLIT_BACK:
-                begun[u] = advance(sum_banks)
-                for c in range(0, S, P):
-                    turn(begun[u][:, c : c + P], pulls[u][:, c : c + P], c == 0, False)
-            if passes:
-                total = begun[u - 1] if u - 1 in begun else advance(sum_banks)
-                for k, (c, block) in enumerate(passes):
-                    turn(total[:, c : c + P], block, k == 0 and u - 1 not in begun, k == len(passes) - 1)
-            for step, t, n0, width, pair, base, turned, c0 in plans:
-                rest = [term for way, term in pair if way == "v"]
-                if turned:
-                    rest = rest + [total[:, c0 : c0 + width]]
-                factor = half_gain[:, t : t + 1]
-                if step == 0:
-                    for k, term in enumerate(rest):
-                        target = h[t][:, :S] if k == len(rest) - 1 else base_tiles[t][:]
-                        if FIRST_FINAL[t] == "p" and k == len(rest) - 1:
-                            nc.scalar.copy(out=plain[t][:], in_=term)
-                            nc.gpsimd.tensor_tensor(out=target, in0=plain[t][:], in1=base, op=ADD)
-                        else:
-                            nc.vector.tensor_tensor(out=target, in0=term, in1=base, op=ADD)
-                        base = target
-                    later = [(n1, count, ways) for unit in SECOND for t1, a1, n1, count, ways in unit if t1 == t and a1 == 1]
-                    for n1, count, ways in later:
-                        if "v" in ways:
-                            nc.scalar.copy(out=plain[t][:, n1 : n1 + count], in_=h[t][:, n1 : n1 + count])
-                    if GAIN_TILE[t] < 0:
-                        gained(t)
-                    continue
-                if "p" in [way for way, term in pair]:
-                    nc.scalar.activation(out=base, in_=base, func=COPY, scale=factor)
-                else:
-                    base = gain_tiles[t][:, n0 : n0 + width]
-                for term in rest[:-1]:
-                    nc.vector.scalar_tensor_tensor(out=base, in0=term, scalar=factor, in1=base, op0=MULT, op1=ADD)
-                if t in Z_POOL:
-                    nc.scalar.activation(out=plain[t][:, :width], in_=rest[-1], func=COPY, scale=factor)
-                    nc.gpsimd.tensor_tensor(out=z_planes[:, n0 // P : (n0 + width) // P, t, :], in0=plain[t][:, :width].rearrange("p (a n) -> p a n", n=P),
-                                            in1=base.rearrange("p (a n) -> p a n", n=P), op=ADD)
-                else:
-                    nc.vector.scalar_tensor_tensor(out=z_planes[:, n0 // P : (n0 + width) // P, t, :], in0=rest[-1].rearrange("p (a n) -> p a n", n=P),
-                                               scalar=factor, in1=base.rearrange("p (a n) -> p a n", n=P), op0=MULT, op1=ADD)
-                for b in range(n0 // P, (n0 + width) // P):
-                    done[b].add(t)
-                for i, (first, count) in enumerate(BLOCKS):
-                    if n0 <= first < n0 + width and len(done[first // P]) == PACK:
-                        finish(i)
-
-        def finish(i):
-            n0, width = BLOCKS[i]
-            z_grouped = keep.tile([P, width, PACK], BF16, name="z_grouped_%d" % i, align_bytes=64)
-            source = z_planes[:, n0 // P : (n0 + width) // P].rearrange("p a t (c i) -> p a c t i", i=PACK)
-            target = z_grouped[:].rearrange("p (a c i) t -> p a c t i", c=P // PACK, i=PACK)
-            if WEAVE[i] == "v":
-                nc.vector.tensor_copy(out=target, in_=source)
-            elif WEAVE[i] == "g":
-                nc.gpsimd.tensor_scalar(out=z_grouped[:].rearrange("p (a n) t -> p a n t", n=P),
-                                        in0=z_planes[:, n0 // P : (n0 + width) // P].rearrange("p a t n -> p a n t"),
-                                        scalar1=1.0, scalar2=0.0, op0=MULT, op1=ADD)
-            else:
-                nc.scalar.copy(out=target, in_=source)
-            woven[i] = z_grouped
-            if QUANT_AT[i] < 0:
-                quantize_z(i)
-
-        def quantize_z(i):
-            n0, width = BLOCKS[i]
-            z_grouped = woven[i]
-            z_codes = keep.tile([P, width], U32, name="z_codes_%d" % i, tag=CODE_TAG[i] or "z_codes_%d" % i, align_bytes=64)
-            z_scales = keep.tile([P, width], U8, name="z_scales_%d" % i, align_bytes=64)
-            nc.vector.quantize_mx(out=z_codes[:].bitcast(FP8X4), scales=z_scales[:], in_=z_grouped[:].rearrange("p n t -> p (n t)"))
-            quantized[i] = (z_codes, z_scales)
-            if PRODUCT_AT[i] < 0:
-                multiply(i)
-
-        def multiply(i):
-            n0, width = BLOCKS[i]
-            z_codes, z_scales = quantized[i]
-            last = i == len(BLOCKS) - 1
-            per_bank = PACK // len(EMPTY[i])
-            for b0 in range(0, N // P, per_bank):
-                acc = advance(difference_banks if OUT_RING[i] == "d" else sum_banks)
-                for b in range(per_bank):
-                    rows = slice((b0 + b) * P, (b0 + b + 1) * P)
-                    nc.tensor.matmul_mx(out=acc[:, b * width : (b + 1) * width], lhsT=w2_codes[:, rows].bitcast(FP8X4), lhsT_scale=w2_scales[:, rows],
+        def finish(b):
+            z_codes = keep.tile([P, P], U32, name="z_codes_%d" % b, align_bytes=64)
+            z_scales = keep.tile([P, P], U8, name="z_scales_%d" % b, align_bytes=64)
+            nc.vector.quantize_mx(out=z_codes[:].bitcast(FP8X4), scales=z_scales[:], in_=z_grouped[b][:])
+            last = b == BLOCKS - 1
+            parts = [(block_banks[b], 0, 2), (banks[7], 2, 2)] if last else [(block_banks[b], 0, 4)]
+            for acc, r0, count in parts:
+                for r in range(count):
+                    rows = slice((r0 + r) * P, (r0 + r + 1) * P)
+                    nc.tensor.matmul_mx(out=acc[:, r * P : (r + 1) * P], lhsT=w2_codes[:, rows].bitcast(FP8X4), lhsT_scale=w2_scales[:, rows],
                                         rhs=z_codes[:].bitcast(FP8X4), rhs_scale=z_scales[:], start=True, stop=True)
-                result = keep.tile([P, per_bank, width], F32, name="result_%d_%d" % (i, b0), align_bytes=64)
-                if EMPTY[i][b0 // per_bank] == "v":
-                    nc.vector.tensor_copy(out=result[:].rearrange("p b n -> p (b n)"), in_=acc[:, : per_bank * width])
+                result = keep.tile([P, count, P], F32, name="result_%d_%d" % (b, r0), align_bytes=64)
+                if r0:
+                    nc.vector.tensor_copy(out=result[:].rearrange("p b n -> p (b n)"), in_=acc[:, : count * P])
                 else:
-                    nc.scalar.copy(out=result[:].rearrange("p b n -> p (b n)"), in_=acc[:, : per_bank * width])
-                queue = nc.scalar if last and b0 == 0 else nc.sync
-                queue.dma_start(out=out_view[:, b0 : b0 + per_bank, n0 : n0 + width], in_=result[:])
+                    nc.scalar.copy(out=result[:].rearrange("p b n -> p (b n)"), in_=acc[:, : count * P])
+                queue = nc.scalar if last and r0 == 0 else nc.sync
+                queue.dma_start(out=out_view[:, r0 : r0 + count, b * P : (b + 1) * P], in_=result[:])
 
-        closed = 0
-        for u in range(len(UNITS)):
-            while closed + LAGS[closed] <= u:
-                close(closed)
-                closed = closed + 1
-            if u == LATE_PRODUCT:
-                for t in (2, 3):
-                    first_product(t, 0, S)
-            pull(u)
-            for i in range(len(BLOCKS)):
-                if PRODUCT_AT[i] == u:
-                    multiply(i)
-            if W2_AT <= u < W2_AT + 2 * PACK and (u - W2_AT) % 2 == 1:
-                c = (u - W2_AT) // 2
-                nc.scalar.copy(out=w2_grouped[:, c * P : (c + 1) * P, :], in_=w2_view[:, c * P : (c + 1) * P, :])
-            if u == max(W2Q_AT, W2_AT + 2 * PACK - 1):
-                    nc.vector.quantize_mx(out=w2_codes[:].bitcast(FP8X4), scales=w2_scales[:], in_=w2_grouped[:].rearrange("p c j -> p (c j)"))
-        for u in range(closed, len(UNITS)):
-            close(u)
-            for i in range(len(BLOCKS)):
-                if QUANT_AT[i] == 100 + u:
-                    quantize_z(i)
-            for i in range(len(BLOCKS)):
-                if PRODUCT_AT[i] == 100 + u:
-                    multiply(i)
+        for b in range(BLOCKS):
+            last_plane(b)
+            turn_back(b)
+        for b in range(BLOCKS):
+            finish(b)

@@ -25,7 +25,7 @@ BANK = 512
 HALF = S // 2
 BLOCKS = S // P
 RING = 3
-CAST_SPLIT = 8
+W2_EARLY = 192
 
 
 def tile_picked_coupled_none_p_kernel(tc, x_words, x_scales, w1, gn, w2, offs, p1, p2, q1, q2, out):
@@ -41,7 +41,7 @@ def tile_picked_coupled_none_p_kernel(tc, x_words, x_scales, w1, gn, w2, offs, p
         x_bytes = keep.tile([P, T], U8, name="x_bytes", align_bytes=64)
         x_packed = keep.tile([P, T], I32, name="x_packed", tag="x_packed", align_bytes=64)
         w1_raw = keep.tile([P, PACK, H], F32, name="w1_raw", align_bytes=64)
-        w2_raw = keep.tile([P, PACK, N], F32, name="w2_raw", align_bytes=64)
+        w2_raw = [keep.tile([P, PACK, width], F32, name="w2_raw_%d" % width, align_bytes=64) for width in (W2_EARLY, N - W2_EARLY)]
         gain = keep.tile([P, PACK], F32, name="gain")
         ident = keep.tile([P, P], F32, name="ident", align_bytes=64)
 
@@ -54,9 +54,11 @@ def tile_picked_coupled_none_p_kernel(tc, x_words, x_scales, w1, gn, w2, offs, p
         nc.sync.dma_start(out=x_packed[:], in_=x_words[0].rearrange("p n t -> p (n t)").bitcast(I32))
         nc.sync.dma_start(out=lists["p1"][:], in_=p1)
         nc.sync.dma_start(out=lists["p2"][:], in_=p2)
+        w2_view = w2.rearrange("(p j) c -> p j c", j=PACK)
+        nc.sync.dma_start(out=w2_raw[0][:], in_=w2_view[:, :, :W2_EARLY])
+        nc.sync.dma_start(out=w2_raw[1][:], in_=w2_view[:, :, W2_EARLY:])
         nc.sync.dma_start(out=lists["q1"][:], in_=q1)
         nc.sync.dma_start(out=lists["q2"][:], in_=q2)
-        nc.sync.dma_start(out=w2_raw[:], in_=w2.rearrange("(p j) c -> p j c", j=PACK))
 
         make_identity(nc, ident[:])
         window = []
@@ -79,27 +81,26 @@ def tile_picked_coupled_none_p_kernel(tc, x_words, x_scales, w1, gn, w2, offs, p
         nc.gpsimd.tensor_scalar(out=half_gain[:], in0=gain[:], scalar1=0.5, scalar2=0.0, op0=MULT, op1=ADD)
         for j in range(PACK):
             turn(banks[7][:, j * P : (j + 1) * P], half_gain[:, j : j + 1].to_broadcast([P, P]), j == 0, j == PACK - 1)
-        spread = banks[7][:].rearrange("n (l e b h c) -> n h l b c e", l=2, e=2, h=2, c=4)
-        for h in range(2):
-            nc.scalar.copy(out=gain_rows[:, 2 * h : 2 * h + 2].rearrange("n l (b c e) -> n l b c e", c=4, e=2), in_=spread[:, h])
+        spread = banks[7][:].rearrange("n (l e b h c) -> n l h b c e", l=2, e=2, h=2, c=4)
+        for l in range(2):
+            nc.scalar.copy(out=gain_rows[:, 2 * l : 2 * l + 2].rearrange("n h (b c e) -> n h b c e", c=4, e=2), in_=spread[:, l])
 
         picked_bytes = keep.tile([P, S], U8, name="picked_bytes", align_bytes=64)
         nc.vector.tensor_copy(out=picked_bytes[:], in_=x_bytes[:].indirect(lists["offs"][:]))
 
         w1_grouped = keep.tile([P, H * PACK], BF16, name="w1_grouped", tag="picked_words", align_bytes=64)
-        source = w1_raw[:].rearrange("p j (b g l e) -> p l b g e j", g=8, l=2, e=2)
-        target = w1_grouped[:].rearrange("p (h l b r) -> p l b h r", h=2, l=2, b=16)
-        nc.vector.tensor_copy(out=target[:, 0, :CAST_SPLIT], in_=source[:, 0, :CAST_SPLIT])
-        nc.gpsimd.tensor_scalar(out=target[:, 0, CAST_SPLIT:], in0=source[:, 0, CAST_SPLIT:].rearrange("p b g e j -> p (b g) e j"),
-                                scalar1=1.0, scalar2=0.0, op0=MULT, op1=ADD)
+        source = w1_raw[:].rearrange("p j (b h i) -> p h b i j", h=2, i=16)
+        target = w1_grouped[:].rearrange("p (l h b c r) -> p h b c l r", h=2, l=2, b=16, c=4)
+        nc.vector.tensor_copy(out=target[:, 0], in_=source[:, 0])
         nc.scalar.copy(out=target[:, 1], in_=source[:, 1])
         w1_codes = keep.tile([P, H], U32, name="w1_codes", align_bytes=64)
         w1_scales = keep.tile([P, H], U8, name="w1_scales", align_bytes=64)
         nc.vector.quantize_mx(out=w1_codes[:].bitcast(FP8X4), scales=w1_scales[:], in_=w1_grouped[:])
         picked_words = keep.tile([P, S], U32, name="picked_words", tag="picked_words", align_bytes=64)
-        for n0 in (0, HALF):
-            nc.vector.tensor_copy(out=picked_words[:, n0 : n0 + HALF],
-                                  in_=x_packed[:].bitcast(U32).indirect(lists["offs"][:, n0 // 16 : (n0 + HALF) // 16]))
+        pieces = [(0, HALF), (HALF, P), (HALF + P, P)]
+        for n0, width in pieces:
+            nc.vector.tensor_copy(out=picked_words[:, n0 : n0 + width],
+                                  in_=x_packed[:].bitcast(U32).indirect(lists["offs"][:, n0 // 16 : (n0 + width) // 16]))
 
         def first_product(acc, t, n0, width):
             nc.tensor.matmul_mx(out=acc[:, :width], lhsT=w1_codes[:, t * P : (t + 1) * P].bitcast(FP8X4), lhsT_scale=w1_scales[:, t * P : (t + 1) * P],
@@ -109,24 +110,24 @@ def tile_picked_coupled_none_p_kernel(tc, x_words, x_scales, w1, gn, w2, offs, p
         sum_banks = [banks[5], banks[6]] * 2
         back_banks = [banks[0], banks[1]] * 2
         z_banks = [banks[5], banks[6], banks[1]]
-        block_banks = [banks[0], banks[2], banks[3], banks[4]]
-        word_banks = [banks[7], banks[5], banks[6], banks[1]]
         ring = [keep.tile([P, S], F32, name="ring_%d" % r, align_bytes=64) for r in range(RING)]
-        pair = keep.tile([P, 2 * S], F32, name="pair", align_bytes=64)
-        turned_h = [pair[:, :S], pair[:, S:]] * 2
-        tile_b = keep.tile([P, S], F32, name="tile_b", align_bytes=64)
-        tile_c = keep.tile([P, S], F32, name="tile_c", align_bytes=64)
-        pulls = [tile_b[:] if u % 2 else (turned_h[u // 2 % 2] if u < 12 else tile_c[:]) for u in range(16)]
+        shared = keep.tile([P, 2 * S], F32, name="shared", align_bytes=64)
+        turned_h = shared[:, 2 * W2_EARLY : 2 * W2_EARLY + S]
+        w2_grouped = shared[:].bitcast(BF16)
+        pulls = [keep.tile([P, S], F32, name="pulls_%d" % a, tag="pulls_%d" % a, align_bytes=64) for a in range(2)]
+        h_window = window[:3] + [keep.tile([P, S], F32, name="last_window", tag="last_window", align_bytes=64)]
+        windows = [window, h_window]
         z_turned = keep.tile([P, BLOCKS * H], BF16, name="z_turned", align_bytes=64)
+        nc.gpsimd.tensor_scalar(out=w2_grouped[:, : PACK * W2_EARLY].rearrange("p (c j) -> p c j", j=PACK), in0=w2_raw[0][:].rearrange("p j c -> p c j"),
+                                scalar1=1.0, scalar2=0.0, op0=MULT, op1=ADD)
 
-        def fused(u, n0=0, width=S):
-            step, t, a = u // 8, u // 2 % PACK, u % 2
-            nc.vector.tensor_tensor(out=ring[u % RING][:, n0 : n0 + width],
-                                    in0=window[t][:].indirect(step_lists[step][a][:, n0 // 16 : (n0 + width) // 16]),
+        def fused(target, step, t, a, n0, width):
+            nc.vector.tensor_tensor(out=target,
+                                    in0=windows[step][t][:].indirect(step_lists[step][a][:, n0 // 16 : (n0 + width) // 16]),
                                     in1=plain[t][:, n0 : n0 + width], op=SUBTRACT)
 
-        def tanh(u):
-            nc.scalar.activation(out=pulls[u], in_=ring[u % RING][:], func=TANH, scale=0.5)
+        def tanh(target, source):
+            nc.scalar.activation(out=target, in_=source, func=TANH, scale=0.5)
 
         def double(target, acc):
             nc.scalar.activation(out=target, in_=acc, func=COPY, scale=2.0)
@@ -135,116 +136,139 @@ def tile_picked_coupled_none_p_kernel(tc, x_words, x_scales, w1, gn, w2, offs, p
             turn_blocks(sum_banks[t], plain[t] if t < 2 else window[t], True, False)
 
         def unit(u):
-            fused(u)
-            tanh(u)
+            fused(ring[u % RING][:], u // 8, u // 2 % PACK, u % 2, 0, S)
+            tanh(pulls[u % 2][:], ring[u % RING][:])
+            bank = sum_banks[u // 2] if u < 8 else z_banks[u // 2 - 4]
             if u >= 8 and u % 2 == 0:
-                turn_blocks(z_banks[u // 2 - 4], window[u // 2 - 4], True, False)
-            turn_blocks(sum_banks[u // 2] if u < 8 else z_banks[u // 2 - 4], pulls[u], False, u % 2 == 1)
+                turn_blocks(bank, window[u // 2 - 4], True, False)
+            turn_blocks(bank, pulls[u % 2], False, u % 2 == 1)
+
+        def open_part(t, b0, count, bank):
+            for b in range(count):
+                turn(bank[:, b * P : (b + 1) * P], h_window[t][:, (b0 + b) * P : (b0 + b + 1) * P], b == 0, False)
+
+        def part_unit(t, which, b0, count, bank, work, result):
+            width = count * P
+            for i, a in enumerate(which):
+                fused(work[:, i * width : (i + 1) * width], 1, t, a, b0 * P, width)
+            tanh(result, work)
+            for c in range(len(which) * count):
+                b = c % count
+                turn(bank[:, b * P : (b + 1) * P], result[:, c * P : (c + 1) * P], False, which[-1] == 1 and c == len(which) * count - 1)
 
         def leave(t):
-            nc.scalar.copy(out=turned_h[t], in_=sum_banks[t][:])
-            turn_blocks(back_banks[t], turned_h[t], True, True)
+            nc.scalar.copy(out=turned_h, in_=sum_banks[t][:])
+            turn_blocks(back_banks[t], turned_h, True, True)
 
         def close(t):
-            nc.scalar.copy(out=window[t][:, :S], in_=back_banks[t][:])
+            nc.scalar.copy(out=h_window[t][:, :S], in_=back_banks[t][:])
             if t:
-                nc.sync.dma_start(out=plain[t][:], in_=window[t][:, :S])
+                nc.sync.dma_start(out=plain[t][:], in_=h_window[t][:, :S])
 
-        def round_z(t, b0, count, source):
-            h, l = divmod(t, 2)
+        def round_z(t, b0, count, bank):
+            l, h = divmod(t, 2)
             target = z_turned[:].rearrange("n (a l b h r) -> n l h a b r", l=2, b=16, h=2, r=8)[:, l, h, b0 : b0 + count]
-            nc.vector.tensor_tensor(out=target, in0=source.rearrange("n (a b r) -> n a b r", b=16, r=8),
+            nc.vector.tensor_tensor(out=target, in0=bank[:, : count * P].rearrange("n (a b r) -> n a b r", b=16, r=8),
                                     in1=gain_rows[:, t].rearrange("n (b r) -> n b r", r=8).unsqueeze(1).to_broadcast([P, count, 16, 8]), op=MULT)
 
-        first_product(banks[0], 0, 0, HALF)
+        first_banks = [banks[0], banks[1], banks[6]]
+        for (n0, width), acc in zip(pieces, first_banks):
+            first_product(acc, 0, n0, width)
         double(window[0][:, :HALF], banks[0][:, :HALF])
-        double(plain[0][:, :HALF], banks[0][:, :HALF])
-        first_product(banks[1], 0, HALF, HALF)
-        nc.vector.tensor_scalar(out=window[0][:, HALF:S], in0=banks[1][:, :HALF], scalar1=2.0, scalar2=0.0, op0=MULT, op1=ADD)
-        double(plain[0][:, HALF:], banks[1][:, :HALF])
+        for (n0, width), acc in zip(pieces[1:], first_banks[1:]):
+            nc.vector.tensor_scalar(out=window[0][:, n0 : n0 + width], in0=acc[:, :width], scalar1=2.0, scalar2=0.0, op0=MULT, op1=ADD)
+        for (n0, width), acc in zip(pieces, first_banks):
+            double(plain[0][:, n0 : n0 + width], acc[:, :width])
         for t in range(1, PACK):
             first_product(banks[t + 1], t, 0, S)
         double(window[1][:, :S], banks[2][:])
         double(window[2][:, :S], banks[3][:])
         nc.sync.dma_start(out=plain[2][:], in_=window[2][:, :S])
         double(plain[1][:], banks[2][:])
-        open_sum(0)
-        fused(0, 0, HALF)
-        fused(0, HALF, HALF)
-        tanh(0)
-        turn_blocks(sum_banks[0], pulls[0], False, False)
         double(window[3][:, :S], banks[4][:])
         nc.sync.dma_start(out=plain[3][:], in_=window[3][:, :S])
-        unit(1)
+        open_sum(0)
+        for n0 in (0, HALF):
+            for a in range(2):
+                fused(ring[a][:, n0 : n0 + HALF], 0, 0, a, n0, HALF)
+        for a in range(2):
+            tanh(pulls[a][:], ring[a][:])
+            turn_blocks(sum_banks[0], pulls[a], False, a == 1)
 
-        w2_grouped = pair[:].bitcast(BF16)
-        w2_view = w2_raw[:].rearrange("p j c -> p c j")
+        word_banks = [banks[7], banks[5], banks[6], banks[0]]
+
+        def turn_words(b, u):
+            words = z_turned[:, b * H : (b + 1) * H].bitcast(F32)
+            turn(word_banks[b][:, u * P : (u + 1) * P], words[:, u * P : (u + 1) * P], True, True)
+
         for u in range(2, 14):
             if u < 8 and u % 2 == 0:
                 open_sum(u // 2)
-            if u == 8:
+            if u == 7:
                 nc.vector.tensor_copy(out=plain[0][:], in_=window[0][:, :S])
             unit(u)
-            if u < 10:
-                (close if u % 2 else leave)(u // 2 - 1)
-            if u in (9, 10):
-                for c in (2 * u - 18, 2 * u - 17):
-                    nc.scalar.copy(out=w2_grouped[:, c * S : (c + 1) * S].rearrange("p (c j) -> p c j", j=PACK), in_=w2_view[:, c * P : (c + 1) * P, :])
-            if u in (10, 12):
-                round_z(u // 2 - 5, 0, BLOCKS, z_banks[u // 2 - 5][:])
+            if u in (4, 6, 8, 10):
+                close(u // 2 - 2)
+            if u in (2, 4, 6, 8):
+                leave(u // 2 - 1)
+            if u in (10, 11):
+                width = (N - W2_EARLY) // 2
+                c0 = (u - 10) * width
+                nc.scalar.copy(out=w2_grouped[:, PACK * (W2_EARLY + c0) : PACK * (W2_EARLY + c0 + width)].rearrange("p (c j) -> p c j", j=PACK),
+                               in_=w2_raw[1][:, :, c0 : c0 + width].rearrange("p j c -> p c j"))
 
-        for b in range(BLOCKS):
-            turn(block_banks[b][:, :P], window[3][:, b * P : (b + 1) * P], True, False)
-        for half in range(2):
-            work = ring[(14 + half) % RING]
-            n0 = half * HALF
-            for a in range(2):
-                nc.vector.tensor_tensor(out=work[:, a * HALF : (a + 1) * HALF],
-                                        in0=window[3][:].indirect(step_lists[1][a][:, n0 // 16 : (n0 + HALF) // 16]),
-                                        in1=plain[3][:, n0 : n0 + HALF], op=SUBTRACT)
-            tanh(14 + half)
-        round_z(2, 0, BLOCKS, z_banks[2][:])
-        w2_codes = keep.tile([P, N], U32, name="w2_codes", tag="window_3", align_bytes=64)
-        w2_scales = keep.tile([P, N], U8, name="w2_scales", align_bytes=64)
-        nc.vector.quantize_mx(out=w2_codes[:].bitcast(FP8X4), scales=w2_scales[:], in_=w2_grouped)
+            if u in (10, 12):
+                round_z(u // 2 - 5, 0, BLOCKS, z_banks[u // 2 - 5])
 
         out_view = out.rearrange("(b p) n -> p b n", p=P)
-        z_grouped = [keep.tile([P, P * PACK], BF16, name="z_grouped_%d" % b, align_bytes=64) for b in range(BLOCKS)]
+        w2_scales = keep.tile([P, N], U8, name="w2_scales", align_bytes=64)
 
-        def last_plane(b):
-            for a in range(2):
-                c0 = a * HALF + b % 2 * P
-                turn(block_banks[b][:, :P], pulls[14 + b // 2][:, c0 : c0 + P], False, a == 1)
-            round_z(3, b, 1, block_banks[b][:, :P])
+        z_grouped = [keep.tile([P, 2 * H], BF16, name="z_grouped_%d" % half, align_bytes=64) for half in range(2)]
 
         def turn_back(b):
-            words = z_turned[:, b * H : (b + 1) * H].bitcast(F32)
-            for u in range(2):
-                turn(word_banks[b][:, u * P : (u + 1) * P], words[:, u * P : (u + 1) * P], True, True)
-            nc.scalar.copy(out=z_grouped[b][:].bitcast(F32).rearrange("p (n u) -> p n u", u=2),
-                           in_=word_banks[b][:, : 2 * P].rearrange("p (u n) -> p n u", u=2))
+            turn_words(b, 1)
+            target = z_grouped[b // 2][:, b % 2 * H : (b % 2 + 1) * H].bitcast(F32).rearrange("p (n u) -> p n u", u=2)
+            source = word_banks[b][:, : 2 * P].rearrange("p (u n) -> p n u", u=2)
+            if b != 2:
+                nc.scalar.copy(out=target, in_=source)
+            else:
+                nc.vector.tensor_copy(out=target, in_=source)
 
-        def finish(b):
-            z_codes = keep.tile([P, P], U32, name="z_codes_%d" % b, align_bytes=64)
-            z_scales = keep.tile([P, P], U8, name="z_scales_%d" % b, align_bytes=64)
-            nc.vector.quantize_mx(out=z_codes[:].bitcast(FP8X4), scales=z_scales[:], in_=z_grouped[b][:])
-            last = b == BLOCKS - 1
-            parts = [(block_banks[b], 0, 2), (banks[7], 2, 2)] if last else [(block_banks[b], 0, 4)]
-            for acc, r0, count in parts:
-                for r in range(count):
-                    rows = slice((r0 + r) * P, (r0 + r + 1) * P)
-                    nc.tensor.matmul_mx(out=acc[:, r * P : (r + 1) * P], lhsT=w2_codes[:, rows].bitcast(FP8X4), lhsT_scale=w2_scales[:, rows],
+        def finish(b0, count, z_grouped, parts):
+            width = count * P
+            z_codes = keep.tile([P, width], U32, name="z_codes_%d" % b0, align_bytes=64)
+            z_scales = keep.tile([P, width], U8, name="z_scales_%d" % b0, align_bytes=64)
+            nc.vector.quantize_mx(out=z_codes[:].bitcast(FP8X4), scales=z_scales[:], in_=z_grouped[:])
+            for acc, r0, rows, engine in parts:
+                for r in range(rows):
+                    cols = slice((r0 + r) * P, (r0 + r + 1) * P)
+                    nc.tensor.matmul_mx(out=acc[:, r * width : (r + 1) * width], lhsT=w2_codes[:, cols].bitcast(FP8X4), lhsT_scale=w2_scales[:, cols],
                                         rhs=z_codes[:].bitcast(FP8X4), rhs_scale=z_scales[:], start=True, stop=True)
-                result = keep.tile([P, count, P], F32, name="result_%d_%d" % (b, r0), align_bytes=64)
-                if r0:
-                    nc.vector.tensor_copy(out=result[:].rearrange("p b n -> p (b n)"), in_=acc[:, : count * P])
+                result = keep.tile([P, rows, width], F32, name="result_%d_%d" % (b0, r0), align_bytes=64)
+                if engine == "vector":
+                    nc.vector.tensor_copy(out=result[:].rearrange("p b n -> p (b n)"), in_=acc[:, : rows * width])
                 else:
-                    nc.scalar.copy(out=result[:].rearrange("p b n -> p (b n)"), in_=acc[:, : count * P])
-                queue = nc.scalar if last and r0 == 0 else nc.sync
-                queue.dma_start(out=out_view[:, r0 : r0 + count, b * P : (b + 1) * P], in_=result[:])
+                    nc.scalar.copy(out=result[:].rearrange("p b n -> p (b n)"), in_=acc[:, : rows * width])
+                queue = nc.scalar if b0 == 2 and r0 == 2 else nc.sync
+                queue.dma_start(out=out_view[:, r0 : r0 + rows, b0 * P : b0 * P + width], in_=result[:])
 
         for b in range(BLOCKS):
-            last_plane(b)
+            turn_words(b, 0)
+        open_part(3, 0, 2, banks[2])
+        part_unit(3, (0, 1), 0, 2, banks[2], ring[14 % RING][:], pulls[0][:])
+        for b in (2, 3):
+            open_part(3, b, 1, banks[b + 1])
+            cols = slice((b - 2) * HALF, (b - 1) * HALF)
+            part_unit(3, (0, 1), b, 1, banks[b + 1], ring[15 % RING][:, cols], pulls[1][:, cols])
+        round_z(2, 0, BLOCKS, z_banks[2])
+        round_z(3, 0, 2, banks[2])
+        for b in range(2):
             turn_back(b)
-        for b in range(BLOCKS):
-            finish(b)
+        for b in (2, 3):
+            round_z(3, b, 1, banks[b + 1])
+        w2_codes = keep.tile([P, N], U32, name="w2_codes", tag="pulls_1", align_bytes=64)
+        nc.vector.quantize_mx(out=w2_codes[:].bitcast(FP8X4), scales=w2_scales[:], in_=w2_grouped)
+        for b in (2, 3):
+            turn_back(b)
+        finish(0, 2, z_grouped[0], [(banks[2], 0, 2, "scalar"), (banks[1], 2, 2, "vector")])
+        finish(2, 2, z_grouped[1], [(banks[3], 0, 2, "scalar"), (banks[4], 2, 1, "scalar"), (banks[7], 3, 1, "vector")])

@@ -25,7 +25,6 @@ BANK = 512
 HALF = S // 2
 BLOCKS = S // P
 RING = 3
-W2_EARLY = 192
 
 
 def tile_picked_coupled_none_p_kernel(tc, x_words, x_scales, w1, gn, w2, offs, p1, p2, q1, q2, out):
@@ -41,7 +40,7 @@ def tile_picked_coupled_none_p_kernel(tc, x_words, x_scales, w1, gn, w2, offs, p
         x_bytes = keep.tile([P, T], U8, name="x_bytes", align_bytes=64)
         x_packed = keep.tile([P, T], I32, name="x_packed", tag="x_packed", align_bytes=64)
         w1_raw = keep.tile([P, PACK, H], F32, name="w1_raw", align_bytes=64)
-        w2_raw = [keep.tile([P, PACK, width], F32, name="w2_raw_%d" % width, align_bytes=64) for width in (W2_EARLY, N - W2_EARLY)]
+        w2_raw = [keep.tile([P, PACK, width], F32, name="w2_raw_%d" % width, align_bytes=64) for width in (P, N - P)]
         gain = keep.tile([P, PACK], F32, name="gain")
         ident = keep.tile([P, P], F32, name="ident", align_bytes=64)
 
@@ -55,10 +54,10 @@ def tile_picked_coupled_none_p_kernel(tc, x_words, x_scales, w1, gn, w2, offs, p
         nc.sync.dma_start(out=lists["p1"][:], in_=p1)
         nc.sync.dma_start(out=lists["p2"][:], in_=p2)
         w2_view = w2.rearrange("(p j) c -> p j c", j=PACK)
-        nc.sync.dma_start(out=w2_raw[0][:], in_=w2_view[:, :, :W2_EARLY])
-        nc.sync.dma_start(out=w2_raw[1][:], in_=w2_view[:, :, W2_EARLY:])
+        nc.sync.dma_start(out=w2_raw[0][:], in_=w2_view[:, :, :P])
         nc.sync.dma_start(out=lists["q1"][:], in_=q1)
         nc.sync.dma_start(out=lists["q2"][:], in_=q2)
+        nc.sync.dma_start(out=w2_raw[1][:], in_=w2_view[:, :, P:])
 
         make_identity(nc, ident[:])
         window = []
@@ -108,18 +107,31 @@ def tile_picked_coupled_none_p_kernel(tc, x_words, x_scales, w1, gn, w2, offs, p
                                 start=True, stop=True)
 
         sum_banks = [banks[5], banks[6]] * 2
-        back_banks = [banks[0], banks[1]] * 2
+        back_banks = [banks[0], banks[1]]
         z_banks = [banks[5], banks[6], banks[1]]
         ring = [keep.tile([P, S], F32, name="ring_%d" % r, align_bytes=64) for r in range(RING)]
-        shared = keep.tile([P, 2 * S], F32, name="shared", align_bytes=64)
-        turned_h = shared[:, 2 * W2_EARLY : 2 * W2_EARLY + S]
-        w2_grouped = shared[:].bitcast(BF16)
         pulls = [keep.tile([P, S], F32, name="pulls_%d" % a, tag="pulls_%d" % a, align_bytes=64) for a in range(2)]
+        turned_h = keep.tile([P, S], F32, name="turned_h", tag="turned_h", align_bytes=64)[:]
+        first_pull = keep.tile([P, S], F32, name="first_pull", tag="first_pull", align_bytes=64)[:]
+        results = [pulls[1][:] if u % 2 else (first_pull if u < 12 else pulls[0][:]) for u in range(13)]
+        results[10] = turned_h
+        results.append(keep.tile([P, S], F32, name="last_whole_pull", tag="w2_codes", align_bytes=64)[:])
         h_window = window[:3] + [keep.tile([P, S], F32, name="last_window", tag="last_window", align_bytes=64)]
         windows = [window, h_window]
         z_turned = keep.tile([P, BLOCKS * H], BF16, name="z_turned", align_bytes=64)
-        nc.gpsimd.tensor_scalar(out=w2_grouped[:, : PACK * W2_EARLY].rearrange("p (c j) -> p c j", j=PACK), in0=w2_raw[0][:].rearrange("p j c -> p c j"),
-                                scalar1=1.0, scalar2=0.0, op0=MULT, op1=ADD)
+
+        w2_grouped = {}
+
+        def w2_part(c, tag):
+            if tag not in w2_grouped:
+                w2_grouped[tag] = keep.tile([P, 2 * S if c == 1 else S], BF16, name="w2_grouped_%d" % c, tag=tag, align_bytes=64)
+            first = S if c == 2 else 0
+            return w2_grouped[tag][:, first : first + S].rearrange("p (c j) -> p c j", j=PACK)
+
+        def w2_source(c):
+            return (w2_raw[1][:, :, (c - 1) * P : c * P] if c else w2_raw[0][:]).rearrange("p j c -> p c j")
+
+        nc.gpsimd.tensor_scalar(out=w2_part(0, "w2_early"), in0=w2_source(0), scalar1=1.0, scalar2=0.0, op0=MULT, op1=ADD)
 
         def fused(target, step, t, a, n0, width):
             nc.vector.tensor_tensor(out=target,
@@ -137,11 +149,11 @@ def tile_picked_coupled_none_p_kernel(tc, x_words, x_scales, w1, gn, w2, offs, p
 
         def unit(u):
             fused(ring[u % RING][:], u // 8, u // 2 % PACK, u % 2, 0, S)
-            tanh(pulls[u % 2][:], ring[u % RING][:])
+            tanh(results[u], ring[u % RING][:])
             bank = sum_banks[u // 2] if u < 8 else z_banks[u // 2 - 4]
             if u >= 8 and u % 2 == 0:
                 turn_blocks(bank, window[u // 2 - 4], True, False)
-            turn_blocks(bank, pulls[u % 2], False, u % 2 == 1)
+            turn_blocks(bank, results[u], False, u % 2 == 1)
 
         def open_part(t, b0, count, bank):
             for b in range(count):
@@ -158,11 +170,11 @@ def tile_picked_coupled_none_p_kernel(tc, x_words, x_scales, w1, gn, w2, offs, p
 
         def leave(t):
             nc.scalar.copy(out=turned_h, in_=sum_banks[t][:])
-            turn_blocks(back_banks[t], turned_h, True, True)
+            turn_blocks(back_banks[t % 2], turned_h, True, True)
 
         def close(t):
-            nc.scalar.copy(out=h_window[t][:, :S], in_=back_banks[t][:])
-            if t:
+            nc.scalar.copy(out=h_window[t][:, :S], in_=back_banks[t % 2][:])
+            if t >= 2:
                 nc.sync.dma_start(out=plain[t][:], in_=h_window[t][:, :S])
 
         def round_z(t, b0, count, bank):
@@ -192,8 +204,8 @@ def tile_picked_coupled_none_p_kernel(tc, x_words, x_scales, w1, gn, w2, offs, p
             for a in range(2):
                 fused(ring[a][:, n0 : n0 + HALF], 0, 0, a, n0, HALF)
         for a in range(2):
-            tanh(pulls[a][:], ring[a][:])
-            turn_blocks(sum_banks[0], pulls[a], False, a == 1)
+            tanh(results[a], ring[a][:])
+            turn_blocks(sum_banks[0], results[a], False, a == 1)
 
         word_banks = [banks[7], banks[5], banks[6], banks[0]]
 
@@ -204,53 +216,54 @@ def tile_picked_coupled_none_p_kernel(tc, x_words, x_scales, w1, gn, w2, offs, p
         for u in range(2, 14):
             if u < 8 and u % 2 == 0:
                 open_sum(u // 2)
-            if u == 7:
-                nc.vector.tensor_copy(out=plain[0][:], in_=window[0][:, :S])
+            if u in (7, 9):
+                nc.vector.tensor_copy(out=plain[u // 2 - 3][:], in_=window[u // 2 - 3][:, :S])
             unit(u)
-            if u in (4, 6, 8, 10):
+            if u in (4, 6, 8):
                 close(u // 2 - 2)
             if u in (2, 4, 6, 8):
                 leave(u // 2 - 1)
-            if u in (10, 11):
-                width = (N - W2_EARLY) // 2
-                c0 = (u - 10) * width
-                nc.scalar.copy(out=w2_grouped[:, PACK * (W2_EARLY + c0) : PACK * (W2_EARLY + c0 + width)].rearrange("p (c j) -> p c j", j=PACK),
-                               in_=w2_raw[1][:, :, c0 : c0 + width].rearrange("p j c -> p c j"))
-
+            if u in (9, 11, 12):
+                c = 3 if u == 9 else u - 10
+                nc.scalar.copy(out=w2_part(c, "first_pull" if c == 3 else "turned_h"), in_=w2_source(c))
+            if u == 9:
+                close(3)
             if u in (10, 12):
                 round_z(u // 2 - 5, 0, BLOCKS, z_banks[u // 2 - 5])
 
-        out_view = out.rearrange("(b p) n -> p b n", p=P)
         w2_scales = keep.tile([P, N], U8, name="w2_scales", align_bytes=64)
 
-        z_grouped = [keep.tile([P, 2 * H], BF16, name="z_grouped_%d" % half, align_bytes=64) for half in range(2)]
+        z_grouped = [keep.tile([P, 2 * H], BF16, name="z_grouped_%d" % half, tag="z_grouped_%d" % half, align_bytes=64) for half in range(2)]
 
         def turn_back(b):
             turn_words(b, 1)
             target = z_grouped[b // 2][:, b % 2 * H : (b % 2 + 1) * H].bitcast(F32).rearrange("p (n u) -> p n u", u=2)
             source = word_banks[b][:, : 2 * P].rearrange("p (u n) -> p n u", u=2)
-            if b != 2:
+            if b % 2 == 0:
                 nc.scalar.copy(out=target, in_=source)
             else:
                 nc.vector.tensor_copy(out=target, in_=source)
 
-        def finish(b0, count, z_grouped, parts):
-            width = count * P
-            z_codes = keep.tile([P, width], U32, name="z_codes_%d" % b0, align_bytes=64)
-            z_scales = keep.tile([P, width], U8, name="z_scales_%d" % b0, align_bytes=64)
-            nc.vector.quantize_mx(out=z_codes[:].bitcast(FP8X4), scales=z_scales[:], in_=z_grouped[:])
-            for acc, r0, rows, engine in parts:
-                for r in range(rows):
-                    cols = slice((r0 + r) * P, (r0 + r + 1) * P)
-                    nc.tensor.matmul_mx(out=acc[:, r * width : (r + 1) * width], lhsT=w2_codes[:, cols].bitcast(FP8X4), lhsT_scale=w2_scales[:, cols],
-                                        rhs=z_codes[:].bitcast(FP8X4), rhs_scale=z_scales[:], start=True, stop=True)
-                result = keep.tile([P, rows, width], F32, name="result_%d_%d" % (b0, r0), align_bytes=64)
+        z_codes = keep.tile([P, S], U32, name="z_codes", align_bytes=64)
+        z_scales = keep.tile([P, S], U8, name="z_scales", align_bytes=64)
+
+        def quantize_z(half):
+            cols = slice(half * HALF, (half + 1) * HALF)
+            nc.vector.quantize_mx(out=z_codes[:, cols].bitcast(FP8X4), scales=z_scales[:, cols], in_=z_grouped[half][:])
+
+        def second_product(r, parts):
+            result = keep.tile([P, S], F32, name="result_%d" % r, align_bytes=64)
+            width = S // len(parts)
+            for i, (acc, engine) in enumerate(parts):
+                nodes = slice(i * width, (i + 1) * width)
+                nc.tensor.matmul_mx(out=acc[:, :width], lhsT=w2_codes[:, r * P : (r + 1) * P].bitcast(FP8X4),
+                                    lhsT_scale=w2_scales[:, r * P : (r + 1) * P],
+                                    rhs=z_codes[:, nodes].bitcast(FP8X4), rhs_scale=z_scales[:, nodes], start=True, stop=True)
                 if engine == "vector":
-                    nc.vector.tensor_copy(out=result[:].rearrange("p b n -> p (b n)"), in_=acc[:, : rows * width])
+                    nc.vector.tensor_copy(out=result[:, nodes], in_=acc[:, :width])
                 else:
-                    nc.scalar.copy(out=result[:].rearrange("p b n -> p (b n)"), in_=acc[:, : rows * width])
-                queue = nc.scalar if b0 == 2 and r0 == 2 else nc.sync
-                queue.dma_start(out=out_view[:, r0 : r0 + rows, b0 * P : b0 * P + width], in_=result[:])
+                    nc.scalar.copy(out=result[:, nodes], in_=acc[:, :width])
+            nc.sync.dma_start(out=out[r * P : (r + 1) * P, :], in_=result[:])
 
         for b in range(BLOCKS):
             turn_words(b, 0)
@@ -261,14 +274,18 @@ def tile_picked_coupled_none_p_kernel(tc, x_words, x_scales, w1, gn, w2, offs, p
             cols = slice((b - 2) * HALF, (b - 1) * HALF)
             part_unit(3, (0, 1), b, 1, banks[b + 1], ring[15 % RING][:, cols], pulls[1][:, cols])
         round_z(2, 0, BLOCKS, z_banks[2])
+        w2_codes = keep.tile([P, N], U32, name="w2_codes", tag="w2_codes", align_bytes=64)
+        for tag, cols in (("w2_early", slice(0, P)), ("turned_h", slice(P, 3 * P)), ("first_pull", slice(3 * P, N))):
+            nc.vector.quantize_mx(out=w2_codes[:, cols].bitcast(FP8X4), scales=w2_scales[:, cols], in_=w2_grouped[tag][:])
         round_z(3, 0, 2, banks[2])
-        for b in range(2):
-            turn_back(b)
         for b in (2, 3):
             round_z(3, b, 1, banks[b + 1])
-        w2_codes = keep.tile([P, N], U32, name="w2_codes", tag="pulls_1", align_bytes=64)
-        nc.vector.quantize_mx(out=w2_codes[:].bitcast(FP8X4), scales=w2_scales[:], in_=w2_grouped)
-        for b in (2, 3):
+        for b in range(3):
             turn_back(b)
-        finish(0, 2, z_grouped[0], [(banks[2], 0, 2, "scalar"), (banks[1], 2, 2, "vector")])
-        finish(2, 2, z_grouped[1], [(banks[3], 0, 2, "scalar"), (banks[4], 2, 1, "scalar"), (banks[7], 3, 1, "vector")])
+        quantize_z(0)
+        turn_back(3)
+        quantize_z(1)
+        second_product(0, [(banks[2], "scalar"), (banks[7], "vector")])
+        second_product(1, [(banks[1], "scalar")])
+        second_product(2, [(banks[3], "vector")])
+        second_product(3, [(banks[2], "scalar"), (banks[7], "vector")])

@@ -109,24 +109,22 @@ def tile_picked_coupled_none_p_kernel(tc, x_words, x_scales, w1, gn, w2, offs, p
         sum_banks = [banks[5], banks[6]] * 2
         back_banks = [banks[0], banks[1]]
         z_banks = [banks[5], banks[6], banks[1]]
-        ring = [keep.tile([P, S], F32, name="ring_%d" % r, align_bytes=64) for r in range(RING)]
+        ring = [keep.tile([P, S], F32, name="ring_%d" % r, tag="ring_%d" % r, align_bytes=64) for r in range(RING)]
         pulls = [keep.tile([P, S], F32, name="pulls_%d" % a, tag="pulls_%d" % a, align_bytes=64) for a in range(2)]
         turned_h = keep.tile([P, S], F32, name="turned_h", tag="turned_h", align_bytes=64)[:]
         first_pull = keep.tile([P, S], F32, name="first_pull", tag="first_pull", align_bytes=64)[:]
-        results = [pulls[1][:] if u % 2 else (first_pull if u < 12 else pulls[0][:]) for u in range(13)]
-        results[10] = turned_h
-        results.append(keep.tile([P, S], F32, name="last_whole_pull", tag="w2_codes", align_bytes=64)[:])
-        h_window = window[:3] + [keep.tile([P, S], F32, name="last_window", tag="last_window", align_bytes=64)]
+        turned = [first_pull, turned_h]
+        results = [pulls[1][:] if u % 2 else (turned[u // 2 % 2] if u < 12 else pulls[0][:]) for u in range(13)]
+        results.append(keep.tile([P, S], F32, name="last_whole_pull", align_bytes=64)[:])
+        h_window = window[:3] + [keep.tile([P, S], F32, name="last_window", align_bytes=64)]
         windows = [window, h_window]
-        z_turned = keep.tile([P, BLOCKS * H], BF16, name="z_turned", align_bytes=64)
+        late = [keep.tile([P, S], F32, name="late_%d" % i, tag="late_%d" % i, align_bytes=64) for i in range(2)]
 
-        w2_grouped = {}
+        w2_grouped = []
 
         def w2_part(c, tag):
-            if tag not in w2_grouped:
-                w2_grouped[tag] = keep.tile([P, 2 * S if c == 1 else S], BF16, name="w2_grouped_%d" % c, tag=tag, align_bytes=64)
-            first = S if c == 2 else 0
-            return w2_grouped[tag][:, first : first + S].rearrange("p (c j) -> p c j", j=PACK)
+            w2_grouped.append(keep.tile([P, S], BF16, name="w2_grouped_%d" % c, tag=tag, align_bytes=64))
+            return w2_grouped[c][:].rearrange("p (c j) -> p c j", j=PACK)
 
         def w2_source(c):
             return (w2_raw[1][:, :, (c - 1) * P : c * P] if c else w2_raw[0][:]).rearrange("p j c -> p c j")
@@ -148,8 +146,9 @@ def tile_picked_coupled_none_p_kernel(tc, x_words, x_scales, w1, gn, w2, offs, p
             turn_blocks(sum_banks[t], plain[t] if t < 2 else window[t], True, False)
 
         def unit(u):
-            fused(ring[u % RING][:], u // 8, u // 2 % PACK, u % 2, 0, S)
-            tanh(results[u], ring[u % RING][:])
+            work = ring[u % RING][:] if u < 13 else turned[0]
+            fused(work, u // 8, u // 2 % PACK, u % 2, 0, S)
+            tanh(results[u], work)
             bank = sum_banks[u // 2] if u < 8 else z_banks[u // 2 - 4]
             if u >= 8 and u % 2 == 0:
                 turn_blocks(bank, window[u // 2 - 4], True, False)
@@ -169,13 +168,16 @@ def tile_picked_coupled_none_p_kernel(tc, x_words, x_scales, w1, gn, w2, offs, p
                 turn(bank[:, b * P : (b + 1) * P], result[:, c * P : (c + 1) * P], False, which[-1] == 1 and c == len(which) * count - 1)
 
         def leave(t):
-            nc.scalar.copy(out=turned_h, in_=sum_banks[t][:])
-            turn_blocks(back_banks[t % 2], turned_h, True, True)
+            for half in range(2):
+                cols = slice(half * HALF, (half + 1) * HALF)
+                nc.scalar.copy(out=turned[t % 2][:, cols], in_=sum_banks[t][:, cols])
+                for c in range(2):
+                    turn(back_banks[half][:, c * P : (c + 1) * P], turned[t % 2][:, half * HALF + c * P : half * HALF + (c + 1) * P], c == 0, c == 1)
 
         def close(t):
-            nc.scalar.copy(out=h_window[t][:, :S], in_=back_banks[t % 2][:])
-            if t >= 2:
-                nc.sync.dma_start(out=plain[t][:], in_=h_window[t][:, :S])
+            for half in range(2):
+                nc.scalar.copy(out=h_window[t][:, half * HALF : (half + 1) * HALF], in_=back_banks[half][:, :HALF])
+            nc.sync.dma_start(out=plain[t][:], in_=h_window[t][:, :S])
 
         def round_z(t, b0, count, bank):
             l, h = divmod(t, 2)
@@ -216,20 +218,15 @@ def tile_picked_coupled_none_p_kernel(tc, x_words, x_scales, w1, gn, w2, offs, p
         for u in range(2, 14):
             if u < 8 and u % 2 == 0:
                 open_sum(u // 2)
-            if u in (7, 9):
-                nc.vector.tensor_copy(out=plain[u // 2 - 3][:], in_=window[u // 2 - 3][:, :S])
             unit(u)
-            if u in (4, 6, 8):
-                close(u // 2 - 2)
+            if u in (3, 5, 7):
+                close(u // 2 - 1)
             if u in (2, 4, 6, 8):
                 leave(u // 2 - 1)
-            if u in (9, 11, 12):
-                c = 3 if u == 9 else u - 10
-                nc.scalar.copy(out=w2_part(c, "first_pull" if c == 3 else "turned_h"), in_=w2_source(c))
+            if u in (11, 12, 13):
+                nc.scalar.copy(out=w2_part(u - 10, "ring_%d" % ((u - 1) % RING)), in_=w2_source(u - 10))
             if u == 9:
                 close(3)
-            if u in (10, 12):
-                round_z(u // 2 - 5, 0, BLOCKS, z_banks[u // 2 - 5])
 
         w2_scales = keep.tile([P, N], U8, name="w2_scales", align_bytes=64)
 
@@ -265,21 +262,24 @@ def tile_picked_coupled_none_p_kernel(tc, x_words, x_scales, w1, gn, w2, offs, p
                     nc.scalar.copy(out=result[:, nodes], in_=acc[:, :width])
             nc.sync.dma_start(out=out[r * P : (r + 1) * P, :], in_=result[:])
 
-        for b in range(BLOCKS):
-            turn_words(b, 0)
         open_part(3, 0, 2, banks[2])
-        part_unit(3, (0, 1), 0, 2, banks[2], ring[14 % RING][:], pulls[0][:])
+        part_unit(3, (0, 1), 0, 2, banks[2], late[0][:], pulls[0][:])
         for b in (2, 3):
             open_part(3, b, 1, banks[b + 1])
             cols = slice((b - 2) * HALF, (b - 1) * HALF)
-            part_unit(3, (0, 1), b, 1, banks[b + 1], ring[15 % RING][:, cols], pulls[1][:, cols])
-        round_z(2, 0, BLOCKS, z_banks[2])
-        w2_codes = keep.tile([P, N], U32, name="w2_codes", tag="w2_codes", align_bytes=64)
-        for tag, cols in (("w2_early", slice(0, P)), ("turned_h", slice(P, 3 * P)), ("first_pull", slice(3 * P, N))):
-            nc.vector.quantize_mx(out=w2_codes[:, cols].bitcast(FP8X4), scales=w2_scales[:, cols], in_=w2_grouped[tag][:])
+            part_unit(3, (0, 1), b, 1, banks[b + 1], late[1][:, cols], pulls[1][:, cols])
+        z_turned = keep.tile([P, BLOCKS * H], BF16, name="z_turned", tag="late_0", align_bytes=64)
+        for t in range(3):
+            round_z(t, 0, BLOCKS, z_banks[t])
+        for b in range(BLOCKS):
+            turn_words(b, 0)
         round_z(3, 0, 2, banks[2])
         for b in (2, 3):
             round_z(3, b, 1, banks[b + 1])
+        w2_codes = keep.tile([P, N], U32, name="w2_codes", tag="pulls_1", align_bytes=64)
+        for c in range(PACK):
+            cols = slice(c * P, (c + 1) * P)
+            nc.vector.quantize_mx(out=w2_codes[:, cols].bitcast(FP8X4), scales=w2_scales[:, cols], in_=w2_grouped[c][:])
         for b in range(3):
             turn_back(b)
         quantize_z(0)

@@ -47,8 +47,8 @@ def tile_picked_coupled_none_p_kernel(tc, x_words, x_scales, w1, gn, w2, offs, p
         nc.vector.memset(x_bytes[:].bitcast(I32), 0)
         nc.sync.dma_start(out=w1_raw[:], in_=w1.rearrange("(p j) c -> p j c", j=PACK))
         nc.sync.dma_start(out=lists["offs"][:], in_=offs)
-        for q in range(4):
-            nc.sync.dma_start(out=x_bytes[32 * q : 32 * q + 4, :].bitcast(I32), in_=x_scales[0, 4 * q : 4 * q + 4, :].bitcast(I32))
+        for r in range(4):
+            nc.sync.dma_start(out=x_bytes[r:P:32, :].bitcast(I32), in_=x_scales[0, r:16:4, :].bitcast(I32))
         nc.sync.dma_start(out=gain[:], in_=gn.rearrange("(p j) o -> p (j o)", j=PACK))
         nc.sync.dma_start(out=x_packed[:], in_=x_words[0].rearrange("p n t -> p (n t)").bitcast(I32))
         nc.sync.dma_start(out=lists["p1"][:], in_=p1)
@@ -260,7 +260,10 @@ def tile_picked_coupled_none_p_kernel(tc, x_words, x_scales, w1, gn, w2, offs, p
                     nc.vector.tensor_copy(out=result[:, nodes], in_=acc[:, :width])
                 else:
                     nc.scalar.copy(out=result[:, nodes], in_=acc[:, :width])
-            nc.sync.dma_start(out=out[r * P : (r + 1) * P, :], in_=result[:])
+                if r == 0:
+                    nc.sync.dma_start(out=out[:P, nodes], in_=result[:, nodes])
+            if r:
+                nc.sync.dma_start(out=out[r * P : (r + 1) * P, :], in_=result[:])
 
         open_part(3, 0, 2, banks[2])
         part_unit(3, (0, 1), 0, 2, banks[2], late[0][:], pulls[0][:])
@@ -285,7 +288,5 @@ def tile_picked_coupled_none_p_kernel(tc, x_words, x_scales, w1, gn, w2, offs, p
         quantize_z(0)
         turn_back(3)
         quantize_z(1)
-        second_product(0, [(banks[2], "scalar"), (banks[7], "vector")])
-        second_product(1, [(banks[1], "scalar")])
-        second_product(2, [(banks[3], "vector")])
-        second_product(3, [(banks[2], "scalar"), (banks[7], "vector")])
+        for r in range(N // P):
+            second_product(r, [(banks[(2 * r + 1) % 8], "scalar"), (banks[(2 * r + 2) % 8], "vector")])

@@ -47,8 +47,8 @@ def tile_picked_coupled_none_p_kernel(tc, x_words, x_scales, w1, gn, w2, offs, p
         nc.vector.memset(x_bytes[:].bitcast(I32), 0)
         nc.sync.dma_start(out=w1_raw[:], in_=w1.rearrange("(p j) c -> p j c", j=PACK))
         nc.sync.dma_start(out=lists["offs"][:], in_=offs)
-        for r in range(4):
-            nc.sync.dma_start(out=x_bytes[r:P:32, :].bitcast(I32), in_=x_scales[0, r:16:4, :].bitcast(I32))
+        for q in range(4):
+            nc.sync.dma_start(out=x_bytes[32 * q : 32 * q + 4, :].bitcast(I32), in_=x_scales[0, 4 * q : 4 * q + 4, :].bitcast(I32))
         nc.sync.dma_start(out=gain[:], in_=gn.rearrange("(p j) o -> p (j o)", j=PACK))
         nc.sync.dma_start(out=x_packed[:], in_=x_words[0].rearrange("p n t -> p (n t)").bitcast(I32))
         nc.sync.dma_start(out=lists["p1"][:], in_=p1)
@@ -181,7 +181,7 @@ def tile_picked_coupled_none_p_kernel(tc, x_words, x_scales, w1, gn, w2, offs, p
 
         def round_z(t, b0, count, bank):
             l, h = divmod(t, 2)
-            target = z_turned[:].rearrange("n (a l b h r) -> n l h a b r", l=2, b=16, h=2, r=8)[:, l, h, b0 : b0 + count]
+            target = z_turned[b0 // 2][l][:].rearrange("n (a b h r) -> n h a b r", b=16, h=2, r=8)[:, h, b0 % 2 : b0 % 2 + count]
             nc.vector.tensor_tensor(out=target, in0=bank[:, : count * P].rearrange("n (a b r) -> n a b r", b=16, r=8),
                                     in1=gain_rows[:, t].rearrange("n (b r) -> n b r", r=8).unsqueeze(1).to_broadcast([P, count, 16, 8]), op=MULT)
 
@@ -209,11 +209,11 @@ def tile_picked_coupled_none_p_kernel(tc, x_words, x_scales, w1, gn, w2, offs, p
             tanh(results[a], ring[a][:])
             turn_blocks(sum_banks[0], results[a], False, a == 1)
 
-        word_banks = [banks[7], banks[5], banks[6], banks[0]]
+        word_banks = [banks[7], banks[0], banks[5], banks[6]]
 
         def turn_words(b, u):
-            words = z_turned[:, b * H : (b + 1) * H].bitcast(F32)
-            turn(word_banks[b][:, u * P : (u + 1) * P], words[:, u * P : (u + 1) * P], True, True)
+            words = z_turned[b // 2][u][:].bitcast(F32)
+            turn(word_banks[b][:, u * P : (u + 1) * P], words[:, b % 2 * P : (b % 2 + 1) * P], True, True)
 
         for u in range(2, 14):
             if u < 8 and u % 2 == 0:
@@ -223,23 +223,20 @@ def tile_picked_coupled_none_p_kernel(tc, x_words, x_scales, w1, gn, w2, offs, p
                 close(u // 2 - 1)
             if u in (2, 4, 6, 8):
                 leave(u // 2 - 1)
-            if u in (11, 12, 13):
+            if u in (11, 12):
                 nc.scalar.copy(out=w2_part(u - 10, "ring_%d" % ((u - 1) % RING)), in_=w2_source(u - 10))
             if u == 9:
                 close(3)
 
         w2_scales = keep.tile([P, N], U8, name="w2_scales", align_bytes=64)
 
-        z_grouped = [keep.tile([P, 2 * H], BF16, name="z_grouped_%d" % half, tag="z_grouped_%d" % half, align_bytes=64) for half in range(2)]
+        z_grouped = [keep.tile([P, 2 * H], BF16, name="z_grouped_%d" % half, align_bytes=64) for half in range(2)]
 
         def turn_back(b):
             turn_words(b, 1)
             target = z_grouped[b // 2][:, b % 2 * H : (b % 2 + 1) * H].bitcast(F32).rearrange("p (n u) -> p n u", u=2)
             source = word_banks[b][:, : 2 * P].rearrange("p (u n) -> p n u", u=2)
-            if b % 2 == 0:
-                nc.scalar.copy(out=target, in_=source)
-            else:
-                nc.vector.tensor_copy(out=target, in_=source)
+            nc.scalar.copy(out=target, in_=source)
 
         z_codes = keep.tile([P, S], U32, name="z_codes", align_bytes=64)
         z_scales = keep.tile([P, S], U8, name="z_scales", align_bytes=64)
@@ -248,22 +245,23 @@ def tile_picked_coupled_none_p_kernel(tc, x_words, x_scales, w1, gn, w2, offs, p
             cols = slice(half * HALF, (half + 1) * HALF)
             nc.vector.quantize_mx(out=z_codes[:, cols].bitcast(FP8X4), scales=z_scales[:, cols], in_=z_grouped[half][:])
 
-        def second_product(r, parts):
-            result = keep.tile([P, S], F32, name="result_%d" % r, align_bytes=64)
-            width = S // len(parts)
-            for i, (acc, engine) in enumerate(parts):
-                nodes = slice(i * width, (i + 1) * width)
-                nc.tensor.matmul_mx(out=acc[:, :width], lhsT=w2_codes[:, r * P : (r + 1) * P].bitcast(FP8X4),
-                                    lhsT_scale=w2_scales[:, r * P : (r + 1) * P],
+        out_view = out.rearrange("(r p) n -> p r n", p=P)
+
+        def second_product(half, r0, accs):
+            nodes = slice(half * HALF, (half + 1) * HALF)
+            result = keep.tile([P, 2, HALF], F32, name="result_%d_%d" % (half, r0), align_bytes=64)
+            for r, acc in enumerate(accs):
+                cols = slice((r0 + r) * P, (r0 + r + 1) * P)
+                nc.tensor.matmul_mx(out=acc[:, :HALF], lhsT=w2_codes[:, cols].bitcast(FP8X4), lhsT_scale=w2_scales[:, cols],
                                     rhs=z_codes[:, nodes].bitcast(FP8X4), rhs_scale=z_scales[:, nodes], start=True, stop=True)
-                if engine == "vector":
-                    nc.vector.tensor_copy(out=result[:, nodes], in_=acc[:, :width])
+                if r:
+                    nc.vector.tensor_copy(out=result[:, r], in_=acc[:, :HALF])
                 else:
-                    nc.scalar.copy(out=result[:, nodes], in_=acc[:, :width])
-                if r == 0:
-                    nc.sync.dma_start(out=out[:P, nodes], in_=result[:, nodes])
-            if r:
-                nc.sync.dma_start(out=out[r * P : (r + 1) * P, :], in_=result[:])
+                    nc.scalar.copy(out=result[:, r], in_=acc[:, :HALF])
+                if half == 0 and r0 == 0:
+                    nc.sync.dma_start(out=out_view[:, r, nodes], in_=result[:, r])
+            if half or r0:
+                nc.sync.dma_start(out=out_view[:, r0 : r0 + 2, nodes], in_=result[:])
 
         open_part(3, 0, 2, banks[2])
         part_unit(3, (0, 1), 0, 2, banks[2], late[0][:], pulls[0][:])
@@ -271,22 +269,30 @@ def tile_picked_coupled_none_p_kernel(tc, x_words, x_scales, w1, gn, w2, offs, p
             open_part(3, b, 1, banks[b + 1])
             cols = slice((b - 2) * HALF, (b - 1) * HALF)
             part_unit(3, (0, 1), b, 1, banks[b + 1], late[1][:, cols], pulls[1][:, cols])
-        z_turned = keep.tile([P, BLOCKS * H], BF16, name="z_turned", tag="late_0", align_bytes=64)
-        for t in range(3):
-            round_z(t, 0, BLOCKS, z_banks[t])
-        for b in range(BLOCKS):
-            turn_words(b, 0)
-        round_z(3, 0, 2, banks[2])
+        nc.scalar.copy(out=w2_part(3, "late_1"), in_=w2_source(3))
+        z_turned = [[keep.tile([P, H], BF16, name="z_turned_%d_%d" % (half, l), tag="pulls_0" if (half, l) == (1, 0) else "z_turned_%d_%d" % (half, l), align_bytes=64)
+                     for l in range(2)] for half in range(2)]
+        for half in range(2):
+            for t in range(3):
+                round_z(t, 2 * half, 2, z_banks[t][:, half * HALF :])
+                if t == 1:
+                    for b in (2 * half, 2 * half + 1):
+                        turn_words(b, 0)
+            if half == 0:
+                round_z(3, 0, 2, banks[2])
+                for b in range(2):
+                    turn_back(b)
         for b in (2, 3):
             round_z(3, b, 1, banks[b + 1])
+        quantize_z(0)
         w2_codes = keep.tile([P, N], U32, name="w2_codes", tag="pulls_1", align_bytes=64)
         for c in range(PACK):
             cols = slice(c * P, (c + 1) * P)
             nc.vector.quantize_mx(out=w2_codes[:, cols].bitcast(FP8X4), scales=w2_scales[:, cols], in_=w2_grouped[c][:])
-        for b in range(3):
+        for b in (2, 3):
             turn_back(b)
-        quantize_z(0)
-        turn_back(3)
         quantize_z(1)
-        for r in range(N // P):
-            second_product(r, [(banks[(2 * r + 1) % 8], "scalar"), (banks[(2 * r + 2) % 8], "vector")])
+        second_product(0, 0, [banks[2], banks[1]])
+        second_product(0, 2, [banks[3], banks[4]])
+        second_product(1, 0, [banks[7], banks[0]])
+        second_product(1, 2, [banks[5], banks[6]])

@@ -40,7 +40,7 @@ def tile_picked_coupled_none_p_kernel(tc, x_words, x_scales, w1, gn, w2, offs, p
         x_bytes = keep.tile([P, T], U8, name="x_bytes", align_bytes=64)
         x_packed = keep.tile([P, T], I32, name="x_packed", tag="x_packed", align_bytes=64)
         w1_raw = keep.tile([P, PACK, H], F32, name="w1_raw", align_bytes=64)
-        w2_raw = [keep.tile([P, PACK, width], F32, name="w2_raw_%d" % width, align_bytes=64) for width in (P, N - P)]
+        w2_raw = keep.tile([P, PACK, N], F32, name="w2_raw", align_bytes=64)
         gain = keep.tile([P, PACK], F32, name="gain")
         ident = keep.tile([P, P], F32, name="ident", align_bytes=64)
 
@@ -53,11 +53,9 @@ def tile_picked_coupled_none_p_kernel(tc, x_words, x_scales, w1, gn, w2, offs, p
         nc.sync.dma_start(out=x_packed[:], in_=x_words[0].rearrange("p n t -> p (n t)").bitcast(I32))
         nc.sync.dma_start(out=lists["p1"][:], in_=p1)
         nc.sync.dma_start(out=lists["p2"][:], in_=p2)
-        w2_view = w2.rearrange("(p j) c -> p j c", j=PACK)
-        nc.sync.dma_start(out=w2_raw[0][:], in_=w2_view[:, :, :P])
         nc.sync.dma_start(out=lists["q1"][:], in_=q1)
         nc.sync.dma_start(out=lists["q2"][:], in_=q2)
-        nc.sync.dma_start(out=w2_raw[1][:], in_=w2_view[:, :, P:])
+        nc.sync.dma_start(out=w2_raw[:], in_=w2.rearrange("(p j) c -> p j c", j=PACK))
 
         make_identity(nc, ident[:])
         window = []
@@ -89,7 +87,7 @@ def tile_picked_coupled_none_p_kernel(tc, x_words, x_scales, w1, gn, w2, offs, p
 
         w1_grouped = keep.tile([P, H * PACK], BF16, name="w1_grouped", tag="picked_words", align_bytes=64)
         source = w1_raw[:].rearrange("p j (b h i) -> p h b i j", h=2, i=16)
-        target = w1_grouped[:].rearrange("p (l h b c r) -> p h b c l r", h=2, l=2, b=16, c=4)
+        target = w1_grouped[:].rearrange("p (h l b c r) -> p h b c l r", h=2, l=2, b=16, c=4)
         nc.vector.tensor_copy(out=target[:, 0], in_=source[:, 0])
         nc.scalar.copy(out=target[:, 1], in_=source[:, 1])
         w1_codes = keep.tile([P, H], U32, name="w1_codes", align_bytes=64)
@@ -102,7 +100,8 @@ def tile_picked_coupled_none_p_kernel(tc, x_words, x_scales, w1, gn, w2, offs, p
                                   in_=x_packed[:].bitcast(U32).indirect(lists["offs"][:, n0 // 16 : (n0 + width) // 16]))
 
         def first_product(acc, t, n0, width):
-            nc.tensor.matmul_mx(out=acc[:, :width], lhsT=w1_codes[:, t * P : (t + 1) * P].bitcast(FP8X4), lhsT_scale=w1_scales[:, t * P : (t + 1) * P],
+            cols = slice((t % 2 * 2 + t // 2) * P, (t % 2 * 2 + t // 2 + 1) * P)
+            nc.tensor.matmul_mx(out=acc[:, :width], lhsT=w1_codes[:, cols].bitcast(FP8X4), lhsT_scale=w1_scales[:, cols],
                                 rhs=picked_words[:, n0 : n0 + width].bitcast(FP8X4), rhs_scale=picked_bytes[:, n0 : n0 + width],
                                 start=True, stop=True)
 
@@ -127,9 +126,7 @@ def tile_picked_coupled_none_p_kernel(tc, x_words, x_scales, w1, gn, w2, offs, p
             return w2_grouped[c][:].rearrange("p (c j) -> p c j", j=PACK)
 
         def w2_source(c):
-            return (w2_raw[1][:, :, (c - 1) * P : c * P] if c else w2_raw[0][:]).rearrange("p j c -> p c j")
-
-        nc.gpsimd.tensor_scalar(out=w2_part(0, "w2_early"), in0=w2_source(0), scalar1=1.0, scalar2=0.0, op0=MULT, op1=ADD)
+            return w2_raw[:, :, c * P : (c + 1) * P].rearrange("p j c -> p c j")
 
         def fused(target, step, t, a, n0, width):
             nc.vector.tensor_tensor(out=target,
@@ -176,8 +173,9 @@ def tile_picked_coupled_none_p_kernel(tc, x_words, x_scales, w1, gn, w2, offs, p
 
         def close(t):
             for half in range(2):
-                nc.scalar.copy(out=h_window[t][:, half * HALF : (half + 1) * HALF], in_=back_banks[half][:, :HALF])
-            nc.sync.dma_start(out=plain[t][:], in_=h_window[t][:, :S])
+                cols = slice(half * HALF, (half + 1) * HALF)
+                nc.scalar.copy(out=h_window[t][:, cols], in_=back_banks[half][:, :HALF])
+                nc.sync.dma_start(out=plain[t][:, cols], in_=h_window[t][:, cols])
 
         def round_z(t, b0, count, bank):
             l, h = divmod(t, 2)
@@ -223,8 +221,8 @@ def tile_picked_coupled_none_p_kernel(tc, x_words, x_scales, w1, gn, w2, offs, p
                 close(u // 2 - 1)
             if u in (2, 4, 6, 8):
                 leave(u // 2 - 1)
-            if u in (11, 12):
-                nc.scalar.copy(out=w2_part(u - 10, "ring_%d" % ((u - 1) % RING)), in_=w2_source(u - 10))
+            if u in (11, 12, 13):
+                nc.scalar.copy(out=w2_part(u - 11, "ring_%d" % ((u - 1) % RING)), in_=w2_source(u - 11))
             if u == 9:
                 close(3)
 

@@ -25,6 +25,7 @@ BANK = 512
 HALF = S // 2
 BLOCKS = S // P
 RING = 3
+VECTOR_BLOCKS = 12
 
 
 def tile_picked_coupled_none_p_kernel(tc, x_words, x_scales, w1, gn, w2, offs, p1, p2, q1, q2, out):
@@ -88,8 +89,9 @@ def tile_picked_coupled_none_p_kernel(tc, x_words, x_scales, w1, gn, w2, offs, p
         w1_grouped = keep.tile([P, H * PACK], BF16, name="w1_grouped", tag="picked_words", align_bytes=64)
         source = w1_raw[:].rearrange("p j (b h i) -> p h b i j", h=2, i=16)
         target = w1_grouped[:].rearrange("p (h l b c r) -> p h b c l r", h=2, l=2, b=16, c=4)
-        nc.vector.tensor_copy(out=target[:, 0], in_=source[:, 0])
+        nc.vector.tensor_copy(out=target[:, 0, :VECTOR_BLOCKS], in_=source[:, 0, :VECTOR_BLOCKS])
         nc.scalar.copy(out=target[:, 1], in_=source[:, 1])
+        nc.scalar.copy(out=target[:, 0, VECTOR_BLOCKS:], in_=source[:, 0, VECTOR_BLOCKS:])
         w1_codes = keep.tile([P, H], U32, name="w1_codes", align_bytes=64)
         w1_scales = keep.tile([P, H], U8, name="w1_scales", align_bytes=64)
         nc.vector.quantize_mx(out=w1_codes[:].bitcast(FP8X4), scales=w1_scales[:], in_=w1_grouped[:])
@@ -256,9 +258,9 @@ def tile_picked_coupled_none_p_kernel(tc, x_words, x_scales, w1, gn, w2, offs, p
                     nc.vector.tensor_copy(out=result[:, r], in_=acc[:, :HALF])
                 else:
                     nc.scalar.copy(out=result[:, r], in_=acc[:, :HALF])
-                if half == 0 and r0 == 0:
-                    nc.sync.dma_start(out=out_view[:, r, nodes], in_=result[:, r])
-            if half or r0:
+                if (half, r0) in ((0, 0), (1, 2)):
+                    nc.sync.dma_start(out=out_view[:, r0 + r, nodes], in_=result[:, r])
+            if (half, r0) in ((0, 2), (1, 0)):
                 nc.sync.dma_start(out=out_view[:, r0 : r0 + 2, nodes], in_=result[:])
 
         open_part(3, 0, 2, banks[2])

@@ -25,7 +25,7 @@ BANK = 512
 HALF = S // 2
 BLOCKS = S // P
 RING = 3
-VECTOR_BLOCKS = 12
+VECTOR_BLOCKS = 8
 
 
 def tile_picked_coupled_none_p_kernel(tc, x_words, x_scales, w1, gn, w2, offs, p1, p2, q1, q2, out):
@@ -86,24 +86,31 @@ def tile_picked_coupled_none_p_kernel(tc, x_words, x_scales, w1, gn, w2, offs, p
         picked_bytes = keep.tile([P, S], U8, name="picked_bytes", align_bytes=64)
         nc.vector.tensor_copy(out=picked_bytes[:], in_=x_bytes[:].indirect(lists["offs"][:]))
 
-        w1_grouped = keep.tile([P, H * PACK], BF16, name="w1_grouped", tag="picked_words", align_bytes=64)
         source = w1_raw[:].rearrange("p j (b h i) -> p h b i j", h=2, i=16)
-        target = w1_grouped[:].rearrange("p (h l b c r) -> p h b c l r", h=2, l=2, b=16, c=4)
-        nc.vector.tensor_copy(out=target[:, 0, :VECTOR_BLOCKS], in_=source[:, 0, :VECTOR_BLOCKS])
-        nc.scalar.copy(out=target[:, 1], in_=source[:, 1])
-        nc.scalar.copy(out=target[:, 0, VECTOR_BLOCKS:], in_=source[:, 0, VECTOR_BLOCKS:])
-        w1_codes = keep.tile([P, H], U32, name="w1_codes", align_bytes=64)
-        w1_scales = keep.tile([P, H], U8, name="w1_scales", align_bytes=64)
-        nc.vector.quantize_mx(out=w1_codes[:].bitcast(FP8X4), scales=w1_scales[:], in_=w1_grouped[:])
+        w1_grouped = [keep.tile([P, 2 * H], BF16, name="w1_grouped_%d" % h, tag=tag, align_bytes=64) for h, tag in enumerate(("picked_words", "ring_0"))]
+        target = [tile[:].rearrange("p (l b c r) -> p b c l r", l=2, b=16, c=4) for tile in w1_grouped]
+        nc.vector.tensor_copy(out=target[0][:, :VECTOR_BLOCKS], in_=source[:, 0, :VECTOR_BLOCKS])
+        nc.scalar.copy(out=target[0][:, VECTOR_BLOCKS:], in_=source[:, 0, VECTOR_BLOCKS:])
+        nc.scalar.copy(out=target[1], in_=source[:, 1])
+        w1_codes, w1_scales = [], []
+
+        def quantize_w1(h, tag):
+            w1_codes.append(keep.tile([P, HALF], U32, name="w1_codes_%d" % h, tag=tag, align_bytes=64))
+            w1_scales.append(keep.tile([P, HALF], U8, name="w1_scales_%d" % h, align_bytes=64))
+            nc.vector.quantize_mx(out=w1_codes[h][:].bitcast(FP8X4), scales=w1_scales[h][:], in_=w1_grouped[h][:])
+
+        quantize_w1(0, "w1_codes_0")
         picked_words = keep.tile([P, S], U32, name="picked_words", tag="picked_words", align_bytes=64)
         pieces = [(0, HALF), (HALF, P), (HALF + P, P)]
         for n0, width in pieces:
             nc.vector.tensor_copy(out=picked_words[:, n0 : n0 + width],
                                   in_=x_packed[:].bitcast(U32).indirect(lists["offs"][:, n0 // 16 : (n0 + width) // 16]))
+        quantize_w1(1, "x_packed")
 
         def first_product(acc, t, n0, width):
-            cols = slice((t % 2 * 2 + t // 2) * P, (t % 2 * 2 + t // 2 + 1) * P)
-            nc.tensor.matmul_mx(out=acc[:, :width], lhsT=w1_codes[:, cols].bitcast(FP8X4), lhsT_scale=w1_scales[:, cols],
+            l, h = divmod(t, 2)
+            cols = slice(l * P, (l + 1) * P)
+            nc.tensor.matmul_mx(out=acc[:, :width], lhsT=w1_codes[h][:, cols].bitcast(FP8X4), lhsT_scale=w1_scales[h][:, cols],
                                 rhs=picked_words[:, n0 : n0 + width].bitcast(FP8X4), rhs_scale=picked_bytes[:, n0 : n0 + width],
                                 start=True, stop=True)
 

@@ -32,6 +32,7 @@ def tile_picked_coupled_none_p_kernel(tc, x_words, x_scales, w1, gn, w2, offs, p
     nc = tc.nc
     with ExitStack() as ctx:
         keep = ctx.enter_context(tc.tile_pool(name="keep", bufs=1))
+        shared = ctx.enter_context(tc.tile_pool(name="shared", bufs=1))
         psum = ctx.enter_context(tc.psum_pool(name="psum", bufs=1))
 
         banks = [psum.tile([P, BANK], F32, name="bank_%d" % b) for b in range(8)]
@@ -64,7 +65,8 @@ def tile_picked_coupled_none_p_kernel(tc, x_words, x_scales, w1, gn, w2, offs, p
             tile = keep.tile([P, 2 * S], F32, name="window_%d" % t, tag="window_%d" % t, align_bytes=64)
             nc.gpsimd.memset(tile[:, S:], 0.0)
             window.append(tile)
-        plain = [keep.tile([P, S], F32, name="plain_%d" % t, align_bytes=64) for t in range(PACK)]
+        plain = [keep.tile([P, S], F32, name="plain_%d" % t, align_bytes=64) for t in range(PACK - 1)]
+        plain.append(shared.tile([P, 2 * S], F32, name="plain_3", align_bytes=64, offset=0)[:, :S])
 
         def turn(dst, src, start, stop):
             nc.tensor.matmul(dst, lhsT=src, rhs=ident[:], start=start, stop=stop, is_transpose=True)
@@ -130,8 +132,7 @@ def tile_picked_coupled_none_p_kernel(tc, x_words, x_scales, w1, gn, w2, offs, p
 
         w2_grouped = []
 
-        def w2_part(c, tag):
-            w2_grouped.append(keep.tile([P, S], BF16, name="w2_grouped_%d" % c, tag=tag, align_bytes=64))
+        def w2_target(c):
             return w2_grouped[c][:].rearrange("p (c j) -> p c j", j=PACK)
 
         def w2_source(c):
@@ -207,7 +208,7 @@ def tile_picked_coupled_none_p_kernel(tc, x_words, x_scales, w1, gn, w2, offs, p
         nc.sync.dma_start(out=plain[2][:], in_=window[2][:, :S])
         double(plain[1][:], banks[2][:])
         double(window[3][:, :S], banks[4][:])
-        nc.sync.dma_start(out=plain[3][:], in_=window[3][:, :S])
+        nc.sync.dma_start(out=plain[3], in_=window[3][:, :S])
         open_sum(0)
         for n0 in (0, HALF):
             for a in range(2):
@@ -230,10 +231,11 @@ def tile_picked_coupled_none_p_kernel(tc, x_words, x_scales, w1, gn, w2, offs, p
                 close(u // 2 - 1)
             if u in (2, 4, 6, 8):
                 leave(u // 2 - 1)
-            if u in (11, 12, 13):
-                nc.scalar.copy(out=w2_part(u - 11, "ring_%d" % ((u - 1) % RING)), in_=w2_source(u - 11))
             if u == 9:
                 close(3)
+            if u == 13:
+                w2_grouped.append(keep.tile([P, S], BF16, name="w2_part_0", tag="ring_0", align_bytes=64))
+                nc.scalar.copy(out=w2_target(0), in_=w2_source(0))
 
         w2_scales = keep.tile([P, N], U8, name="w2_scales", align_bytes=64)
 
@@ -276,7 +278,11 @@ def tile_picked_coupled_none_p_kernel(tc, x_words, x_scales, w1, gn, w2, offs, p
             open_part(3, b, 1, banks[b + 1])
             cols = slice((b - 2) * HALF, (b - 1) * HALF)
             part_unit(3, (0, 1), b, 1, banks[b + 1], late[1][:, cols], pulls[1][:, cols])
-        nc.scalar.copy(out=w2_part(3, "late_1"), in_=w2_source(3))
+        for c in (1, 2):
+            w2_grouped.append(shared.tile([P, S], BF16, name="w2_part_%d" % c, align_bytes=64, offset=2 * S * c))
+            nc.gpsimd.tensor_scalar(out=w2_target(c), in0=w2_source(c), scalar1=1.0, scalar2=0.0, op0=MULT, op1=ADD)
+        w2_grouped.append(keep.tile([P, S], BF16, name="w2_part_3", tag="late_1", align_bytes=64))
+        nc.scalar.copy(out=w2_target(3), in_=w2_source(3))
         z_turned = [[keep.tile([P, H], BF16, name="z_turned_%d_%d" % (half, l), tag="pulls_0" if (half, l) == (1, 0) else "z_turned_%d_%d" % (half, l), align_bytes=64)
                      for l in range(2)] for half in range(2)]
         for half in range(2):

@@ -138,6 +138,8 @@ def tile_picked_coupled_none_p_kernel(tc, x_words, x_scales, w1, gn, w2, offs, p
         def w2_source(c):
             return w2_raw[:, :, c * P : (c + 1) * P].rearrange("p j c -> p c j")
 
+        fetched = keep.tile([P, S], F32, name="fetched", align_bytes=64)
+
         def fused(target, step, t, a, n0, width):
             nc.vector.tensor_tensor(out=target,
                                     in0=windows[step][t][:].indirect(step_lists[step][a][:, n0 // 16 : (n0 + width) // 16]),
@@ -167,8 +169,9 @@ def tile_picked_coupled_none_p_kernel(tc, x_words, x_scales, w1, gn, w2, offs, p
 
         def part_unit(t, which, b0, count, bank, work, result):
             width = count * P
-            for i, a in enumerate(which):
-                fused(work[:, i * width : (i + 1) * width], 1, t, a, b0 * P, width)
+            nodes = slice(b0 * P, b0 * P + width)
+            fused(work[:, :width], 1, t, 0, b0 * P, width)
+            nc.vector.tensor_tensor(out=work[:, width:], in0=fetched[:, nodes], in1=plain[t][:, nodes], op=SUBTRACT)
             tanh(result, work)
             for c in range(len(which) * count):
                 b = c % count
@@ -233,6 +236,10 @@ def tile_picked_coupled_none_p_kernel(tc, x_words, x_scales, w1, gn, w2, offs, p
                 leave(u // 2 - 1)
             if u == 9:
                 close(3)
+            if u == 11:
+                for n0 in (0, HALF):
+                    nc.scalar.activation(out=fetched[:, n0 : n0 + HALF], func=COPY,
+                                         in_=h_window[3][:].indirect(lists["q2"][:, n0 // 16 : (n0 + HALF) // 16]))
             if u == 13:
                 w2_grouped.append(keep.tile([P, S], BF16, name="w2_part_0", tag="ring_0", align_bytes=64))
                 nc.scalar.copy(out=w2_target(0), in_=w2_source(0))

@@ -116,9 +116,9 @@ def tile_picked_coupled_none_p_kernel(tc, x_words, x_scales, w1, gn, w2, offs, p
                                 rhs=picked_words[:, n0 : n0 + width].bitcast(FP8X4), rhs_scale=picked_bytes[:, n0 : n0 + width],
                                 start=True, stop=True)
 
-        sum_banks = [banks[5], banks[6]] * 2
+        sum_banks = [banks[5], banks[6], banks[2], banks[3]]
         back_banks = [banks[0], banks[1]]
-        z_banks = [banks[5], banks[6], banks[1]]
+        z_banks = [banks[2], banks[3], banks[1]]
         ring = [keep.tile([P, S], F32, name="ring_%d" % r, tag="ring_%d" % r, align_bytes=64) for r in range(RING)]
         pulls = [keep.tile([P, S], F32, name="pulls_%d" % a, tag="pulls_%d" % a, align_bytes=64) for a in range(2)]
         turned_h = keep.tile([P, S], F32, name="turned_h", tag="turned_h", align_bytes=64)[:]
@@ -152,11 +152,15 @@ def tile_picked_coupled_none_p_kernel(tc, x_words, x_scales, w1, gn, w2, offs, p
             nc.scalar.activation(out=target, in_=acc, func=COPY, scale=2.0)
 
         def open_sum(t):
-            turn_blocks(sum_banks[t], plain[t] if t < 2 else window[t], True, False)
+            turn_blocks(sum_banks[t], window[t], True, False)
 
         def unit(u):
             work = ring[u % RING][:] if u < 13 else turned[0]
-            fused(work, u // 8, u // 2 % PACK, u % 2, 0, S)
+            if u in (8, 10, 12):
+                for n0 in (0, HALF):
+                    fused(work[:, n0 : n0 + HALF], 1, u // 2 % PACK, 0, n0, HALF)
+            else:
+                fused(work, u // 8, u // 2 % PACK, u % 2, 0, S)
             tanh(results[u], work)
             bank = sum_banks[u // 2] if u < 8 else z_banks[u // 2 - 4]
             if u >= 8 and u % 2 == 0:
@@ -184,11 +188,10 @@ def tile_picked_coupled_none_p_kernel(tc, x_words, x_scales, w1, gn, w2, offs, p
                 for c in range(2):
                     turn(back_banks[half][:, c * P : (c + 1) * P], turned[t % 2][:, half * HALF + c * P : half * HALF + (c + 1) * P], c == 0, c == 1)
 
-        def close(t):
-            for half in range(2):
-                cols = slice(half * HALF, (half + 1) * HALF)
-                nc.scalar.copy(out=h_window[t][:, cols], in_=back_banks[half][:, :HALF])
-                nc.sync.dma_start(out=plain[t][:, cols], in_=h_window[t][:, cols])
+        def close(t, half):
+            cols = slice(half * HALF, (half + 1) * HALF)
+            nc.scalar.copy(out=h_window[t][:, cols], in_=back_banks[half][:, :HALF])
+            nc.sync.dma_start(out=plain[t][:, cols], in_=h_window[t][:, cols])
 
         def round_z(t, b0, count, bank):
             l, h = divmod(t, 2)
@@ -212,7 +215,8 @@ def tile_picked_coupled_none_p_kernel(tc, x_words, x_scales, w1, gn, w2, offs, p
         double(plain[1][:], banks[2][:])
         double(window[3][:, :S], banks[4][:])
         nc.sync.dma_start(out=plain[3], in_=window[3][:, :S])
-        open_sum(0)
+        for t in range(PACK):
+            open_sum(t)
         for n0 in (0, HALF):
             for a in range(2):
                 fused(ring[a][:, n0 : n0 + HALF], 0, 0, a, n0, HALF)
@@ -220,22 +224,23 @@ def tile_picked_coupled_none_p_kernel(tc, x_words, x_scales, w1, gn, w2, offs, p
             tanh(results[a], ring[a][:])
             turn_blocks(sum_banks[0], results[a], False, a == 1)
 
-        word_banks = [banks[7], banks[0], banks[5], banks[6]]
+        word_banks = [banks[7], banks[0], banks[2], banks[3]]
+        part_banks = [banks[5], banks[6], banks[4]]
 
         def turn_words(b, u):
             words = z_turned[b // 2][u][:].bitcast(F32)
             turn(word_banks[b][:, u * P : (u + 1) * P], words[:, b % 2 * P : (b % 2 + 1) * P], True, True)
 
         for u in range(2, 14):
-            if u < 8 and u % 2 == 0:
-                open_sum(u // 2)
             unit(u)
-            if u in (3, 5, 7):
-                close(u // 2 - 1)
+            if u in (3, 5, 7, 9):
+                close(u // 2 - 1, 0)
+            if u in (4, 6, 8):
+                close(u // 2 - 2, 1)
             if u in (2, 4, 6, 8):
                 leave(u // 2 - 1)
             if u == 9:
-                close(3)
+                close(3, 1)
             if u == 11:
                 for n0 in (0, HALF):
                     nc.scalar.activation(out=fetched[:, n0 : n0 + HALF], func=COPY,
@@ -279,12 +284,12 @@ def tile_picked_coupled_none_p_kernel(tc, x_words, x_scales, w1, gn, w2, offs, p
             if (half, r0) in ((0, 2), (1, 0)):
                 nc.sync.dma_start(out=out_view[:, r0 : r0 + 2, nodes], in_=result[:])
 
-        open_part(3, 0, 2, banks[2])
-        part_unit(3, (0, 1), 0, 2, banks[2], late[0][:], pulls[0][:])
+        open_part(3, 0, 2, part_banks[0])
+        part_unit(3, (0, 1), 0, 2, part_banks[0], late[0][:], pulls[0][:])
         for b in (2, 3):
-            open_part(3, b, 1, banks[b + 1])
+            open_part(3, b, 1, part_banks[b - 1])
             cols = slice((b - 2) * HALF, (b - 1) * HALF)
-            part_unit(3, (0, 1), b, 1, banks[b + 1], late[1][:, cols], pulls[1][:, cols])
+            part_unit(3, (0, 1), b, 1, part_banks[b - 1], late[1][:, cols], pulls[1][:, cols])
         for c in (1, 2):
             w2_grouped.append(shared.tile([P, S], BF16, name="w2_part_%d" % c, align_bytes=64, offset=2 * S * c))
             nc.gpsimd.tensor_scalar(out=w2_target(c), in0=w2_source(c), scalar1=1.0, scalar2=0.0, op0=MULT, op1=ADD)
@@ -299,11 +304,11 @@ def tile_picked_coupled_none_p_kernel(tc, x_words, x_scales, w1, gn, w2, offs, p
                     for b in (2 * half, 2 * half + 1):
                         turn_words(b, 0)
             if half == 0:
-                round_z(3, 0, 2, banks[2])
+                round_z(3, 0, 2, part_banks[0])
                 for b in range(2):
                     turn_back(b)
         for b in (2, 3):
-            round_z(3, b, 1, banks[b + 1])
+            round_z(3, b, 1, part_banks[b - 1])
         quantize_z(0)
         w2_codes = keep.tile([P, N], U32, name="w2_codes", tag="pulls_1", align_bytes=64)
         for c in range(PACK):
@@ -312,7 +317,7 @@ def tile_picked_coupled_none_p_kernel(tc, x_words, x_scales, w1, gn, w2, offs, p
         for b in (2, 3):
             turn_back(b)
         quantize_z(1)
-        second_product(0, 0, [banks[2], banks[1]])
-        second_product(0, 2, [banks[3], banks[4]])
+        second_product(0, 0, [banks[5], banks[1]])
+        second_product(0, 2, [banks[6], banks[4]])
         second_product(1, 0, [banks[7], banks[0]])
-        second_product(1, 2, [banks[5], banks[6]])
+        second_product(1, 2, [banks[2], banks[3]])

@@ -224,6 +224,9 @@ def tile_picked_coupled_none_p_kernel(tc, x_words, x_scales, w1, gn, w2, offs, p
             tanh(results[a], ring[a][:])
             turn_blocks(sum_banks[0], results[a], False, a == 1)
 
+        w2_grouped.append(keep.tile([P, S], BF16, name="w2_part_0", align_bytes=64))
+        nc.scalar.copy(out=w2_target(0), in_=w2_source(0))
+
         word_banks = [banks[7], banks[0], banks[2], banks[3]]
         part_banks = [banks[5], banks[6], banks[4]]
 
@@ -245,9 +248,6 @@ def tile_picked_coupled_none_p_kernel(tc, x_words, x_scales, w1, gn, w2, offs, p
                 for n0 in (0, HALF):
                     nc.scalar.activation(out=fetched[:, n0 : n0 + HALF], func=COPY,
                                          in_=h_window[3][:].indirect(lists["q2"][:, n0 // 16 : (n0 + HALF) // 16]))
-            if u == 13:
-                w2_grouped.append(keep.tile([P, S], BF16, name="w2_part_0", tag="ring_0", align_bytes=64))
-                nc.scalar.copy(out=w2_target(0), in_=w2_source(0))
 
         w2_scales = keep.tile([P, N], U8, name="w2_scales", align_bytes=64)
 

@@ -138,7 +138,7 @@ def tile_picked_coupled_none_p_kernel(tc, x_words, x_scales, w1, gn, w2, offs, p
         def w2_source(c):
             return w2_raw[:, :, c * P : (c + 1) * P].rearrange("p j c -> p c j")
 
-        fetched = keep.tile([P, S], F32, name="fetched", align_bytes=64)
+        fetched = keep.tile([P, 3, HALF], F32, name="fetched", align_bytes=64)
 
         def fused(target, step, t, a, n0, width):
             nc.vector.tensor_tensor(out=target,
@@ -174,8 +174,12 @@ def tile_picked_coupled_none_p_kernel(tc, x_words, x_scales, w1, gn, w2, offs, p
         def part_unit(t, which, b0, count, bank, work, result):
             width = count * P
             nodes = slice(b0 * P, b0 * P + width)
-            fused(work[:, :width], 1, t, 0, b0 * P, width)
-            nc.vector.tensor_tensor(out=work[:, width:], in0=fetched[:, nodes], in1=plain[t][:, nodes], op=SUBTRACT)
+            if b0 == 0:
+                nc.vector.tensor_tensor(out=work.rearrange("p (a n) -> p a n", a=2), in0=fetched[:, :2],
+                                        in1=h_window[t][:, nodes].unsqueeze(1).to_broadcast([P, 2, HALF]), op=SUBTRACT)
+            else:
+                fused(work[:, :width], 1, t, 0, b0 * P, width)
+                nc.vector.tensor_tensor(out=work[:, width:], in0=fetched[:, 2, b0 * P - HALF : b0 * P - HALF + width], in1=plain[t][:, nodes], op=SUBTRACT)
             tanh(result, work)
             for c in range(len(which) * count):
                 b = c % count
@@ -191,7 +195,8 @@ def tile_picked_coupled_none_p_kernel(tc, x_words, x_scales, w1, gn, w2, offs, p
         def close(t, half):
             cols = slice(half * HALF, (half + 1) * HALF)
             nc.scalar.copy(out=h_window[t][:, cols], in_=back_banks[half][:, :HALF])
-            nc.sync.dma_start(out=plain[t][:, cols], in_=h_window[t][:, cols])
+            if (t, half) != (3, 0):
+                nc.sync.dma_start(out=plain[t][:, cols], in_=h_window[t][:, cols])
 
         def round_z(t, b0, count, bank):
             l, h = divmod(t, 2)
@@ -244,10 +249,9 @@ def tile_picked_coupled_none_p_kernel(tc, x_words, x_scales, w1, gn, w2, offs, p
                 leave(u // 2 - 1)
             if u == 9:
                 close(3, 1)
-            if u == 11:
-                for n0 in (0, HALF):
-                    nc.scalar.activation(out=fetched[:, n0 : n0 + HALF], func=COPY,
-                                         in_=h_window[3][:].indirect(lists["q2"][:, n0 // 16 : (n0 + HALF) // 16]))
+            if u in (10, 11, 12):
+                a, n0 = ((0, 0), (1, 0), (1, HALF))[u - 10]
+                nc.scalar.activation(out=fetched[:, u - 10], func=COPY, in_=h_window[3][:].indirect(step_lists[1][a][:, n0 // 16 : (n0 + HALF) // 16]))
 
         w2_scales = keep.tile([P, N], U8, name="w2_scales", align_bytes=64)
 

@@ -42,7 +42,8 @@ def tile_picked_coupled_none_p_kernel(tc, x_words, x_scales, w1, gn, w2, offs, p
         x_bytes = keep.tile([P, T], U8, name="x_bytes", align_bytes=64)
         x_packed = keep.tile([P, T], I32, name="x_packed", tag="x_packed", align_bytes=64)
         w1_raw = keep.tile([P, PACK, H], F32, name="w1_raw", align_bytes=64)
-        w2_raw = keep.tile([P, PACK, N], F32, name="w2_raw", align_bytes=64)
+        w2_first = keep.tile([P, PACK, P], F32, name="w2_first", align_bytes=64)
+        w2_rest = keep.tile([P, PACK, N - P], F32, name="w2_rest", align_bytes=64)
         gain = keep.tile([P, PACK], F32, name="gain")
         ident = keep.tile([P, P], F32, name="ident", align_bytes=64)
 
@@ -53,11 +54,13 @@ def tile_picked_coupled_none_p_kernel(tc, x_words, x_scales, w1, gn, w2, offs, p
             nc.sync.dma_start(out=x_bytes[32 * q : 32 * q + 4, :].bitcast(I32), in_=x_scales[0, 4 * q : 4 * q + 4, :].bitcast(I32))
         nc.sync.dma_start(out=gain[:], in_=gn.rearrange("(p j) o -> p (j o)", j=PACK))
         nc.sync.dma_start(out=x_packed[:], in_=x_words[0].rearrange("p n t -> p (n t)").bitcast(I32))
+        w2_rows = w2.rearrange("(p j) c -> p j c", j=PACK)
+        nc.sync.dma_start(out=w2_first[:], in_=w2_rows[:, :, :P])
         nc.sync.dma_start(out=lists["p1"][:], in_=p1)
         nc.sync.dma_start(out=lists["p2"][:], in_=p2)
         nc.sync.dma_start(out=lists["q1"][:], in_=q1)
         nc.sync.dma_start(out=lists["q2"][:], in_=q2)
-        nc.sync.dma_start(out=w2_raw[:], in_=w2.rearrange("(p j) c -> p j c", j=PACK))
+        nc.sync.dma_start(out=w2_rest[:], in_=w2_rows[:, :, P:])
 
         make_identity(nc, ident[:])
         window = []
@@ -116,9 +119,9 @@ def tile_picked_coupled_none_p_kernel(tc, x_words, x_scales, w1, gn, w2, offs, p
                                 rhs=picked_words[:, n0 : n0 + width].bitcast(FP8X4), rhs_scale=picked_bytes[:, n0 : n0 + width],
                                 start=True, stop=True)
 
-        sum_banks = [banks[5], banks[6], banks[2], banks[3]]
-        back_banks = [banks[0], banks[1]]
-        z_banks = [banks[2], banks[3], banks[1]]
+        sum_banks = [banks[5], banks[6], banks[4], banks[0]]
+        back_banks = [(banks[b], banks[1]) for b in (0, 2, 7, 2)]
+        z_banks = [banks[7], banks[0], banks[1]]
         ring = [keep.tile([P, S], F32, name="ring_%d" % r, tag="ring_%d" % r, align_bytes=64) for r in range(RING)]
         pulls = [keep.tile([P, S], F32, name="pulls_%d" % a, tag="pulls_%d" % a, align_bytes=64) for a in range(2)]
         turned_h = keep.tile([P, S], F32, name="turned_h", tag="turned_h", align_bytes=64)[:]
@@ -136,7 +139,7 @@ def tile_picked_coupled_none_p_kernel(tc, x_words, x_scales, w1, gn, w2, offs, p
             return w2_grouped[c][:].rearrange("p (c j) -> p c j", j=PACK)
 
         def w2_source(c):
-            return w2_raw[:, :, c * P : (c + 1) * P].rearrange("p j c -> p c j")
+            return (w2_rest[:, :, (c - 1) * P : c * P] if c else w2_first[:]).rearrange("p j c -> p c j")
 
         fetched = keep.tile([P, 3, HALF], F32, name="fetched", align_bytes=64)
 
@@ -190,11 +193,11 @@ def tile_picked_coupled_none_p_kernel(tc, x_words, x_scales, w1, gn, w2, offs, p
                 cols = slice(half * HALF, (half + 1) * HALF)
                 nc.scalar.copy(out=turned[t % 2][:, cols], in_=sum_banks[t][:, cols])
                 for c in range(2):
-                    turn(back_banks[half][:, c * P : (c + 1) * P], turned[t % 2][:, half * HALF + c * P : half * HALF + (c + 1) * P], c == 0, c == 1)
+                    turn(back_banks[t][half][:, c * P : (c + 1) * P], turned[t % 2][:, half * HALF + c * P : half * HALF + (c + 1) * P], c == 0, c == 1)
 
         def close(t, half):
             cols = slice(half * HALF, (half + 1) * HALF)
-            nc.scalar.copy(out=h_window[t][:, cols], in_=back_banks[half][:, :HALF])
+            nc.scalar.copy(out=h_window[t][:, cols], in_=back_banks[t][half][:, :HALF])
             if (t, half) != (3, 0):
                 nc.sync.dma_start(out=plain[t][:, cols], in_=h_window[t][:, cols])
 
@@ -218,9 +221,7 @@ def tile_picked_coupled_none_p_kernel(tc, x_words, x_scales, w1, gn, w2, offs, p
         double(window[2][:, :S], banks[3][:])
         nc.sync.dma_start(out=plain[2][:], in_=window[2][:, :S])
         double(plain[1][:], banks[2][:])
-        double(window[3][:, :S], banks[4][:])
-        nc.sync.dma_start(out=plain[3], in_=window[3][:, :S])
-        for t in range(PACK):
+        for t in range(2):
             open_sum(t)
         for n0 in (0, HALF):
             for a in range(2):
@@ -229,10 +230,13 @@ def tile_picked_coupled_none_p_kernel(tc, x_words, x_scales, w1, gn, w2, offs, p
             tanh(results[a], ring[a][:])
             turn_blocks(sum_banks[0], results[a], False, a == 1)
 
+        double(window[3][:, :S], banks[4][:])
+        nc.sync.dma_start(out=plain[3], in_=window[3][:, :S])
+        open_sum(2)
         w2_grouped.append(keep.tile([P, S], BF16, name="w2_part_0", align_bytes=64))
         nc.scalar.copy(out=w2_target(0), in_=w2_source(0))
 
-        word_banks = [banks[7], banks[0], banks[2], banks[3]]
+        word_banks = [banks[3], banks[2], banks[7], banks[0]]
         part_banks = [banks[5], banks[6], banks[4]]
 
         def turn_words(b, u):
@@ -243,6 +247,8 @@ def tile_picked_coupled_none_p_kernel(tc, x_words, x_scales, w1, gn, w2, offs, p
             unit(u)
             if u in (3, 5, 7, 9):
                 close(u // 2 - 1, 0)
+            if u == 3:
+                open_sum(3)
             if u in (4, 6, 8):
                 close(u // 2 - 2, 1)
             if u in (2, 4, 6, 8):
@@ -323,5 +329,5 @@ def tile_picked_coupled_none_p_kernel(tc, x_words, x_scales, w1, gn, w2, offs, p
         quantize_z(1)
         second_product(0, 0, [banks[5], banks[1]])
         second_product(0, 2, [banks[6], banks[4]])
-        second_product(1, 0, [banks[7], banks[0]])
-        second_product(1, 2, [banks[2], banks[3]])
+        second_product(1, 0, [banks[3], banks[2]])
+        second_product(1, 2, [banks[7], banks[0]])

from contextlib import ExitStack

import concourse.mybir as mybir
from concourse.masks import make_identity

K, T, S, N, H = 512, 2048, 512, 512, 512
FLOPS = 2 * K * H * S + 2 * H * N * S

F32 = mybir.dt.float32
BF16 = mybir.dt.bfloat16
I32 = mybir.dt.int32
U32 = mybir.dt.uint32
U16 = mybir.dt.uint16
U8 = mybir.dt.uint8
FP8X4 = mybir.dt.float8_e4m3fn_x4
MULT = mybir.AluOpType.mult
ADD = mybir.AluOpType.add
SUBTRACT = mybir.AluOpType.subtract
TANH = mybir.ActivationFunctionType.Tanh
COPY = mybir.ActivationFunctionType.Copy

P = 128
PACK = 4
BANK = 512
HALF = S // 2
BLOCKS = S // P
RING = 3
VECTOR_BLOCKS = 8


def tile_picked_coupled_none_p_kernel(tc, x_words, x_scales, w1, gn, w2, offs, p1, p2, q1, q2, out):
    nc = tc.nc
    with ExitStack() as ctx:
        keep = ctx.enter_context(tc.tile_pool(name="keep", bufs=1))
        shared = ctx.enter_context(tc.tile_pool(name="shared", bufs=1))
        psum = ctx.enter_context(tc.psum_pool(name="psum", bufs=1))

        banks = [psum.tile([P, BANK], F32, name="bank_%d" % b) for b in range(8)]
        lists = {name: keep.tile([P, S // 16], U16, name="list_" + name) for name in ("offs", "p1", "p2", "q1", "q2")}
        step_lists = [(lists["p1"], lists["p2"]), (lists["q1"], lists["q2"])]

        x_bytes = keep.tile([P, T], U8, name="x_bytes", align_bytes=64)
        x_packed = keep.tile([P, T], I32, name="x_packed", tag="x_packed", align_bytes=64)
        w1_raw = keep.tile([P, PACK, H], F32, name="w1_raw", align_bytes=64)
        w2_first = keep.tile([P, PACK, P], F32, name="w2_first", align_bytes=64)
        w2_rest = keep.tile([P, PACK, N - P], F32, name="w2_rest", align_bytes=64)
        gain = keep.tile([P, PACK], F32, name="gain")
        ident = keep.tile([P, P], F32, name="ident", align_bytes=64)

        nc.vector.memset(x_bytes[:].bitcast(I32), 0)
        nc.sync.dma_start(out=w1_raw[:], in_=w1.rearrange("(p j) c -> p j c", j=PACK))
        nc.sync.dma_start(out=lists["offs"][:], in_=offs)
        for q in range(4):
            nc.sync.dma_start(out=x_bytes[32 * q : 32 * q + 4, :].bitcast(I32), in_=x_scales[0, 4 * q : 4 * q + 4, :].bitcast(I32))
        nc.sync.dma_start(out=gain[:], in_=gn.rearrange("(p j) o -> p (j o)", j=PACK))
        nc.sync.dma_start(out=x_packed[:], in_=x_words[0].rearrange("p n t -> p (n t)").bitcast(I32))
        w2_rows = w2.rearrange("(p j) c -> p j c", j=PACK)
        nc.sync.dma_start(out=w2_first[:], in_=w2_rows[:, :, :P])
        nc.sync.dma_start(out=lists["p1"][:], in_=p1)
        nc.sync.dma_start(out=lists["p2"][:], in_=p2)
        nc.sync.dma_start(out=lists["q1"][:], in_=q1)
        nc.sync.dma_start(out=lists["q2"][:], in_=q2)
        nc.sync.dma_start(out=w2_rest[:], in_=w2_rows[:, :, P:])

        make_identity(nc, ident[:])
        window = []
        for t in range(PACK):
            tile = keep.tile([P, 2 * S], F32, name="window_%d" % t, tag="window_%d" % t, align_bytes=64)
            nc.gpsimd.memset(tile[:, S:], 0.0)
            window.append(tile)
        plain = [keep.tile([P, S], F32, name="plain_%d" % t, align_bytes=64) for t in range(PACK - 1)]
        plain.append(shared.tile([P, 2 * S], F32, name="plain_3", align_bytes=64, offset=0)[:, :S])

        def turn(dst, src, start, stop):
            nc.tensor.matmul(dst, lhsT=src, rhs=ident[:], start=start, stop=stop, is_transpose=True)

        def turn_blocks(bank, src, start, stop):
            for b in range(BLOCKS):
                cols = slice(b * P, (b + 1) * P)
                turn(bank[:, cols], src[:, cols], start and b == 0, stop and b == BLOCKS - 1)

        half_gain = keep.tile([P, PACK], F32, name="half_gain")
        gain_rows = keep.tile([P, PACK, P], F32, name="gain_rows", align_bytes=64)
        nc.gpsimd.tensor_scalar(out=half_gain[:], in0=gain[:], scalar1=0.5, scalar2=0.0, op0=MULT, op1=ADD)
        for j in range(PACK):
            turn(banks[7][:, j * P : (j + 1) * P], half_gain[:, j : j + 1].to_broadcast([P, P]), j == 0, j == PACK - 1)
        spread = banks[7][:].rearrange("n (l e b h c) -> n l h b c e", l=2, e=2, h=2, c=4)
        for l in range(2):
            nc.scalar.copy(out=gain_rows[:, 2 * l : 2 * l + 2].rearrange("n h (b c e) -> n h b c e", c=4, e=2), in_=spread[:, l])

        picked_bytes = keep.tile([P, S], U8, name="picked_bytes", align_bytes=64)
        nc.vector.tensor_copy(out=picked_bytes[:], in_=x_bytes[:].indirect(lists["offs"][:]))

        source = w1_raw[:].rearrange("p j (b h i) -> p h b i j", h=2, i=16)
        w1_grouped = [keep.tile([P, 2 * H], BF16, name="w1_grouped_%d" % h, tag=tag, align_bytes=64) for h, tag in enumerate(("picked_words", "ring_0"))]
        target = [tile[:].rearrange("p (l b c r) -> p b c l r", l=2, b=16, c=4) for tile in w1_grouped]
        nc.vector.tensor_copy(out=target[0][:, :VECTOR_BLOCKS], in_=source[:, 0, :VECTOR_BLOCKS])
        nc.scalar.copy(out=target[0][:, VECTOR_BLOCKS:], in_=source[:, 0, VECTOR_BLOCKS:])
        nc.scalar.copy(out=target[1], in_=source[:, 1])
        w1_codes, w1_scales = [], []

        def quantize_w1(h, tag):
            w1_codes.append(keep.tile([P, HALF], U32, name="w1_codes_%d" % h, tag=tag, align_bytes=64))
            w1_scales.append(keep.tile([P, HALF], U8, name="w1_scales_%d" % h, align_bytes=64))
            nc.vector.quantize_mx(out=w1_codes[h][:].bitcast(FP8X4), scales=w1_scales[h][:], in_=w1_grouped[h][:])

        quantize_w1(0, "w1_codes_0")
        picked_words = keep.tile([P, S], U32, name="picked_words", tag="picked_words", align_bytes=64)
        pieces = [(0, HALF), (HALF, P), (HALF + P, P)]
        for n0, width in pieces:
            nc.vector.tensor_copy(out=picked_words[:, n0 : n0 + width],
                                  in_=x_packed[:].bitcast(U32).indirect(lists["offs"][:, n0 // 16 : (n0 + width) // 16]))
        quantize_w1(1, "x_packed")

        def first_product(acc, t, n0, width):
            l, h = divmod(t, 2)
            cols = slice(l * P, (l + 1) * P)
            nc.tensor.matmul_mx(out=acc[:, :width], lhsT=w1_codes[h][:, cols].bitcast(FP8X4), lhsT_scale=w1_scales[h][:, cols],
                                rhs=picked_words[:, n0 : n0 + width].bitcast(FP8X4), rhs_scale=picked_bytes[:, n0 : n0 + width],
                                start=True, stop=True)

        sum_banks = [banks[5], banks[6], banks[4], banks[0]]
        back_banks = [(banks[b], banks[1]) for b in (0, 2, 7, 2)]
        z_banks = [banks[7], banks[0], banks[1]]
        ring = [keep.tile([P, S], F32, name="ring_%d" % r, tag="ring_%d" % r, align_bytes=64) for r in range(RING)]
        pulls = [keep.tile([P, S], F32, name="pulls_%d" % a, tag="pulls_%d" % a, align_bytes=64) for a in range(2)]
        turned_h = keep.tile([P, S], F32, name="turned_h", tag="turned_h", align_bytes=64)[:]
        first_pull = keep.tile([P, S], F32, name="first_pull", tag="first_pull", align_bytes=64)[:]
        turned = [first_pull, turned_h]
        results = [pulls[1][:] if u % 2 else (turned[u // 2 % 2] if u < 12 else pulls[0][:]) for u in range(13)]
        results.append(keep.tile([P, S], F32, name="last_whole_pull", align_bytes=64)[:])
        h_window = window[:3] + [keep.tile([P, S], F32, name="last_window", align_bytes=64)]
        windows = [window, h_window]
        late = [keep.tile([P, S], F32, name="late_%d" % i, tag="late_%d" % i, align_bytes=64) for i in range(2)]

        w2_grouped = []

        def w2_target(c):
            return w2_grouped[c][:].rearrange("p (c j) -> p c j", j=PACK)

        def w2_source(c):
            return (w2_rest[:, :, (c - 1) * P : c * P] if c else w2_first[:]).rearrange("p j c -> p c j")

        fetched = keep.tile([P, 3, HALF], F32, name="fetched", align_bytes=64)

        def fused(target, step, t, a, n0, width):
            nc.vector.tensor_tensor(out=target,
                                    in0=windows[step][t][:].indirect(step_lists[step][a][:, n0 // 16 : (n0 + width) // 16]),
                                    in1=plain[t][:, n0 : n0 + width], op=SUBTRACT)

        def tanh(target, source):
            nc.scalar.activation(out=target, in_=source, func=TANH, scale=0.5)

        def double(target, acc):
            nc.scalar.activation(out=target, in_=acc, func=COPY, scale=2.0)

        def open_sum(t):
            turn_blocks(sum_banks[t], window[t], True, False)

        def unit(u):
            work = ring[u % RING][:] if u < 13 else turned[0]
            if u in (8, 10, 12):
                for n0 in (0, HALF):
                    fused(work[:, n0 : n0 + HALF], 1, u // 2 % PACK, 0, n0, HALF)
            else:
                fused(work, u // 8, u // 2 % PACK, u % 2, 0, S)
            tanh(results[u], work)
            bank = sum_banks[u // 2] if u < 8 else z_banks[u // 2 - 4]
            if u >= 8 and u % 2 == 0:
                turn_blocks(bank, window[u // 2 - 4], True, False)
            turn_blocks(bank, results[u], False, u % 2 == 1)

        def open_part(t, b0, count, bank):
            for b in range(count):
                turn(bank[:, b * P : (b + 1) * P], h_window[t][:, (b0 + b) * P : (b0 + b + 1) * P], b == 0, False)

        def part_unit(t, which, b0, count, bank, work, result):
            width = count * P
            nodes = slice(b0 * P, b0 * P + width)
            if b0 == 0:
                nc.vector.tensor_tensor(out=work.rearrange("p (a n) -> p a n", a=2), in0=fetched[:, :2],
                                        in1=h_window[t][:, nodes].unsqueeze(1).to_broadcast([P, 2, HALF]), op=SUBTRACT)
            else:
                fused(work[:, :width], 1, t, 0, b0 * P, width)
                nc.vector.tensor_tensor(out=work[:, width:], in0=fetched[:, 2, b0 * P - HALF : b0 * P - HALF + width], in1=plain[t][:, nodes], op=SUBTRACT)
            tanh(result, work)
            for c in range(len(which) * count):
                b = c % count
                turn(bank[:, b * P : (b + 1) * P], result[:, c * P : (c + 1) * P], False, which[-1] == 1 and c == len(which) * count - 1)

        def leave(t):
            for half in range(2):
                cols = slice(half * HALF, (half + 1) * HALF)
                nc.scalar.copy(out=turned[t % 2][:, cols], in_=sum_banks[t][:, cols])
                for c in range(2):
                    turn(back_banks[t][half][:, c * P : (c + 1) * P], turned[t % 2][:, half * HALF + c * P : half * HALF + (c + 1) * P], c == 0, c == 1)

        def close(t, half):
            cols = slice(half * HALF, (half + 1) * HALF)
            nc.scalar.copy(out=h_window[t][:, cols], in_=back_banks[t][half][:, :HALF])
            if (t, half) != (3, 0):
                nc.sync.dma_start(out=plain[t][:, cols], in_=h_window[t][:, cols])

        def round_z(t, b0, count, bank):
            l, h = divmod(t, 2)
            target = z_turned[b0 // 2][l][:].rearrange("n (a b h r) -> n h a b r", b=16, h=2, r=8)[:, h, b0 % 2 : b0 % 2 + count]
            nc.vector.tensor_tensor(out=target, in0=bank[:, : count * P].rearrange("n (a b r) -> n a b r", b=16, r=8),
                                    in1=gain_rows[:, t].rearrange("n (b r) -> n b r", r=8).unsqueeze(1).to_broadcast([P, count, 16, 8]), op=MULT)

        first_banks = [banks[0], banks[1], banks[6]]
        for (n0, width), acc in zip(pieces, first_banks):
            first_product(acc, 0, n0, width)
        double(window[0][:, :HALF], banks[0][:, :HALF])
        for (n0, width), acc in zip(pieces[1:], first_banks[1:]):
            nc.vector.tensor_scalar(out=window[0][:, n0 : n0 + width], in0=acc[:, :width], scalar1=2.0, scalar2=0.0, op0=MULT, op1=ADD)
        for (n0, width), acc in zip(pieces, first_banks):
            double(plain[0][:, n0 : n0 + width], acc[:, :width])
        for t in range(1, PACK):
            first_product(banks[t + 1], t, 0, S)
        double(window[1][:, :S], banks[2][:])
        double(window[2][:, :S], banks[3][:])
        nc.sync.dma_start(out=plain[2][:], in_=window[2][:, :S])
        double(plain[1][:], banks[2][:])
        for t in range(2):
            open_sum(t)
        for n0 in (0, HALF):
            for a in range(2):
                fused(ring[a][:, n0 : n0 + HALF], 0, 0, a, n0, HALF)
        for a in range(2):
            tanh(results[a], ring[a][:])
            turn_blocks(sum_banks[0], results[a], False, a == 1)

        double(window[3][:, :S], banks[4][:])
        nc.sync.dma_start(out=plain[3], in_=window[3][:, :S])
        open_sum(2)
        w2_grouped.append(keep.tile([P, S], BF16, name="w2_part_0", align_bytes=64))
        nc.scalar.copy(out=w2_target(0), in_=w2_source(0))

        word_banks = [banks[3], banks[2], banks[7], banks[0]]
        part_banks = [banks[5], banks[6], banks[4]]

        def turn_words(b, u):
            words = z_turned[b // 2][u][:].bitcast(F32)
            turn(word_banks[b][:, u * P : (u + 1) * P], words[:, b % 2 * P : (b % 2 + 1) * P], True, True)

        for u in range(2, 14):
            unit(u)
            if u in (3, 5, 7, 9):
                close(u // 2 - 1, 0)
            if u == 3:
                open_sum(3)
            if u in (4, 6, 8):
                close(u // 2 - 2, 1)
            if u in (2, 4, 6, 8):
                leave(u // 2 - 1)
            if u == 9:
                close(3, 1)
            if u in (10, 11, 12):
                a, n0 = ((0, 0), (1, 0), (1, HALF))[u - 10]
                nc.scalar.activation(out=fetched[:, u - 10], func=COPY, in_=h_window[3][:].indirect(step_lists[1][a][:, n0 // 16 : (n0 + HALF) // 16]))

        w2_scales = keep.tile([P, N], U8, name="w2_scales", align_bytes=64)

        z_grouped = [keep.tile([P, 2 * H], BF16, name="z_grouped_%d" % half, align_bytes=64) for half in range(2)]

        def turn_back(b):
            turn_words(b, 1)
            target = z_grouped[b // 2][:, b % 2 * H : (b % 2 + 1) * H].bitcast(F32).rearrange("p (n u) -> p n u", u=2)
            source = word_banks[b][:, : 2 * P].rearrange("p (u n) -> p n u", u=2)
            nc.scalar.copy(out=target, in_=source)

        z_codes = keep.tile([P, S], U32, name="z_codes", align_bytes=64)
        z_scales = keep.tile([P, S], U8, name="z_scales", align_bytes=64)

        def quantize_z(half):
            cols = slice(half * HALF, (half + 1) * HALF)
            nc.vector.quantize_mx(out=z_codes[:, cols].bitcast(FP8X4), scales=z_scales[:, cols], in_=z_grouped[half][:])

        out_view = out.rearrange("(r p) n -> p r n", p=P)

        def second_product(half, r0, accs):
            nodes = slice(half * HALF, (half + 1) * HALF)
            result = keep.tile([P, 2, HALF], F32, name="result_%d_%d" % (half, r0), align_bytes=64)
            for r, acc in enumerate(accs):
                cols = slice((r0 + r) * P, (r0 + r + 1) * P)
                nc.tensor.matmul_mx(out=acc[:, :HALF], lhsT=w2_codes[:, cols].bitcast(FP8X4), lhsT_scale=w2_scales[:, cols],
                                    rhs=z_codes[:, nodes].bitcast(FP8X4), rhs_scale=z_scales[:, nodes], start=True, stop=True)
                if r:
                    nc.vector.tensor_copy(out=result[:, r], in_=acc[:, :HALF])
                else:
                    nc.scalar.copy(out=result[:, r], in_=acc[:, :HALF])
                if (half, r0) in ((0, 0), (1, 2)):
                    nc.sync.dma_start(out=out_view[:, r0 + r, nodes], in_=result[:, r])
            if (half, r0) in ((0, 2), (1, 0)):
                nc.sync.dma_start(out=out_view[:, r0 : r0 + 2, nodes], in_=result[:])

        open_part(3, 0, 2, part_banks[0])
        part_unit(3, (0, 1), 0, 2, part_banks[0], late[0][:], pulls[0][:])
        for b in (2, 3):
            open_part(3, b, 1, part_banks[b - 1])
            cols = slice((b - 2) * HALF, (b - 1) * HALF)
            part_unit(3, (0, 1), b, 1, part_banks[b - 1], late[1][:, cols], pulls[1][:, cols])
        for c in (1, 2):
            w2_grouped.append(shared.tile([P, S], BF16, name="w2_part_%d" % c, align_bytes=64, offset=2 * S * c))
            nc.gpsimd.tensor_scalar(out=w2_target(c), in0=w2_source(c), scalar1=1.0, scalar2=0.0, op0=MULT, op1=ADD)
        w2_grouped.append(keep.tile([P, S], BF16, name="w2_part_3", tag="late_1", align_bytes=64))
        nc.scalar.copy(out=w2_target(3), in_=w2_source(3))
        z_turned = [[keep.tile([P, H], BF16, name="z_turned_%d_%d" % (half, l), tag="pulls_0" if (half, l) == (1, 0) else "z_turned_%d_%d" % (half, l), align_bytes=64)
                     for l in range(2)] for half in range(2)]
        for half in range(2):
            for t in range(3):
                round_z(t, 2 * half, 2, z_banks[t][:, half * HALF :])
                if t == 1:
                    for b in (2 * half, 2 * half + 1):
                        turn_words(b, 0)
            if half == 0:
                round_z(3, 0, 2, part_banks[0])
                for b in range(2):
                    turn_back(b)
        for b in (2, 3):
            round_z(3, b, 1, part_banks[b - 1])
        quantize_z(0)
        w2_codes = keep.tile([P, N], U32, name="w2_codes", tag="pulls_1", align_bytes=64)
        for c in range(PACK):
            cols = slice(c * P, (c + 1) * P)
            nc.vector.quantize_mx(out=w2_codes[:, cols].bitcast(FP8X4), scales=w2_scales[:, cols], in_=w2_grouped[c][:])
        for b in (2, 3):
            turn_back(b)
        quantize_z(1)
        second_product(0, 0, [banks[5], banks[1]])
        second_product(0, 2, [banks[6], banks[4]])
        second_product(1, 0, [banks[3], banks[2]])
        second_product(1, 2, [banks[7], banks[0]])
